import numpy as np, ml_dtypes
CORES = [16,17,18,19,32,33,34,35]
N = 8
import mx_ref
BF = ml_dtypes.bfloat16
def gentries(a):
    return np.ascontiguousarray(a.reshape(8, 16, -1).transpose(0, 2, 1)).reshape(8, -1)
def gtable(e):
    e = np.asarray(e); return np.ascontiguousarray(e.reshape(8, -1, 16).transpose(0, 2, 1)).reshape(128, -1).astype(np.int32)
def gcols(t, e):
    v = np.concatenate([t.reshape(8, 16, -1, 4), np.zeros((8, 16, 1, 4), BF)], axis=2)
    return np.ascontiguousarray(np.stack([v[g][:, e[g]] for g in range(8)])).reshape(128, -1)
def tile(rs):
    return np.stack(rs, axis=2).reshape(128, -1).astype(BF)
def pick(q, e):
    c = np.concatenate([q[0].reshape(128, -1, 4), np.zeros((128, 1, 4), np.uint8)], axis=1); s = np.concatenate([q[1], np.ones((16, 1), np.uint8)], axis=1)
    return (np.ascontiguousarray(c[:, e].reshape(128, -1)), np.ascontiguousarray(s[:, e]))
def join(*qs):
    return (np.concatenate([q[0] for q in qs], axis=1), np.concatenate([q[1] for q in qs], axis=1))
def put(q, e, v):
    c, s = q[0].reshape(128, -1, 4).copy(), q[1].copy(); c[:, e] = v[0].reshape(128, -1, 4); s[:, e] = v[1]
    return (c.reshape(128, -1), s)
def pk(c, s):
    return (np.ascontiguousarray(c), mx_ref.live(s))
def emit(q):
    return q[0], q[1]
def packed(v, rng):
    q = [mx_ref.quantize(np.ascontiguousarray(v[r])) for r in range(N)]
    return np.stack([a for a, b in q]), np.stack([mx_ref.plane(b, rng) for a, b in q])
def values_of_codes():
    e, c = np.zeros((128, 128, 4), np.float32), np.zeros((128, 2, 4), np.uint8)
    e[np.arange(128), np.arange(128), 0] = 1
    c[:127, :, 0] = np.arange(256).reshape(2, 128).T[:127]
    return mx_ref.matmul(mx_ref.quantize(e.reshape(128, 512).astype(BF)), (c.reshape(128, 8), np.full((16, 2), 127, np.uint8))).T.reshape(-1).astype(np.float64)
CODE_VALUE, SCALE_VALUE = values_of_codes(), 2.0 ** (np.arange(256) - 127.0)
def decode(q):
    return (CODE_VALUE[q[0]].reshape(16, 8, -1, 4) * SCALE_VALUE[q[1]][:, None, :, None] + 0.0).reshape(128, -1).astype(np.float32)
def f(rng, *shape):
    return mx_ref.flush((rng.standard_normal(shape, dtype=np.float32) * np.exp2(rng.integers(-2, 3, shape[:-1] + (1,)))).astype(BF))
def wide(rng, *shape, cols=0):
    v = rng.standard_normal(shape, dtype=np.float32) * np.exp2(rng.integers(-12, 13, shape)).astype(np.float32)
    if cols: v *= np.repeat(np.exp2(rng.integers(-cols, cols + 1, shape[:-2] + (1, shape[-1] // 4))) * (rng.random(shape[:-2] + (1, shape[-1] // 4)) > 0.0625), 4, axis=-1).astype(np.float32)
    return mx_ref.flush(v.astype(BF))
C, T, P, A = 256, 16, 7, 7
MASK = [1, 2, 4]
def numbers_of(rng):
    return {"x": np.array(f(rng, N, 128, 4 * C)), "u": np.array(f(rng, N, 128, 512)), "v": np.array(f(rng, N, 128, 512))}
def lists_of(e):
    return np.stack([gtable(e[r]) for r in range(N)])
def places(rng):
    return np.argsort(rng.random((N, 8, C)), axis=2)
def grow(rng, b):
    b[:, 0], b[:, 1] = 1, 0
    o = np.argsort(rng.random(b.shape), axis=1)
    e = np.zeros(b.shape, np.int64)
    np.put_along_axis(e, o, np.take_along_axis(o, b, axis=1), axis=1)
    return lists_of(e.reshape(N, 8, C))
def trees(rng):
    return grow(rng, rng.integers(0, np.maximum(np.arange(16), 1), (N * 8 * T, 16)))
def layers(rng):
    return np.array(f(rng, N, 128, 2048)).reshape(N, 8, 16, 4, 8, 16, 4)
def weights(rng, w, still=[]):
    for i in still:
        w[:, :, i] = 0
        w[:, :, :, :, :, i] = 0
    c, s = packed(np.ascontiguousarray(w).reshape(N, 128, 2048), rng)
    return {"wc": c, "ws": s}
def setup_inputs(rng):
    return {**numbers_of(rng), "nod": lists_of(places(rng)), "par": trees(rng), **weights(rng, layers(rng))}
def setup_inputs_ties(rng):
    d = numbers_of(rng)
    x = d["x"].reshape(N, 8, 16, C, 4)
    x[:, :, 0] = 0
    x[:, :, 0, :, 0] = rng.integers(0, 3, (N, 8, C)).astype(np.float32).astype(BF)
    u = d["u"].reshape(N, 128, 128, 4)
    u[:, :, ::16] = 0
    o = rng.permutation(N)
    for r in range(N):
        for h in range(0, 128, 16): u[r, h, h, 0] = 0.0 if r == o[0] else -1.0 if r == o[1] else 1.0
    return {"x": x.reshape(N, 128, 4 * C), "u": u.reshape(N, 128, 512), "v": d["v"], "nod": lists_of(places(rng)), "par": trees(rng), **weights(rng, layers(rng), [0])}
def setup_inputs_near(rng):
    d = numbers_of(rng)
    e = places(rng)
    o = rng.permutation(N) % 4
    x = d["x"].astype(np.float32).reshape(N, 8, 16, C, 4)
    x[:, :, 0] = 0
    x[:, :, 8:] = 0
    x[:, :, 0, :, 0] = rng.choice([-1.0, 1.0], 8)[None, :, None]
    x[:, :, 8] = ((rng.integers(0, 16, (N, 8, C))[..., None] >> np.arange(4)) & 1) * np.exp2(np.arange(4) - 23.0)
    x[:, :, 11, :, 0] = 2.0 ** -10
    u = d["u"].reshape(N, 128, 128, 4)
    u[:, :, ::16] = 0
    for r in range(N):
        k = 1.0 if o[r] == 0 else 2.0 ** -30
        if o[r] == 2:
            far = np.take_along_axis(e[r].reshape(8, T, 16), np.argsort(rng.random((8, T, 16)), axis=2)[:, :, :2], axis=2)
            x[r, :, 0] = 0
            for g in range(8):
                x[r, g, 0, far[g, :, 0], 0] = 1.0
                x[r, g, 0, far[g, :, 1], 0] = -1.0
        if o[r] == 3:
            x[r, :, 8:] = 0
            x[r, :, 10, :, 0] = rng.choice([1.0, 1.125], (8, C)) * 2.0 ** -27
        for h in range(0, 128, 16):
            if o[r] < 2:
                u[r, h, h, 0] = k
                u[r, h + 11, h, 0] = k
            if o[r] == 2: u[r, h, h, 0] = 1.0
            if o[r] < 3: u[r, h + 8, h] = k
            else: u[r, h + 10, h, 0] = k
    return {"x": x.reshape(N, 128, 4 * C).astype(BF), "u": u.reshape(N, 128, 512), "v": d["v"], "nod": lists_of(e), "par": trees(rng), **weights(rng, layers(rng), [0, 8, 9, 10, 11, 12, 13, 14, 15])}
def setup_inputs_huge(rng):
    d = numbers_of(rng)
    o = rng.permutation(N)
    h = int(np.argmin(o))
    c = rng.choice([-1.0, 1.0], (N, 1, 1, C, 1))
    c[o % 4 == 1] = -1.0
    x = (0.6 + 0.09 * rng.random((N, 8, 16, C, 4))) * c
    x[h] = 0.875 * c[h]
    x[h, 0, 0] = (0.5 + 0.375 * rng.random((C, 4))) * c[h, 0, 0]
    a = 1.0 - 0.1 * rng.random((N, 128, 8, 4))
    a[h] = 1.0
    u = d["u"].reshape(N, 128, 128, 4)
    u[:, :, ::16] = (2.0 ** 30 * a).astype(np.float32).astype(BF)
    w = np.zeros((N, 128, 4, 128, 4), np.float32)
    i = np.arange(128)
    for b in range(4): w[:, i, b, i, b] = -1
    return {"x": (2.0 ** 30 * x).astype(np.float32).reshape(N, 128, 4 * C).astype(BF), "u": u.reshape(N, 128, 512), "v": d["v"], "nod": lists_of(places(rng)), "par": trees(rng), **weights(rng, w.astype(BF))}
def setup_inputs_forms(rng):
    d = numbers_of(rng)
    x = d["x"].reshape(N, 8, 16, C, 4)
    z = (N, 8, 8, C, 4)
    n = rng.integers(8, 15, z)
    n[:, :, 1, :, 0] = (rng.permutation(8) % 7 + 8)[:, None]
    x[:, :, 8:] = ((9 + 2 * rng.integers(0, 4, z)) * np.exp2(-3.0 - n) * rng.choice([-1.0, 1.0], z)).astype(np.float32).astype(BF)
    x[:, :, 8, :, 0] = 1.96875
    i = np.arange(16)
    b = np.stack([0 * i, np.maximum(i - 1, 0), i % 2, np.where(i < 8, np.maximum(i - 1, 0), 7)])
    k = rng.integers(0, 4, (N, 8 * T))
    e = rng.permutation(N)
    k[e[0]] = 0
    k[e[1]] = 1
    u = d["u"].reshape(N, 128, 128, 4)
    for r in e[N // 2:]:
        u[r, :, ::16] = 0
        for h in range(0, 128, 16): u[r, h + 9, h, 0] = 1.0
    w = layers(rng)
    w[:, :, :, :, :, 8:] = 0
    return {"x": x.reshape(N, 128, 4 * C), "u": u.reshape(N, 128, 512), "v": d["v"], "nod": lists_of(places(rng)), "par": grow(rng, b[k.reshape(-1)]), **weights(rng, w)}
def setup_inputs_spread(rng):
    d = setup_inputs(rng)
    d["x"] = wide(rng, N, 128, 4 * C, cols=6)
    return d
def check_inputs(d):
    b = []
    for k in ("x", "u", "v"):
        a = np.abs(d[k].astype(np.float32))
        if not (np.isfinite(a).all() and ((a == 0) | (a >= 2.0 ** -30) & (a <= 2.0 ** 30)).all()): b.append("a value of " + k)
    e = np.stack([gentries(d["nod"][r]) for r in range(N)])
    if (np.sort(e, axis=2) != np.arange(C)).any(): b.append("nod: a group whose entries aren't every column once")
    e = np.stack([gentries(d["par"][r]) for r in range(N)]).reshape(-1, 16).astype(np.int64)
    i = np.arange(16)
    if ((e < 0) | (e > 15)).any(): b.append("an entry of par")
    else:
        two = (np.take_along_axis(e, e, axis=1) == i) & (e != i)
        far = e
        for j in range(4): far = np.take_along_axis(far, far, axis=1)
        if (np.count_nonzero(two, axis=1) != 2).any() or (e == i).any() or not np.take_along_axis(two, far, axis=1).all(): b.append("par: links that aren't a tree's")
    none, least, most = [emit(mx_ref.quantize(np.full((128, 16), k, np.float32).astype(BF)))[1][0, 0] for k in (0.0, 2.0 ** -30, 2.0 ** 30)]
    for r in range(N):
        if ((d["wc"][r] == 0x7F) | (d["wc"][r] == 0xFF)).any(): b.append("wc: a code that is no number")
        s = mx_ref.live(d["ws"][r])
        if ((s != none) & ((s < least) | (s > most))).any(): b.append("ws: a scale out of range")
    return b
def reference(x, u, v, nod, par, wc, ws):
    qu = [mx_ref.quantize(u[r]) for r in range(N)]
    lay = [pk(wc[r], ws[r]) for r in range(N)]
    now = [x[r] for r in range(N)]
    place = np.stack([gentries(nod[r]) for r in range(N)]).reshape(-1, 16).astype(np.int64)
    link = np.stack([gentries(par[r]) for r in range(N)]).reshape(-1, 16).astype(np.int64)
    m = np.arange(N * 8 * T)
    for mask in MASK:
        q = [mx_ref.quantize(now[r]) for r in range(N)]
        own = [decode(q[r]) for r in range(N)]
        s = np.stack([mx_ref.matmul(qu[r], q[r])[::16] for r in range(N)]) + np.float32(0.0)
        s = np.take_along_axis(s, place.reshape(N, 8, C), axis=2).reshape(-1, 16)
        o = np.argsort(-s, axis=1, kind="stable")
        st = np.argsort(o, axis=1)
        col = np.take_along_axis(place, o, axis=1)
        to = np.take_along_axis(st, link, axis=1)
        edge = np.zeros((len(m), 16, 16), bool)
        edge[m[:, None], st, to] = True
        edge[m[:, None], to, st] = True
        word = np.zeros((len(m), 14), np.int64)
        for j in range(14):
            a = np.argmax(np.count_nonzero(edge, axis=2) == 1, axis=1)
            word[:, j] = np.argmax(edge[m, a], axis=1)
            edge[m, a, word[:, j]] = False
            edge[m, word[:, j], a] = False
        give = np.take_along_axis(col, word[:, A:], axis=1).reshape(N, 8, T * P)
        sent = [mx_ref.quantize(gcols(own[r].astype(BF), give[r])) for r in range(N)]
        other = word.reshape(N, 8 * T, 14)[np.arange(N) ^ mask].reshape(-1, 14)
        c = np.concatenate([word[:, :A], other[:, A:]], axis=1)
        free = np.ones((len(m), 16), bool)
        need = np.count_nonzero(c[:, :, None] == np.arange(16), axis=1)
        to, src = np.zeros((len(m), 16), np.int64), np.zeros((len(m), 16), np.int64)
        for j in range(14):
            a = np.argmax(free & (need == 0), axis=1)
            to[m, a] = c[:, j]
            src[m, a] = col[m, c[:, j]] if j < A else C + P * (m % T) + j - A
            free[m, a] = False
            need[m, c[:, j]] -= 1
        a = np.argmax(free, axis=1)
        free[m, a] = False
        b = np.argmax(free, axis=1)
        to[m, a], to[m, b] = b, a
        src[m, a], src[m, b] = col[m, b], col[m, a]
        link = np.zeros((len(m), 16), np.int64)
        np.put_along_axis(link, o, np.take_along_axis(o, to, axis=1), axis=1)
        e = np.zeros((N, 8, C), np.int64)
        np.put_along_axis(e, col.reshape(N, 8, C), src.reshape(N, 8, C), axis=2)
        for r in range(N):
            both = np.concatenate([own[r], decode(sent[r ^ mask])], axis=1).astype(BF)
            z = ((own[r] + gcols(both, e[r]).astype(np.float32)) * np.float32(0.5)).astype(BF)
            qz = mx_ref.quantize(z)
            now[r] = tile([mx_ref.matmul(pick(lay[r], np.arange(128 * k, 128 * k + 128)), qz) * np.float32(0.03125) + z[:, k::4].astype(np.float32) for k in range(4)])
    y = np.zeros((N, 128, C), np.float32)
    oc, osc = np.zeros((N, 128, 4 * C), np.uint8), np.zeros((N, 16, C), np.uint8)
    for r in range(N):
        q = mx_ref.quantize(now[r])
        y[r] = mx_ref.matmul(mx_ref.quantize(v[r]), q)
        oc[r], osc[r] = emit(q)
    return {"y": y, "op": link.reshape(N, 8, C).astype(np.float32), "oc": oc, "osc": osc}

@@ -1,0 +1,654 @@
+import math
+import numpy as np
+from concourse.mybir import dt, AluOpType as OP, ActivationFunctionType as AF
+
+ROUNDS = 3
+F, B, I, U, Q4, S1 = "float32", "bfloat16", "int32", "uint16", "float8_e4m3fn_x4", "uint8"
+SIZE = {F: 4, B: 2, I: 4, U: 2, Q4: 4, S1: 1}
+BUF = {
+    "xt": (B, 1024), "qx": (Q4, 256), "sx": (S1, 256), "ut": (B, 512), "qu0": (Q4, 128), "su0": (S1, 128), "qu": (Q4, 128), "su": (S1, 128),
+    "vt": (B, 512), "qv": (Q4, 128), "sv": (S1, 128), "qw": (Q4, 512), "sw": (S1, 512), "ez": (B, 520), "qe": (Q4, 512), "se": (S1, 512),
+    "fw": (B, 1536), "give": (B, 512), "hn": (B, 1024), "zt": (B, 1024), "z32": (B, 1024), "x32": (B, 1024), "qz": (Q4, 256), "sz": (S1, 256),
+    "ysb": (F, 256), "lq": (Q4, 352), "ls": (S1, 352),
+    "pi": (I, 8), "pf": (F, 16), "iof": (F, 32), "lc": (U, 208), "la": (I, 96), "lb": (I, 128), "rm": (B, 256), "ms": (B, 256), "ib": (B, 256),
+    "tc": (B, 256), "yc": (B, 128), "dn": (B, 256), "ns": (B, 256), "didb": (B, 128), "scv": (B, 256), "z16": (F, 16), "pw2": (B, 16),
+    "ni": (I, 32), "nf": (F, 64), "nt": (F, 64), "t3": (F, 64), "lg1": (U, 16), "lnod": (U, 16), "rr": (B, 256), "r5": (B, 512), "t5": (B, 512),
+    "sel": (F, 16), "inv": (U, 16), "dcol": (B, 16), "dcolb": (B, 256), "dca": (B, 16), "sm": (F, 96),
+    "ssb": (F, 256), "g1": (F, 256), "tr": (F, 256), "gb": (F, 256), "c1": (B, 256), "s1": (B, 256), "own": (F, 64), "w": (B, 16),
+    "dst": (B, 16), "dstb": (B, 256), "sti": (B, 256), "sto": (B, 128), "pr": (B, 256), "bm": (F, 256), "gg": (F, 16),
+    "ai": (F, 256), "c2": (B, 256), "posm": (B, 256), "sp": (B, 256), "df": (F, 48), "fl": (F, 96), "pay": (F, 64), "d3": (B, 48), "db": (B, 384),
+    "mk": (B, 256), "eb": (B, 384), "ef": (F, 256), "vl": (U, 8), "vs": (F, 32), "ds": (F, 16), "dsb": (F, 256), "vp": (F, 32),
+    "qq": (B, 256), "rq": (B, 256), "rd": (B, 256), "av": (B, 256), "n1": (B, 256), "n3": (B, 256), "px": (B, 32), "vv": (B, 16),
+    "ma": (B, 64), "mm": (B, 256), "sr": (F, 256), "sl": (U, 16), "mo": (B, 256), "dp": (B, 16), "dpb": (B, 256), "ep": (B, 256),
+    "pmd": (B, 256), "pms": (B, 256), "pm": (B, 256), "cp": (B, 256), "v0": (B, 16), "val": (F, 48), "w4": (I, 64), "bits": (I, 256), "lk": (F, 16),
+}
+for _r in range(ROUNDS):
+    BUF["ws%d" % _r] = (B, 8)
+    BUF["ct%d" % _r] = (B, 32)
+    BUF["qo%d" % _r] = (Q4, 128)
+    BUF["so%d" % _r] = (S1, 128)
+PS = {"pa": 2048, "ps": 1024}
+HOME, _fill = {}, {"shortf": 0, "shortb": 0}
+for _k in ("pf", "sel", "sm", "gg", "df", "fl", "pay", "vs", "ds", "vp", "val", "pw2", "dcol", "dca", "w", "dst", "d3", "px", "vv", "ma", "dp", "v0"):
+    _h = "shortf" if BUF[_k][0] == F else "shortb"
+    HOME[_k] = (_h, _fill[_h])
+    _fill[_h] += BUF[_k][1]
+SCRATCH = {k: ("sbuf", [128, n], d) for k, (d, n) in BUF.items() if k not in HOME}
+SCRATCH["shortf"] = ("sbuf", [128, _fill["shortf"]], F)
+SCRATCH["shortb"] = ("sbuf", [128, _fill["shortb"]], B)
+for _k, _n in PS.items():
+    SCRATCH[_k] = ("psum", [128, _n], F)
+QUEUES = ["v", "a", "p", "g", "s"]
+NDMA = 16
+SEMAPHORES = ["q" + q for q in QUEUES] + ["d%d" % i for i in range(NDMA)] + ["sent"] + ["aw%d" % r for r in range(ROUNDS)] + ["av%d" % r for r in range(ROUNDS)]
+
+CYC = 1.0
+WAKES = ((50.0, 100.0), (100.0, 200.0), (25.0, 100.0))
+PLANS = [(p, k) for p in (100.0, 200.0, 400.0) for k in range(6)]
+MOVES, SLACK = 40000, 40.0
+LN2 = math.log(2.0)
+HALF = 32767.5
+STEP, TOP = 0.0625, 1.9375
+LD, LO, LE, LI, LO16, L8, L8B, LA, LB, LU, LT3, LSEL, LR = 0, 32, 80, 88, 104, 120, 128, 136, 152, 168, 176, 180, 184
+
+
+def V(name, lo=0, hi=None, step=1):
+    if hi is None:
+        hi = (BUF[name][1] if name in BUF else PS[name])
+    return (name, lo, hi, step)
+
+
+def col(name, c):
+    return (name, c, c + 1, 1)
+
+
+def L(at, n):
+    return V("lc", at, at + n)
+
+
+def G(win, off):
+    return ("@", win, off)
+
+
+def count(v):
+    if v[0] == "@":
+        return 16 * count(v[2])
+    return len(range(v[1], v[2], v[3]))
+
+
+def cells(v):
+    if v[0] == "@":
+        return cells(v[1]) | cells(v[2])
+    if v[0] in PS:
+        return {(v[0], c // 512) for c in range(v[1], v[2], v[3])}
+    return {(v[0], c) for c in range(v[1], v[2], v[3])}
+
+
+def narrow(*vs):
+    return all(v[0] in BUF and SIZE[BUF[v[0]][0]] == 2 for v in vs)
+
+
+def program():
+    ops = []
+
+    def add(q, kind, args, reads, writes, cost, late=0.0):
+        ops.append({"q": q, "kind": kind, "args": args, "r": [x for x in reads if isinstance(x, tuple)], "w": writes, "cost": cost, "late": late})
+
+    def vcost(n, src, per):
+        if src[0] == "@":
+            return 50 + 1.5 * n * CYC
+        return max(64, n * per) * CYC
+
+    def cp(out, src):
+        if out[0] == "@":
+            add("v", "copy", (out, src), [src, out[2]], [out[1]], 50 + 3.0 * count(src) * CYC)
+        else:
+            add("v", "copy", (out, src), [src], [out], vcost(count(out), src, 0.5 if narrow(out, src) else 1))
+
+    def tt(out, a, b, op):
+        add("v", "tt", (out, a, b, op), [a, b], [out], vcost(count(out), a, 1 if a[0] in PS else 2))
+
+    def ts(out, a, s1, op0, s2=None, op1=None):
+        add("v", "ts", (out, a, s1, s2, op0, op1), [a, s1, s2], [out], vcost(count(out), a, 0.5 if narrow(out, a) else 1))
+
+    def scan(out, d0, d1, op0=OP.mult, op1=OP.add, init=0.0):
+        add("v", "scan", (out, d0, d1, init, op0, op1), [d0, d1], [out], vcost(count(out), d0, 0.5 if narrow(out, d0, d1) else 1))
+
+    def tp(out, src):
+        add("v", "tp", (out, src), [src], [out], vcost(count(out), src, 0.5 if narrow(out, src) else 1))
+
+    def fill(out, c):
+        add("v", "fill", (out, c), [], [out], vcost(count(out), out, 0.5 if narrow(out) else 1))
+
+    def quant(q, s, src):
+        add("v", "quant", (q, s, src), [src], [q, s], 12 + 0.22 * count(src) * 1.2)
+
+    def act(out, src, func=AF.Copy, scale=1.0, bias=None):
+        n = count(out)
+        add("a", "act", (out, src, func, scale, bias), [src, bias], [out], 65 + 1.5 * n * CYC if src[0] == "@" else max(64, n) * CYC)
+
+    def mx(out, lq, ls, rq, rs):
+        add("p", "mx", (out, lq, ls, rq, rs), [lq, ls, rq, rs], [out], (count(out) + 16) * CYC)
+
+    def iota(out, pattern, base, chan):
+        add("g", "iota", (out, pattern, base, chan), [], [out], 130 + 2 * count(out) * CYC)
+
+    def load(q, out, name, after=()):
+        add(q, "load", (out, name), [name] + list(after), [out], 60, 2000.0)
+
+    def store(q, name, src, part=None):
+        add(q, "store", (name, src, part), [src], [], 60, 2000.0 if part is not None else 2400.0)
+
+    def send(r, sem, out, src, late):
+        add("g", "send", (r, sem, out, src), [src], [out], 300, late)
+
+    def level(out, c):
+        act(out, V("ib", 0, count(out)), AF.Identity, 0.0, c)
+
+    last16 = lambda name, lo=0, n=256: V(name, lo + 15, lo + n, 16)
+    z = lambda n: V("z16", 0, n)
+    io = lambda n, lo=0: V("iof", lo, lo + n)
+
+    load("s", V("ni", 16, 32), "par")
+    load("a", V("ni", 0, 16), "nod")
+    load("s", V("xt"), "x")
+    load("a", V("ut"), "u")
+    for out, name in (("qw", "wc"), ("sw", "ws"), ("vt", "v")):
+        load("s", V(out), name, (col("xt", 0), col("ut", 0)))
+
+    iota(V("pi", 0, 1), [[0, 1]], 0, 1)
+    iota(V("iof"), [[1, 32]], 0, 0)
+    p0 = col("pi", 0)
+    for i, (shift, mask) in enumerate(((0, 15), (4, 1), (0, 7), (0, 1), (0, 31), (1, 7), (3, 1))):
+        ts(col("pi", 1 + i), p0, shift, OP.logical_shift_right, mask, OP.bitwise_and)
+    cp(V("pf", 0, 7), V("pi", 1, 8))
+    pq, ph, p8, p2, p32, pj, pe = [col("pf", i) for i in range(7)]
+    fill(V("z16"), 0.0)
+    iota(V("lb", 0, 32), [[16, 16], [0, 2]], 0, 0)
+    iota(V("lb", 32, 80), [[16, 3], [0, 16]], 0, 0)
+    ts(L(LD, 80), V("lb", 0, 80), pq, OP.add)
+    ts(col("pf", 7), ph, 8.0, OP.mult, pj, OP.add)
+    ts(L(LT3, 1), p2, 16.0, OP.mult, col("pf", 7), OP.add)
+    ts(L(LT3 + 1, 1), p32, 32.0, OP.add)
+    cp(L(LT3 + 2, 1), p32)
+    ts(col("pf", 8), pq, 16.0, OP.mult, 15.0, OP.add)
+    ts(L(LE, 8), z(8), col("pf", 8), OP.add)
+    ts(col("pf", 9), pq, 8.0, OP.mult, 7.0, OP.add)
+    ts(L(LR, 16), z(16), col("pf", 9), OP.add)
+    iota(V("lb", 80, 96), [[1, 16]], 0, 0)
+    iota(V("lb", 96, 112), [[16, 16]], 15, 0)
+    cp(L(LI, 32), V("lb", 80, 112))
+    ts(col("pf", 10), ph, 16.0, OP.mult)
+    ts(L(LSEL, 1), pq, 32.0, OP.mult, col("pf", 10), OP.add)
+    ts(col("pf", 11), p2, 16.0, OP.mult)
+    iota(V("la", 32, 40), [[32, 4], [0, 2]], 0, 0)
+    ts(L(LU, 8), V("la", 32, 40), col("pf", 11), OP.add)
+    ts(col("pf", 12), p8, 0.0, OP.is_equal)
+    ts(col("pf", 13), p8, 0.0, OP.is_gt, 16.0, OP.mult)
+    ts(col("pf", 14), p8, col("pf", 13), OP.add)
+    ts(col("pf", 15), col("pf", 13), 0.4375, OP.mult, col("pf", 14), OP.add)
+    ts(V("la", 0, 8), io(8), 2.0, OP.mult, pe, OP.add)
+    ts(L(L8, 8), V("la", 0, 8), col("pf", 12), OP.mult, col("pf", 14), OP.add)
+    ts(L(L8B, 8), V("la", 0, 8), col("pf", 12), OP.mult, col("pf", 15), OP.add)
+    ts(V("la", 48, 64), io(16), pq, OP.max)
+    ts(V("la", 64, 80), io(16), pq, OP.min)
+    ts(V("w4", 0, 32), V("la", 48, 80), 3, OP.logical_shift_right)
+    ts(V("w4", 32, 64), V("w4", 0, 32), -240.0, OP.mult, ph, OP.add)
+    ts(V("w4", 0, 32), V("la", 48, 80), 32.0, OP.mult)
+    tt(V("fl", 0, 32), V("w4", 0, 32), V("w4", 32, 64), OP.add)
+    cp(L(LA, 32), V("fl", 0, 32))
+    fill(V("rm"), 1.0)
+    fill(V("rm", 0, 256, 16), 0.0)
+    fill(V("ms"), 1.0)
+    fill(V("ms", 0, 256, 16), 0.0)
+    fill(V("ms", 17, 256, 17), -1.0)
+    fill(V("pmd"), -1.0)
+    fill(col("t3", 48), 0.0)
+    fill(V("give", 448, 512), 0.0)
+    act(V("pw2"), io(16), AF.Exp, LN2)
+    ops[-1]["cost"] += 1500.0
+    fill(V("ez"), 0.5)
+    iota(V("ib"), [[1, 16], [0, 16]], 0, 0)
+    add("g", "select", (V("ez"), [[1, 520]], OP.is_equal, 0.0, -3, -4), [V("ez")], [V("ez")], 170 + 1040 * CYC)
+    iota(V("yc"), [[1, 16], [0, 8]], 0, 0)
+    iota(V("scv"), [[1, 16], [16, 16]], 0, 0)
+    level(V("dn"), STEP)
+    level(V("dn", 0, 256, 16), -64.0)
+    level(V("rd"), STEP)
+    level(V("ns"), 0.0)
+    act(V("ns", 0, 256, 16), io(16), AF.Copy, -1.0)
+    level(V("didb"), -1.0)
+    level(V("didb", 15, 128, 16), 15.0)
+    for name, c, value in (("own", 48, 0.0), ("pay", 48, 0.0), ("vs", 16, 0.0), ("vp", 16, 0.0), ("vp", 0, 16.0), ("n3", 15, 4.0), ("vv", 0, 1.0)):
+        level(col(name, c), value)
+    level(V("rr"), 0.0)
+    act(V("own", 16, 32), io(16))
+    ts(V("vs", 8, 15), io(7, 16), 16.0, OP.mult, pq, OP.add)
+    act(V("yc"), V("yc"), AF.Identity, -STEP, TOP)
+    act(V("tc"), V("ib"), AF.Identity, -STEP, 15 * STEP)
+    for r in range(ROUNDS):
+        act(V("ct%d" % r, 0, 16), io(16), AF.Identity, -STEP, TOP)
+    for b in range(4):
+        quant(V("qe", 128 * b, 128 * b + 128), V("se", 128 * b, 128 * b + 128), V("ez", 3 - b, 515 - b))
+
+    cp(V("nf"), G(V("ni"), L(LD, 4)))
+    tp(V("nt"), V("nf"))
+    cp(V("t3", 0, 48), G(V("nt"), L(LT3, 3)))
+    par0, colv = V("t3", 16, 32), V("t3", 32, 48)
+    cp(V("lg1"), V("t3", 0, 16))
+    act(V("own", 0, 16), colv)
+    tt(V("dcol"), colv, V("t3", 33, 49), OP.subtract)
+    act(V("dcolb"), G(V("dcol"), L(LO, 16)))
+    act(V("dca", 0, 15), V("dcol", 0, 15))
+    quant(V("qu0"), V("su0"), V("ut"))
+    add("v", "pickq", (V("qu"), V("qu0"), L(LU, 8)), [V("qu0"), L(LU, 8)], [V("qu")], 50 + 1.5 * 128 * CYC)
+    add("a", "picks", (V("su"), V("su0"), L(LU, 8)), [V("su0"), L(LU, 8)], [V("su")], 65 + 1.5 * 128 * CYC)
+    quant(V("qv"), V("sv"), V("vt"))
+
+    def parent_mask(parents, first):
+        (cp if first else act)(V("pmd", 0, 256, 16), parents)
+        scan(V("pms"), V("rm"), V("pmd"))
+        if first:
+            ts(V("pm"), V("pms"), 0.0, OP.not_equal)
+        else:
+            act(V("pm"), V("pms"), AF.Sign, -1.0)
+        tt(V("df", 16, 32), V("own", 16, 32), parents, OP.subtract)
+        scan(V("cp"), V("pm"), V("dcolb"))
+        tt(V("df", 0, 16), V("own", 0, 16), last16("cp"), OP.subtract)
+
+    def ancestors():
+        cur = V("v0")
+        for k in range(16):
+            ts(V("val", 32, 48), cur, float(2 ** (k + 1)), OP.is_lt, col(cur[0], cur[1] + k), OP.mult)
+            nxt = V("val", 16 * (k % 2), 16 * (k % 2) + 16)
+            tt(nxt, cur, V("val", 32, 48), OP.add)
+            cur = nxt
+        tt(V("w4", 0, 16), cur, V("pw2"), OP.add)
+        ts(V("w4", 16, 32), V("w4", 0, 16), 1, OP.logical_shift_right)
+        ts(V("w4", 32, 64), V("w4", 0, 32), 2, OP.logical_shift_right)
+        for j in range(4):
+            ts(V("bits", 64 * j, 64 * j + 64), V("w4"), 4 * j, OP.logical_shift_right, 1, OP.bitwise_and)
+
+    parent_mask(par0, True)
+    tt(V("dp"), par0, V("t3", 17, 33), OP.subtract)
+    act(V("dpb"), G(V("dp"), L(LO, 16)))
+    scan(V("ep"), V("pm"), V("dpb"))
+    ts(V("sm", 0, 16), io(16), col("t3", 32), OP.subtract)
+    tt(V("sm", 16, 32), par0, io(16), OP.is_lt)
+    ts(V("sm", 32, 48), par0, 0.0625, OP.mult)
+    tt(V("sm", 48, 64), last16("ep"), V("sm", 0, 16), OP.is_equal)
+    tt(V("sm", 64, 80), V("sm", 48, 64), V("sm", 16, 32), OP.mult)
+    tt(V("sm", 80, 96), V("sm", 64, 80), V("sm", 32, 48), OP.max)
+    act(V("v0"), V("sm", 80, 96), AF.Exp, 16 * LN2)
+    ancestors()
+
+    cp(V("lnod"), V("ni", 0, 16))
+    cp(G(V("rr"), V("lnod")), V("scv"))
+    act(V("r5"), G(V("rr"), L(LD, 32)))
+    tp(V("t5"), V("r5"))
+    cp(V("sel"), G(V("t5"), L(LSEL, 1)))
+    cp(V("inv"), V("sel"))
+
+    bank = lambda b, n: V("pa", 512 * b, 512 * b + n)
+    eq = lambda b: (V("qe", 128 * b, 128 * b + 128), V("se", 128 * b, 128 * b + 128))
+    st = V("own", 32, 48)
+
+    def state_product(lq, ls):
+        for h in range(2):
+            q, s = V("qx", 128 * h, 128 * h + 128), V("sx", 128 * h, 128 * h + 128)
+            quant(q, s, V("xt", 512 * h, 512 * h + 512))
+            mx(V("ps", 512 * h, 512 * h + 128), lq, ls, q, s)
+
+    for r in range(ROUNDS):
+        ct, last, at = "ct%d" % r, r == ROUNDS - 1, 112 * (ROUNDS - 1 - r)
+        state_product(V("qu"), V("su"))
+        if r == 0:
+            load("s", V("lq", 336, 352), V("qx", 0, 16))
+            load("s", V("ls", 336, 352), V("sx", 0, 16))
+        for b in range(4):
+            mx(bank(b, 256), eq(b)[0], eq(b)[1], V("qx"), V("sx"))
+        for h in range(2):
+            act(V("ssb", 128 * h, 128 * h + 128), V("ps", 512 * h, 512 * h + 128))
+        act(V("g1"), G(V("ssb"), V("lg1")))
+        tp(V("tr"), V("g1"))
+        act(V("gb"), G(V("tr"), L(LB, 16)))
+        tt(V("c1"), G(V("tr"), L(LA, 16)), V("gb"), OP.is_gt)
+        scan(V("s1"), V("ms"), V("c1"))
+        tt(st, last16("s1"), io(16), OP.add)
+        for b in range(4):
+            act(V("fw", 384 * b, 384 * b + 256), bank(b, 256))
+        act(V("w"), st, AF.Exp, LN2)
+        tt(V("dst"), st, V("own", 33, 49), OP.subtract)
+        act(V("dstb"), G(V("dst"), L(LO, 16)))
+        tt(V("pr"), G(V("w"), L(LO, 16)), V("bits"), OP.mult)
+        scan(V("bm"), V("rm"), V("pr"))
+        act(V("gg"), last16("bm"), AF.Abs, 1.0, -HALF)
+        act(V("ai"), G(V("bm"), L(LO16, 16)), AF.Abs, 1.0, -HALF)
+        tt(V("c2"), G(V("gg"), L(LO, 16)), V("ai"), OP.is_gt)
+        scan(V("posm"), V("rm"), V("c2"))
+        scan(V("sp"), V("pm"), V("dstb"))
+        tt(V("df", 32, 48), st, last16("sp"), OP.subtract)
+        ts(V("fl", 0, 48), G(V("bm"), L(LE, 3)), HALF, OP.is_lt)
+        tt(V("fl", 48, 96), V("df"), V("fl", 0, 48), OP.mult)
+        tt(V("pay", 0, 48), V("own", 0, 48), V("fl", 48, 96), OP.subtract)
+        tt(V("d3"), V("pay", 0, 48), V("pay", 1, 49), OP.subtract)
+        act(V("db", 0, 128), G(V("d3"), L(LO + 32, 8)))
+        act(V("db", 128, 256), G(V("d3"), L(LO, 8)))
+        tt(V("mk", 128, 256), G(V("posm"), L(LE, 8)), V("ib", 128, 256), OP.not_equal)
+        scan(V("eb", 0, 128), V("mk", 128, 256), V("db", 0, 128))
+        ts(V("ws%d" % r), last16("eb", 0, 128), -STEP, OP.mult, TOP, OP.add)
+        send(r, "aw", V(ct, 24, 32), V("ws%d" % r), 1800.0)
+        scan(V("ef", 128, 256), V("mk", 128, 256), V("db", 128, 256))
+        ts(V("vl", 0, 7), last16("ef", 128, 112), col("pay", 16), OP.add)
+        for b in range(4):
+            src = G(V("fw", 384 * b, 384 * b + 256), V("vl", 0, 7))
+            if b % 2:
+                act(V("give", b, 448, 4), src, AF.Copy, 2.0)
+            else:
+                ts(V("give", b, 448, 4), src, 2.0, OP.mult)
+        quant(V("qo%d" % r), V("so%d" % r), V("give"))
+        send(r, "av", V("lq", at, at + 112), V("qo%d" % r, 0, 112), 3600.0 if last else 2300.0)
+        send(r, "av", V("ls", at, at + 112), V("so%d" % r, 0, 112), 3300.0 if last else 2000.0)
+        act(V("db", 256, 384), G(V("d3"), L(LO + 16, 8)))
+        act(V("sto"), G(st, L(LO, 8)), AF.Identity, -STEP, TOP)
+        act(V("sti"), G(st, L(LI, 16)), AF.Identity, -STEP, TOP)
+        tt(V("mk", 0, 128), G(V("posm"), L(LE, 8)), V("ib", 0, 128), OP.not_equal)
+        scan(V("eb", 128, 256), V("mk", 0, 128), V("db", 0, 128))
+        ts(V(ct, 16, 24), last16("eb", 128, 128), -STEP, OP.mult, TOP, OP.add)
+        scan(V("ef", 0, 128), V("mk", 0, 128), V("db", 128, 256))
+        ts(V("vs", 0, 8), last16("ef", 0, 128), col("pay", 16), OP.add)
+        ts(col("vs", 15), col("ef", 255), col("pay", 16), OP.add)
+        tt(V("ds"), V("vs", 0, 16), V("vs", 1, 17), OP.subtract)
+        act(V("dsb"), G(V("ds"), L(LO, 16)))
+        act(col("dca", 15), col("vs", 1), AF.Identity, -1.0, col("t3", 47))
+        scan(V("eb", 256, 384), V("mk", 0, 128), V("db", 256, 384))
+        ts(V("vp", 1, 8), V("eb", 256 + 31, 384, 16), col("pay", 32), OP.add)
+        tt(V("qq", 0, 128), G(V(ct, 0, 24), L(L8, 8)), V("yc"), OP.not_equal)
+        scan(V("rq", 0, 128), V("qq", 0, 128), V("rd", 0, 128))
+        act(V("rd", 128, 256, 8), V("rq", 7, 128, 8))
+        tt(V("qq", 128, 256), G(V(ct), L(L8B, 8)), V("yc"), OP.not_equal)
+        scan(V("rq", 128, 256), V("qq", 128, 256), V("rd", 128, 256))
+        tt(V("av", 0, 240), G(V("rq", 128, 256), L(LR, 15)), V("tc", 0, 240), OP.is_ge)
+        scan(V("n1", 0, 240), V("ns", 0, 240), V("av", 0, 240), OP.min, OP.add)
+        scan(V("n3", 16, 256), V("dn", 0, 240), V("n1", 0, 240), OP.add, OP.max)
+        tt(V("px", 0, 15), last16("n3", 16, 240), last16("n3", 0, 240), OP.is_lt)
+        tt(V("px", 16, 31), V(ct, 16, 31), V("px", 0, 15), OP.subtract)
+        tt(V("vv", 1, 16), last16("n3", 16, 240), V("px", 16, 31), OP.max)
+        ts(V("ma", 0, 16), V("sto", 0, 16), col("vv", 15), OP.not_equal)
+        scan(V("ma", 16, 32), V("ma", 0, 16), V("dca"))
+        act(V("dsb", 0, 256, 16), z(16), AF.Identity, 1.0, col("ma", 31))
+        tt(V("mm"), G(V("vv"), L(LO, 16)), V("sti"), OP.not_equal)
+        scan(V("sr"), V("mm"), V("dsb"))
+        cp(V("sl"), last16("sr"))
+        for b in range(4):
+            mx(bank(b, 128), eq(b)[0], eq(b)[1], V("lq", at, at + 128), V("ls", at, at + 128))
+            act(V("fw", 384 * b + 256, 384 * b + 368), bank(b, 112))
+        for b in range(4):
+            (cp if last and b == 0 else act)(V("hn", 256 * b, 256 * b + 256), G(V("fw", 384 * b, 384 * b + 368), V("sl")))
+            tt(V("zt", b, 1024, 4), G(V("hn", 256 * b, 256 * b + 256), V("inv")), V("fw", 384 * b, 384 * b + 256), OP.add)
+        quant(V("qz"), V("sz"), V("zt"))
+        for b in range(4):
+            act(V("z32", 256 * b, 256 * b + 256), V("zt", b, 1024, 4), AF.Copy, 32.0)
+        for b in range(4):
+            mx(bank(b, 256), V("qw", 128 * b, 128 * b + 128), V("sw", 128 * b, 128 * b + 128), V("qz"), V("sz"))
+        for b in range(4):
+            x32 = V("x32", 256 * b, 256 * b + 256)
+            tt(x32, bank(b, 256), V("z32", 256 * b, 256 * b + 256), OP.add)
+            if b < 3:
+                act(V("xt", b, 1024, 4), x32, AF.Copy, 0.03125)
+            else:
+                ts(V("xt", b, 1024, 4), x32, 0.03125, OP.mult)
+        tt(V("mo", 0, 128), G(V(ct, 16, 32), L(LI + 8, 8)), V("sto"), OP.not_equal)
+        scan(V("mo", 128, 256), V("mo", 0, 128), V("didb"))
+        act(V("vp", 8, 16), last16("mo", 128, 128))
+        if last:
+            scan(V("ma", 32, 48), V("ma", 0, 16), V("didb", 0, 16))
+            act(col("vp", 0), col("ma", 47))
+        tt(V("dp"), V("vp", 0, 16), V("vp", 1, 17), OP.subtract)
+        act(V("dpb"), G(V("dp"), L(LO, 16)))
+        scan(V("ep"), V("mm"), V("dpb"))
+        if last:
+            act(V("lk"), last16("ep"))
+            store("s", "op", V("lk"))
+        else:
+            act(V("v0"), last16("ep"), AF.Exp, LN2)
+            ancestors()
+            parent_mask(last16("ep"), False)
+    state_product(V("qv"), V("sv"))
+    store("s", "oc", V("qx"))
+    act(V("ysb", 0, 128), V("ps", 0, 128))
+    cp(V("ysb", 128, 256), V("ps", 512, 640))
+    store("a", "y", V("ysb"))
+    for k in range(4):
+        store("s", "osc", V("sx"), k)
+    return ops
+
+
+def replay(table, seq):
+    free, end, top = [0.0] * len(QUEUES), [0.0] * len(seq), 0.0
+    for n in seq:
+        q, cost, late, deps = table[n]
+        t = free[q]
+        for d, lag in deps:
+            if end[d] + lag > t:
+                t = end[d] + lag
+        t += cost
+        end[n] = free[q] = t
+        if late and t + late > top:
+            top = t + late
+    return top, end
+
+
+def order(ops):
+    writer, readers = {}, {}
+    for n, o in enumerate(ops):
+        deps, rd, wr = set(), set(), set()
+        for v in o["r"]:
+            rd |= cells(v)
+        for v in o["w"]:
+            wr |= cells(v)
+        wr |= {c for c in rd if c[0] in PS}
+        for c in rd | wr:
+            if c in writer:
+                deps.add(writer[c])
+        for c in wr:
+            deps |= readers.get(c, set())
+        for c in wr:
+            writer[c] = n
+            readers[c] = set()
+        for c in rd:
+            readers.setdefault(c, set()).add(n)
+        deps.discard(n)
+        o["deps"] = deps
+    flat = [[(QUEUES.index(o["q"]), o["cost"], o["late"], [(d, ops[d]["late"] + (a if ops[d]["q"] == o["q"] else b)) for d in sorted(o["deps"])]) for o in ops]
+            for a, b in WAKES]
+    score = lambda s: sum(replay(t, s)[0] for t in flat)
+    tail = [o["cost"] + o["late"] for o in ops]
+    users = [[] for o in ops]
+    for n in range(len(ops) - 1, -1, -1):
+        for d, lag in flat[0][n][3]:
+            tail[d] = max(tail[d], ops[d]["cost"] + lag + tail[n])
+            users[d].append(n)
+    best = None
+    for patience, grain in PLANS:
+        noise = np.random.default_rng(grain).random(len(ops)).tolist()
+        weight = [t + (300.0 * e if grain else 0.0) for t, e in zip(tail, noise)]
+        left = [len(o["deps"]) for o in ops]
+        ready = {n: 0.0 for n in range(len(ops)) if left[n] == 0}
+        free = {q: 0.0 for q in QUEUES}
+        end, seq = {}, []
+        while ready:
+            first = min(ready, key=lambda n: (max(ready[n], free[ops[n]["q"]]), n))
+            q = ops[first]["q"]
+            t = max(ready[first], free[q])
+            n, limit = None, None
+            for m in sorted([m for m in ready if ops[m]["q"] == q], key=lambda m: (-weight[m], m)):
+                if limit is None or max(ready[m], t) + ops[m]["cost"] <= limit:
+                    if ready[m] <= t:
+                        n = m
+                        break
+                    n = m if n is None or ready[m] < ready[n] else n
+                limit = ready[m] + patience if limit is None else min(limit, max(ready[m], t) + patience)
+            if ready[n] > t:
+                others = [max(ready[m], free[ops[m]["q"]]) for m in ready if ops[m]["q"] != q]
+                if others and min(others) < ready[n]:
+                    free[q] = min(others) + 1.0
+                    continue
+            end[n] = free[q] = max(ready.pop(n), free[q]) + ops[n]["cost"]
+            seq.append(n)
+            for m in users[n]:
+                left[m] -= 1
+                if left[m] == 0:
+                    ready[m] = max(end[d] + lag for d, lag in flat[0][m][3])
+        total = score(seq)
+        if best is None or total < best[0]:
+            best = (total, seq)
+    total, seq = best
+    for turn, (a, b, c) in enumerate(np.random.default_rng(7).random((MOVES, 3)).tolist()):
+        i = int(a * len(seq))
+        n = seq[i]
+        step, hops, j, to = (1 if b < 0.5 else -1), 1 + int(c * c * 8), i, None
+        stop = set(users[n]) if step > 0 else ops[n]["deps"]
+        while hops and 0 <= j + step < len(seq) and seq[j + step] not in stop:
+            j += step
+            if ops[seq[j]]["q"] == ops[n]["q"]:
+                hops -= 1
+                to = j
+        if to is None:
+            continue
+        new = seq[:i] + seq[i + 1:]
+        new.insert(to, n)
+        t = score(new)
+        if t <= total + SLACK * (1.0 - turn / MOVES):
+            total, seq = t, new
+            if turn % 8 == 0:
+                end = replay(flat[0], seq)[1]
+                seq.sort(key=lambda m: end[m] - ops[m]["cost"])
+    end = replay(flat[0], seq)[1]
+    for n, o in enumerate(ops):
+        o["at"] = end[n] - o["cost"]
+    place = {n: i for i, n in enumerate(seq)}
+    known = {q: {} for q in QUEUES}
+    for n in seq:
+        o = ops[n]
+        k = known[o["q"]]
+        need = {}
+        for d in o["deps"]:
+            kind = ops[d]["kind"]
+            key = ("in",) + ops[d]["args"][:2] if kind == "send" else ("dma", d) if kind in ("load", "store") else ops[d]["q"]
+            if k.get(key, -1) < place[d] and place[d] > place.get(need.get(key, -1), -1):
+                need[key] = d
+        waits = []
+        for key, d in sorted(need.items(), key=lambda e: -place[e[1]]):
+            if k.get(key, -1) >= place[d]:
+                continue
+            waits.append(d)
+            ops[d]["inc"] = True
+            if key[0] == "in":
+                k[key] = len(seq)
+                continue
+            k[key] = place[d]
+            for kk, vv in ops[d]["seen"].items():
+                if k.get(kk, -1) < vv:
+                    k[kk] = vv
+        o["waits"] = waits
+        o["seen"] = dict(k)
+    return seq
+
+
+OPS = program()
+SEQ = order(OPS)
+
+
+def rank_program(g, core, T, topo):
+    rank = T.rank_of(core)
+    if rank is None:
+        return
+    eng = {"v": g.vector, "a": g.scalar, "p": g.tensor, "g": g, "s": g.sync}
+
+    def ap(v):
+        if not isinstance(v, tuple):
+            return v
+        if v[0] == "@":
+            return ap(v[1]).indirect(ap(v[2]))
+        name, at = HOME.get(v[0], (v[0], 0))
+        if v[3] == 1:
+            return T[name][:, at + v[1]:at + v[2]]
+        return T[name][:, at + v[1]:at + v[2]:v[3]]
+
+    def raw(v):
+        return ap(v).bitcast(dt.uint8) if BUF[v[0]][0] == Q4 else ap(v)
+
+    partner = [T.cores[rank ^ (1 << r)] for r in range(ROUNDS)]
+    common = [e for e in topo.engines(core, partner[0]) if all(e in topo.engines(core, c) for c in partner)]
+    mask = sum(1 << e for e in common)
+    lanes = len(common)
+    done = {q: 0 for q in QUEUES}
+    mark, ndma, sent, stores = {}, [0], [0], []
+    for n in SEQ:
+        o = OPS[n]
+        e, kind, a = eng[o["q"]], o["kind"], o["args"]
+        for d in o["waits"]:
+            e.wait_ge(T.sem[mark[d][0]], mark[d][1])
+        if kind == "send":
+            r, sem, out, src = a
+            rid, pid, sengine = topo.addr(partner[r])
+            g.remote_dma(raw(out), raw(src), T.sem["%s%d" % (sem, r)], T.sem.sent, pid, rid, mask)
+            sent[0] += lanes
+            mark[n] = ("%s%d" % (sem, r), lanes * (1 if sem == "aw" else 2))
+            continue
+        if kind in ("load", "store"):
+            if kind == "load":
+                ins = e.dma_start(raw(a[0]), raw(a[1]) if isinstance(a[1], tuple) else T[a[1]][:])
+            elif a[2] is None:
+                ins = e.dma_start(T[a[0]][:], raw(a[1]))
+            else:
+                ins = e.dma_start(T[a[0]][4 * a[2]:4 * a[2] + 4, :], T[a[1][0]][32 * a[2]:32 * a[2] + 4, :])
+            mark[n] = ("d%d" % ndma[0], 16)
+            ndma[0] += 1
+            ins.then_inc(T.sem[mark[n][0]], 16)
+            if kind == "store":
+                stores.append((e, mark[n]))
+            continue
+        if kind == "copy":
+            ins = e.tensor_copy(ap(a[0]), ap(a[1]))
+        elif kind == "tt":
+            ins = e.tensor_tensor(ap(a[0]), ap(a[1]), ap(a[2]), a[3])
+        elif kind == "ts":
+            if a[5] is None:
+                ins = e.tensor_scalar(ap(a[0]), ap(a[1]), ap(a[2]), None, a[4])
+            else:
+                ins = e.tensor_scalar(ap(a[0]), ap(a[1]), ap(a[2]), ap(a[3]), a[4], a[5])
+        elif kind == "scan":
+            ins = e.tensor_tensor_scan(ap(a[0]), ap(a[1]), ap(a[2]), a[3], a[4], a[5])
+        elif kind == "tp":
+            ins = e.transpose(ap(a[0]), ap(a[1]))
+        elif kind == "fill":
+            ins = e.memset(ap(a[0]), a[1])
+        elif kind == "quant":
+            ins = e.quantize_mx(ap(a[0]), ap(a[1]), ap(a[2]))
+        elif kind == "act":
+            if a[4] is None:
+                ins = e.activation(ap(a[0]), ap(a[1]), a[2], scale=a[3])
+            else:
+                ins = e.activation(ap(a[0]), ap(a[1]), a[2], bias=ap(a[4]), scale=a[3])
+        elif kind == "mx":
+            ins = e.matmul_mx(ap(a[0]), ap(a[1]), ap(a[2]), ap(a[3]), ap(a[4]), True, True)
+        elif kind == "iota":
+            if BUF[a[0][0]][0] == I:
+                ins = e.iota(ap(a[0]), a[1], a[2], a[3])
+            else:
+                ins = e.iota(ap(a[0]), a[1], a[2], a[3], allow_small_or_imprecise_dtypes=True)
+        elif kind == "select":
+            ins = e.affine_select(ap(a[0]), ap(a[0]), a[1], a[2], a[3], a[4], a[5])
+        elif kind == "pickq":
+            ins = e.tensor_copy(ap(a[0]).bitcast(dt.uint32), ap(a[1]).bitcast(dt.uint32).indirect(ap(a[2])))
+        else:
+            ins = e.activation(ap(a[0]), ap(a[1]).indirect(ap(a[2])), AF.Copy)
+        if o.get("inc"):
+            done[o["q"]] += 1
+            mark[n] = ("q" + o["q"], done[o["q"]])
+            ins.then_inc(T.sem[mark[n][0]], 1)
+    g.wait_ge(T.sem.sent, sent[0])
+    for e, m in stores:
+        e.wait_ge(T.sem[m[0]], m[1])

@@ -11,7 +11,7 @@ BUF = {
     "fw": (B, 1536), "give": (B, 512), "hn": (B, 1024), "zt": (B, 1024), "z32": (B, 1024), "x32": (B, 1024), "qz": (Q4, 256), "sz": (S1, 256),
     "ysb": (F, 256), "lq": (Q4, 352), "ls": (S1, 352),
     "pi": (I, 8), "pf": (F, 16), "iof": (F, 32), "lc": (U, 208), "la": (I, 96), "lb": (I, 128), "rm": (B, 256), "ms": (B, 256), "ib": (B, 256),
-    "tc": (B, 256), "yc": (B, 128), "dn": (B, 256), "ns": (B, 256), "didb": (B, 128), "scv": (B, 256), "z16": (F, 16), "pw2": (B, 16),
+    "tc": (B, 256), "yc": (B, 128), "dn": (B, 256), "ns": (B, 256), "didb": (B, 128), "scv": (B, 256), "z16": (F, 16), "pw2": (B, 16), "jb": (B, 256),
     "ni": (I, 32), "nf": (F, 64), "nt": (F, 64), "t3": (F, 64), "lg1": (U, 16), "lnod": (U, 16), "rr": (B, 256), "r5": (B, 512), "t5": (B, 512),
     "sel": (F, 16), "inv": (U, 16), "dcol": (B, 16), "dcolb": (B, 256), "dca": (B, 16), "sm": (F, 96),
     "ssb": (F, 256), "g1": (F, 256), "tr": (F, 256), "gb": (F, 256), "c1": (B, 256), "s1": (B, 256), "own": (F, 64), "w": (B, 16),
@@ -19,8 +19,9 @@ BUF = {
     "ai": (F, 256), "c2": (B, 256), "posm": (B, 256), "sp": (B, 256), "df": (F, 48), "fl": (F, 96), "pay": (F, 64), "d3": (B, 48), "db": (B, 384),
     "mk": (B, 256), "eb": (B, 384), "ef": (F, 256), "vl": (U, 8), "vs": (F, 32), "ds": (F, 16), "dsb": (F, 256), "vp": (F, 32),
     "qq": (B, 256), "rq": (B, 256), "rd": (B, 256), "av": (B, 256), "n1": (B, 256), "n3": (B, 256), "px": (B, 32), "vv": (B, 16),
-    "ma": (B, 64), "mm": (B, 256), "sr": (F, 256), "sl": (U, 16), "mo": (B, 256), "dp": (B, 16), "dpb": (B, 256), "ep": (B, 256),
-    "pmd": (B, 256), "pms": (B, 256), "pm": (B, 256), "cp": (B, 256), "v0": (B, 16), "val": (F, 48), "w4": (I, 64), "bits": (I, 256), "lk": (F, 16),
+    "ma": (B, 64), "mm": (B, 256), "sr": (F, 256), "sl": (U, 16), "mo": (B, 256), "dp": (F, 16), "dpb": (F, 256), "ep": (F, 272),
+    "m2": (B, 256), "pm": (B, 256), "dv": (I, 96), "low": (I, 32), "dd": (F, 16), "ddb": (F, 256), "hop": (F, 256), "ve": (F, 64),
+    "cp": (B, 256), "v0": (B, 16), "w4": (I, 64), "bits": (I, 256), "lk": (F, 16),
 }
 for _r in range(ROUNDS):
     BUF["ws%d" % _r] = (B, 8)
@@ -29,7 +30,7 @@ for _r in range(ROUNDS):
     BUF["so%d" % _r] = (S1, 128)
 PS = {"pa": 2048, "ps": 1024}
 HOME, _fill = {}, {"shortf": 0, "shortb": 0}
-for _k in ("pf", "sel", "sm", "gg", "df", "fl", "pay", "vs", "ds", "vp", "val", "pw2", "dcol", "dca", "w", "dst", "d3", "px", "vv", "ma", "dp", "v0"):
+for _k in ("pf", "sel", "sm", "gg", "df", "fl", "pay", "vs", "ds", "vp", "dd", "ve", "pw2", "dcol", "dca", "w", "dst", "d3", "px", "vv", "ma", "dp", "v0"):
     _h = "shortf" if BUF[_k][0] == F else "shortb"
     HOME[_k] = (_h, _fill[_h])
     _fill[_h] += BUF[_k][1]
@@ -43,8 +44,8 @@ NDMA = 16
 SEMAPHORES = ["q" + q for q in QUEUES] + ["d%d" % i for i in range(NDMA)] + ["sent"] + ["aw%d" % r for r in range(ROUNDS)] + ["av%d" % r for r in range(ROUNDS)]
 
 CYC = 1.0
-WAKES = ((50.0, 100.0), (100.0, 200.0), (25.0, 100.0))
-PLANS = [(p, k) for p in (100.0, 200.0, 400.0) for k in range(6)]
+WAKES = ((120.0, 120.0), (180.0, 180.0), (120.0, 300.0))
+PLANS = [(p, k) for p in (200.0, 400.0, 800.0) for k in range(6)]
 MOVES, SLACK = 40000, 40.0
 LN2 = math.log(2.0)
 HALF = 32767.5
@@ -202,7 +203,10 @@ def program():
     fill(V("ms"), 1.0)
     fill(V("ms", 0, 256, 16), 0.0)
     fill(V("ms", 17, 256, 17), -1.0)
-    fill(V("pmd"), -1.0)
+    iota(V("jb"), [[0, 16], [1, 16]], 0, 0)
+    ts(V("jb"), V("jb"), 65536.0, OP.mult)
+    for c in (16, 48):
+        fill(col("dv", c), 0)
     fill(col("t3", 48), 0.0)
     fill(V("give", 448, 512), 0.0)
     act(V("pw2"), io(16), AF.Exp, LN2)
@@ -219,7 +223,7 @@ def program():
     act(V("ns", 0, 256, 16), io(16), AF.Copy, -1.0)
     level(V("didb"), -1.0)
     level(V("didb", 15, 128, 16), 15.0)
-    for name, c, value in (("own", 48, 0.0), ("pay", 48, 0.0), ("vs", 16, 0.0), ("vp", 16, 0.0), ("vp", 0, 16.0), ("n3", 15, 4.0), ("vv", 0, 1.0)):
+    for name, c, value in (("own", 48, 0.0), ("pay", 48, 0.0), ("vs", 16, 0.0), ("vp", 16, 0.0), ("ep", 271, 0.0), ("ve", 48, 0.0), ("n3", 15, 4.0), ("vv", 0, 1.0)):
         level(col(name, c), value)
     level(V("rr"), 0.0)
     act(V("own", 16, 32), io(16))
@@ -245,42 +249,51 @@ def program():
     add("a", "picks", (V("su"), V("su0"), L(LU, 8)), [V("su0"), L(LU, 8)], [V("su")], 65 + 1.5 * 128 * CYC)
     quant(V("qv"), V("sv"), V("vt"))
 
-    def parent_mask(parents, first):
-        (cp if first else act)(V("pmd", 0, 256, 16), parents)
-        scan(V("pms"), V("rm"), V("pmd"))
-        if first:
-            ts(V("pm"), V("pms"), 0.0, OP.not_equal)
-        else:
-            act(V("pm"), V("pms"), AF.Sign, -1.0)
-        tt(V("df", 16, 32), V("own", 16, 32), parents, OP.subtract)
-        scan(V("cp"), V("pm"), V("dcolb"))
-        tt(V("df", 0, 16), V("own", 0, 16), last16("cp"), OP.subtract)
-
-    def ancestors():
-        cur = V("v0")
-        for k in range(16):
-            ts(V("val", 32, 48), cur, float(2 ** (k + 1)), OP.is_lt, col(cur[0], cur[1] + k), OP.mult)
-            nxt = V("val", 16 * (k % 2), 16 * (k % 2) + 16)
-            tt(nxt, cur, V("val", 32, 48), OP.add)
-            cur = nxt
-        tt(V("w4", 0, 16), cur, V("pw2"), OP.add)
+    def ancestors(cur, nxt, win):
+        for k in range(4):
+            mask = V("m2") if k else V("pm")
+            tt(mask, win, V("jb"), OP.is_lt)
+            tt(V("dd"), cur, nxt, OP.subtract)
+            act(V("ddb"), G(V("dd"), L(LO, 16)))
+            scan(V("hop"), mask, V("ddb"))
+            if BUF[cur[0]][0] != I:
+                cp(V("low", 16, 32), cur)
+                cur = V("low", 16, 32)
+            ts(V("low", 0, 16), cur, 65535, OP.bitwise_and)
+            if k == 0:
+                ts(V("dv", 64, 80), cur, 16, OP.logical_shift_right)
+                tt(V("df", 16, 32), V("own", 16, 32), V("dv", 64, 80), OP.subtract)
+                scan(V("cp"), V("pm"), V("dcolb"))
+                tt(V("df", 0, 16), V("own", 0, 16), last16("cp"), OP.subtract)
+            if k == 3:
+                tt(V("low", 16, 32), V("low", 0, 16), V("pw2"), OP.add)
+                tt(V("w4", 0, 16), last16("hop"), V("low", 16, 32), OP.add)
+            else:
+                at = 32 * (k % 2)
+                cur, nxt = V("dv", at, at + 16), V("dv", at + 1, at + 17)
+                win = G(cur, L(LI, 16))
+                tt(cur, last16("hop"), V("low", 0, 16), OP.add)
         ts(V("w4", 16, 32), V("w4", 0, 16), 1, OP.logical_shift_right)
         ts(V("w4", 32, 64), V("w4", 0, 32), 2, OP.logical_shift_right)
         for j in range(4):
             ts(V("bits", 64 * j, 64 * j + 64), V("w4"), 4 * j, OP.logical_shift_right, 1, OP.bitwise_and)
 
-    parent_mask(par0, True)
+    ts(V("ve", 0, 16), par0, 65536.0, OP.mult)
+    tt(V("m2"), G(V("ve", 0, 16), L(LI, 16)), V("jb"), OP.is_lt)
     tt(V("dp"), par0, V("t3", 17, 33), OP.subtract)
     act(V("dpb"), G(V("dp"), L(LO, 16)))
-    scan(V("ep"), V("pm"), V("dpb"))
+    scan(V("ep", 0, 256), V("m2"), V("dpb"))
+    act(V("w"), par0, AF.Exp, LN2)
     ts(V("sm", 0, 16), io(16), col("t3", 32), OP.subtract)
     tt(V("sm", 16, 32), par0, io(16), OP.is_lt)
-    ts(V("sm", 32, 48), par0, 0.0625, OP.mult)
+    tt(V("ve", 16, 32), V("ve", 0, 16), V("w"), OP.add)
+    act(V("sm", 32, 48), io(16), AF.Copy, 65536.0)
+    tt(V("sm", 64, 80), V("sm", 32, 48), V("ve", 16, 32), OP.subtract)
+    tt(V("sm", 80, 96), V("sm", 64, 80), V("sm", 16, 32), OP.mult)
     tt(V("sm", 48, 64), last16("ep"), V("sm", 0, 16), OP.is_equal)
-    tt(V("sm", 64, 80), V("sm", 48, 64), V("sm", 16, 32), OP.mult)
-    tt(V("sm", 80, 96), V("sm", 64, 80), V("sm", 32, 48), OP.max)
-    act(V("v0"), V("sm", 80, 96), AF.Exp, 16 * LN2)
-    ancestors()
+    tt(V("sm", 32, 48), V("sm", 48, 64), V("sm", 80, 96), OP.mult)
+    tt(V("dv", 32, 48), V("sm", 32, 48), V("ve", 16, 32), OP.add)
+    ancestors(V("dv", 32, 48), V("dv", 33, 49), G(V("dv", 32, 48), L(LI, 16)))
 
     cp(V("lnod"), V("ni", 0, 16))
     cp(G(V("rr"), V("lnod")), V("scv"))
@@ -374,7 +387,8 @@ def program():
         tt(V("px", 0, 15), last16("n3", 16, 240), last16("n3", 0, 240), OP.is_lt)
         tt(V("px", 16, 31), V(ct, 16, 31), V("px", 0, 15), OP.subtract)
         tt(V("vv", 1, 16), last16("n3", 16, 240), V("px", 16, 31), OP.max)
-        ts(V("ma", 0, 16), V("sto", 0, 16), col("vv", 15), OP.not_equal)
+        tt(col("ma", 48), col("n3", 255), col(ct, 30), OP.max)
+        ts(V("ma", 0, 16), V("sto", 0, 16), col("ma", 48), OP.not_equal)
         scan(V("ma", 16, 32), V("ma", 0, 16), V("dca"))
         act(V("dsb", 0, 256, 16), z(16), AF.Identity, 1.0, col("ma", 31))
         tt(V("mm"), G(V("vv"), L(LO, 16)), V("sti"), OP.not_equal)
@@ -404,16 +418,20 @@ def program():
         if last:
             scan(V("ma", 32, 48), V("ma", 0, 16), V("didb", 0, 16))
             act(col("vp", 0), col("ma", 47))
-        tt(V("dp"), V("vp", 0, 16), V("vp", 1, 17), OP.subtract)
+            tt(V("dp"), V("vp", 0, 16), V("vp", 1, 17), OP.subtract)
+        else:
+            act(V("v0", 1, 16), V("vp", 1, 16), AF.Exp, LN2)
+            act(V("ve", 1, 16), V("vp", 1, 16), AF.Copy, 65536.0)
+            act(col("ve", 32), col("vp", 15), AF.Copy, 65536.0)
+            tt(V("ve", 33, 48), V("ve", 1, 16), V("v0", 1, 16), OP.add)
+            tt(V("dp"), V("ve", 32, 48), V("ve", 33, 49), OP.subtract)
         act(V("dpb"), G(V("dp"), L(LO, 16)))
-        scan(V("ep"), V("mm"), V("dpb"))
+        scan(V("ep", 0, 256), V("mm"), V("dpb"))
         if last:
             act(V("lk"), last16("ep"))
             store("s", "op", V("lk"))
         else:
-            act(V("v0"), last16("ep"), AF.Exp, LN2)
-            ancestors()
-            parent_mask(last16("ep"), False)
+            ancestors(last16("ep"), last16("ep", 16), G(V("ep", 0, 256), L(LO16, 16)))
     state_product(V("qv"), V("sv"))
     store("s", "oc", V("qx"))
     act(V("ysb", 0, 128), V("ps", 0, 128))

@@ -10,27 +10,27 @@ BUF = {
     "vt": (B, 512), "qv": (Q4, 128), "sv": (S1, 128), "qw": (Q4, 512), "sw": (S1, 512), "ez": (B, 520), "qe": (Q4, 512), "se": (S1, 512),
     "fw": (B, 1536), "give": (B, 512), "hn": (B, 1024), "zt": (B, 1024), "z32": (B, 1024), "x32": (B, 1024), "qz": (Q4, 256), "sz": (S1, 256),
     "ysb": (F, 256), "lq": (Q4, 352), "ls": (S1, 352),
-    "pi": (I, 8), "pf": (F, 16), "iof": (F, 32), "lc": (U, 208), "la": (I, 96), "lb": (I, 128), "rm": (B, 256), "ms": (B, 256), "ib": (B, 256),
-    "tc": (B, 256), "yc": (B, 128), "dn": (B, 256), "ns": (B, 256), "didb": (B, 128), "scv": (B, 256), "z16": (F, 16), "pw2": (B, 16), "jb": (B, 256),
-    "ni": (I, 32), "nf": (F, 64), "nt": (F, 64), "t3": (F, 64), "lg1": (U, 16), "lnod": (U, 16), "rr": (B, 256), "r5": (B, 512), "t5": (B, 512),
-    "sel": (F, 16), "inv": (U, 16), "dcol": (B, 16), "dcolb": (B, 256), "dca": (B, 16), "sm": (F, 96),
-    "ssb": (F, 256), "g1": (F, 256), "tr": (F, 256), "gb": (F, 256), "c1": (B, 256), "s1": (B, 256), "own": (F, 64), "w": (B, 16),
-    "dst": (B, 16), "dstb": (B, 256), "sti": (B, 256), "sto": (B, 128), "pr": (B, 256), "bm": (F, 256), "gg": (F, 16),
-    "ai": (F, 256), "c2": (B, 256), "posm": (B, 256), "sp": (B, 256), "df": (F, 48), "fl": (F, 96), "pay": (F, 64), "d3": (B, 48), "db": (B, 384),
-    "mk": (B, 256), "eb": (B, 384), "ef": (F, 256), "vl": (U, 8), "vs": (F, 32), "ds": (F, 16), "dsb": (F, 256), "vp": (F, 32),
-    "qq": (B, 256), "rq": (B, 256), "rd": (B, 256), "av": (B, 256), "n1": (B, 256), "n3": (B, 256), "px": (B, 32), "vv": (B, 16),
-    "ma": (B, 64), "mm": (B, 256), "sr": (F, 256), "sl": (U, 16), "mo": (B, 256), "dp": (F, 16), "dpb": (F, 256), "ep": (F, 272),
-    "m2": (B, 256), "pm": (B, 256), "dv": (I, 96), "low": (I, 32), "dd": (F, 16), "ddb": (F, 256), "hop": (F, 256), "ve": (F, 64),
-    "cp": (B, 256), "v0": (B, 16), "w4": (I, 64), "bits": (I, 256), "lk": (F, 16),
+    "pi": (I, 8), "pf": (F, 32), "iof": (F, 48), "lc": (U, 196), "la": (I, 96), "lb": (I, 96), "rm": (B, 256), "ms": (B, 256), "ib": (B, 256),
+    "scv": (B, 256), "z16": (F, 16), "pw2": (B, 16), "un": (F, 48), "a2": (B, 256), "aa": (F, 256),
+    "ni": (I, 32), "nf": (F, 64), "nt": (F, 64), "t3": (F, 48), "lg1": (U, 16), "lnod": (U, 16), "rr": (B, 256), "r5": (B, 512), "t5": (B, 512),
+    "sel": (F, 16), "inv": (U, 16), "dpk": (F, 16), "dpkb": (F, 128), "dca": (F, 16), "sm": (F, 112),
+    "ssb": (F, 256), "g1": (F, 256), "tr": (F, 256), "gb": (F, 256), "c1": (B, 256), "s1": (B, 256), "own": (F, 48), "w": (B, 16),
+    "dstb": (B, 256), "sti": (B, 256), "sto": (B, 128), "pr": (B, 256), "bm": (F, 256), "gg": (F, 16),
+    "ai": (F, 256), "c2": (B, 256), "posm": (B, 256), "sp": (B, 256), "df": (F, 32), "fl": (F, 64), "pay": (F, 48), "d3": (F, 32),
+    "dbp": (F, 128), "dbe": (B, 128), "mk": (B, 256), "eb": (B, 288), "ef": (F, 256), "vl": (U, 8), "vs": (F, 32), "ds": (F, 16), "dsb": (F, 256),
+    "vp": (F, 32), "oq": (B, 64), "ro": (B, 64), "ki": (B, 144), "qq": (B, 128), "rq": (B, 144), "dd": (B, 256), "fi": (B, 256), "ini": (B, 256),
+    "mg": (B, 256), "ma": (F, 48), "mm": (B, 256), "sr": (F, 256), "sl": (U, 16), "mo": (B, 128), "mp": (F, 128), "dp": (F, 16), "dpb": (F, 256),
+    "ep": (F, 256), "li": (I, 32), "p0": (U, 16), "p1": (U, 16), "cu": (F, 16), "hh": (F, 16), "ba": (F, 48), "ddb": (F, 256), "hop": (F, 256),
+    "w4": (I, 64), "bits": (I, 256), "lk": (F, 16),
 }
 for _r in range(ROUNDS):
-    BUF["ws%d" % _r] = (B, 8)
-    BUF["ct%d" % _r] = (B, 32)
+    BUF["ws%d" % _r] = (B, 64)
+    BUF["ct%d" % _r] = (B, 144)
     BUF["qo%d" % _r] = (Q4, 128)
     BUF["so%d" % _r] = (S1, 128)
 PS = {"pa": 2048, "ps": 1024}
 HOME, _fill = {}, {"shortf": 0, "shortb": 0}
-for _k in ("pf", "sel", "sm", "gg", "df", "fl", "pay", "vs", "ds", "vp", "dd", "ve", "pw2", "dcol", "dca", "w", "dst", "d3", "px", "vv", "ma", "dp", "v0"):
+for _k in ("pf", "sel", "sm", "gg", "df", "fl", "pay", "vs", "ds", "vp", "pw2", "dpk", "dca", "w", "d3", "ma", "dp", "un", "cu", "hh", "ba", "oq", "ro"):
     _h = "shortf" if BUF[_k][0] == F else "shortb"
     HOME[_k] = (_h, _fill[_h])
     _fill[_h] += BUF[_k][1]
@@ -49,8 +49,9 @@ PLANS = [(p, k) for p in (200.0, 400.0, 800.0) for k in range(6)]
 MOVES, SLACK = 40000, 40.0
 LN2 = math.log(2.0)
 HALF = 32767.5
-STEP, TOP = 0.0625, 1.9375
-LD, LO, LE, LI, LO16, L8, L8B, LA, LB, LU, LT3, LSEL, LR = 0, 32, 80, 88, 104, 120, 128, 136, 152, 168, 176, 180, 184
+PTR, LIFT = 2.0 ** 17, 2.0 ** 21
+ROUGH = 1.5 * 2.0 ** 24
+LD, LO, LE, LO16, LA, LB, LU, LT3, LSEL, LS, LOWN, LTR, LMO, LK, LSTI, LTO = 0, 32, 64, 72, 88, 104, 120, 128, 132, 136, 140, 144, 152, 160, 176, 192
 
 
 def V(name, lo=0, hi=None, step=1):
@@ -158,7 +159,8 @@ def program():
         load("s", V(out), name, (col("xt", 0), col("ut", 0)))
 
     iota(V("pi", 0, 1), [[0, 1]], 0, 1)
-    iota(V("iof"), [[1, 32]], 0, 0)
+    iota(V("iof", 0, 32), [[1, 32]], 0, 0)
+    iota(V("iof", 32, 48), [[-1, 16]], 16, 0)
     p0 = col("pi", 0)
     for i, (shift, mask) in enumerate(((0, 15), (4, 1), (0, 7), (0, 1), (0, 31), (1, 7), (3, 1))):
         ts(col("pi", 1 + i), p0, shift, OP.logical_shift_right, mask, OP.bitwise_and)
@@ -166,31 +168,68 @@ def program():
     pq, ph, p8, p2, p32, pj, pe = [col("pf", i) for i in range(7)]
     fill(V("z16"), 0.0)
     iota(V("lb", 0, 32), [[16, 16], [0, 2]], 0, 0)
-    iota(V("lb", 32, 80), [[16, 3], [0, 16]], 0, 0)
-    ts(L(LD, 80), V("lb", 0, 80), pq, OP.add)
+    iota(V("lb", 32, 64), [[16, 2], [0, 16]], 0, 0)
+    ts(L(LD, 64), V("lb", 0, 64), pq, OP.add)
     ts(col("pf", 7), ph, 8.0, OP.mult, pj, OP.add)
     ts(L(LT3, 1), p2, 16.0, OP.mult, col("pf", 7), OP.add)
     ts(L(LT3 + 1, 1), p32, 32.0, OP.add)
     cp(L(LT3 + 2, 1), p32)
     ts(col("pf", 8), pq, 16.0, OP.mult, 15.0, OP.add)
     ts(L(LE, 8), z(8), col("pf", 8), OP.add)
-    ts(col("pf", 9), pq, 8.0, OP.mult, 7.0, OP.add)
-    ts(L(LR, 16), z(16), col("pf", 9), OP.add)
-    iota(V("lb", 80, 96), [[1, 16]], 0, 0)
-    iota(V("lb", 96, 112), [[16, 16]], 15, 0)
-    cp(L(LI, 32), V("lb", 80, 112))
+    ts(L(LO16, 16), io(16), 16.0, OP.mult, 15.0, OP.add)
     ts(col("pf", 10), ph, 16.0, OP.mult)
     ts(L(LSEL, 1), pq, 32.0, OP.mult, col("pf", 10), OP.add)
     ts(col("pf", 11), p2, 16.0, OP.mult)
     iota(V("la", 32, 40), [[32, 4], [0, 2]], 0, 0)
     ts(L(LU, 8), V("la", 32, 40), col("pf", 11), OP.add)
-    ts(col("pf", 12), p8, 0.0, OP.is_equal)
-    ts(col("pf", 13), p8, 0.0, OP.is_gt, 16.0, OP.mult)
-    ts(col("pf", 14), p8, col("pf", 13), OP.add)
-    ts(col("pf", 15), col("pf", 13), 0.4375, OP.mult, col("pf", 14), OP.add)
+    ts(V("un", 16, 32), io(16), pq, OP.is_equal)
+    ts(V("un", 32, 48), io(16, 1), pq, OP.is_equal, -2.0, OP.mult)
+    tt(V("un", 0, 15), V("un", 16, 31), V("un", 32, 47), OP.add)
+    ts(col("un", 15), pq, 15.0, OP.is_equal, -2.0, OP.add)
+    ts(V("a2"), G(V("un", 0, 16), L(LO, 16)), 16.0, OP.mult)
+    act(V("aa"), V("a2"), AF.Copy, LIFT / 16)
+    drop, lifts = col("pf", 16), col("pf", 17)
+    ts(drop, col("un", 15), LIFT, OP.mult)
+    ts(lifts, col("un", 15), -LIFT, OP.mult)
     ts(V("la", 0, 8), io(8), 2.0, OP.mult, pe, OP.add)
-    ts(L(L8, 8), V("la", 0, 8), col("pf", 12), OP.mult, col("pf", 14), OP.add)
-    ts(L(L8B, 8), V("la", 0, 8), col("pf", 12), OP.mult, col("pf", 15), OP.add)
+    later, head = col("pf", 13), col("pf", 12)
+    ts(later, p8, 0.0, OP.is_gt)
+    ts(head, p8, 0.0, OP.is_equal, 128.0, OP.mult)
+    act(V("sm", 96, 100), io(4), AF.Identity, 32.0, 15.0)
+    ts(col("pf", 14), pe, 16.0, OP.mult)
+    ts(V("la", 8, 12), V("sm", 96, 100), col("pf", 14), OP.add, later, OP.mult)
+    ts(L(LOWN, 4), V("la", 8, 12), head, OP.add)
+    ts(V("la", 12, 16), V("la", 8, 12), 16.0, OP.add, 127.0, OP.min)
+    ts(V("sm", 100, 104), V("la", 12, 16), later, OP.mult, head, OP.add)
+    act(col("pf", 15), p8, AF.Identity, 16.0, 16.0)
+    ts(col("pf", 22), p8, 5.0, OP.is_le, col("pf", 15), OP.mult)
+    ts(col("pf", 23), col("sm", 100), col("pf", 22), OP.subtract, -31.0, OP.add)
+    ts(col("sm", 104), col("pf", 23), pe, OP.mult, col("pf", 22), OP.add)
+    ts(L(LS, 1), col("sm", 104), 31.0, OP.add)
+    cp(L(LS + 1, 3), V("sm", 101, 104))
+    act(col("pf", 24), p8, AF.Identity, 8.0, -72.0)
+    ts(V("la", 16, 20), V("la", 0, 4), p8, OP.is_ge, col("pf", 24), OP.mult)
+    ts(V("la", 20, 24), V("la", 16, 20), 63.0, OP.add, later, OP.mult)
+    ts(L(LTO, 4), V("la", 20, 24), 1.0, OP.add)
+    ts(col("pf", 25), p8, 1.0, OP.is_equal, 7.0, OP.mult)
+    ts(col("pf", 26), col("pf", 25), p8, OP.add, 5.0, OP.add)
+    ts(V("la", 24, 32), V("la", 0, 8), 6.0, OP.not_equal)
+    ts(V("la", 40, 48), V("la", 0, 8), 1.0, OP.add, p8, OP.is_ge)
+    tt(V("la", 80, 88), V("la", 24, 32), V("la", 40, 48), OP.mult)
+    ts(V("la", 88, 96), V("la", 80, 88), col("pf", 26), OP.mult, 1.0, OP.add)
+    ts(L(LTR, 8), V("la", 88, 96), later, OP.mult)
+    ts(L(LMO + 2, 6), io(6), 8.0, OP.add)
+    fill(L(LMO, 1), 2)
+    fill(L(LMO + 1, 1), 14)
+    ts(col("pf", 18), pq, 9.0, OP.is_ge, 2.0, OP.mult)
+    ts(col("pf", 27), pq, 2.0, OP.is_equal, 7.0, OP.mult)
+    ts(col("pf", 28), col("pf", 18), col("pf", 27), OP.add, pq, OP.add)
+    act(col("pf", 19), col("pf", 28), AF.Identity, 8.0, -145.0)
+    ts(col("pf", 29), pq, 2.0, OP.is_ge, col("pf", 19), OP.mult)
+    ts(L(LK, 16), z(16), col("pf", 29), OP.add, 128.0, OP.add)
+    ts(col("pf", 20), pq, 0.0, OP.is_gt)
+    ts(col("pf", 21), pq, 0.0, OP.is_equal, 16.0, OP.mult)
+    ts(L(LSTI, 16), io(16), col("pf", 20), OP.mult, col("pf", 21), OP.add)
     ts(V("la", 48, 64), io(16), pq, OP.max)
     ts(V("la", 64, 80), io(16), pq, OP.min)
     ts(V("w4", 0, 32), V("la", 48, 80), 3, OP.logical_shift_right)
@@ -203,35 +242,23 @@ def program():
     fill(V("ms"), 1.0)
     fill(V("ms", 0, 256, 16), 0.0)
     fill(V("ms", 17, 256, 17), -1.0)
-    iota(V("jb"), [[0, 16], [1, 16]], 0, 0)
-    ts(V("jb"), V("jb"), 65536.0, OP.mult)
-    for c in (16, 48):
-        fill(col("dv", c), 0)
-    fill(col("t3", 48), 0.0)
     fill(V("give", 448, 512), 0.0)
     act(V("pw2"), io(16), AF.Exp, LN2)
     ops[-1]["cost"] += 1500.0
     fill(V("ez"), 0.5)
-    iota(V("ib"), [[1, 16], [0, 16]], 0, 0)
+    iota(V("ib"), [[-1, 16], [0, 16]], 15, 0)
     add("g", "select", (V("ez"), [[1, 520]], OP.is_equal, 0.0, -3, -4), [V("ez")], [V("ez")], 170 + 1040 * CYC)
-    iota(V("yc"), [[1, 16], [0, 8]], 0, 0)
     iota(V("scv"), [[1, 16], [16, 16]], 0, 0)
-    level(V("dn"), STEP)
-    level(V("dn", 0, 256, 16), -64.0)
-    level(V("rd"), STEP)
-    level(V("ns"), 0.0)
-    act(V("ns", 0, 256, 16), io(16), AF.Copy, -1.0)
-    level(V("didb"), -1.0)
-    level(V("didb", 15, 128, 16), 15.0)
-    for name, c, value in (("own", 48, 0.0), ("pay", 48, 0.0), ("vs", 16, 0.0), ("vp", 16, 0.0), ("ep", 271, 0.0), ("ve", 48, 0.0), ("n3", 15, 4.0), ("vv", 0, 1.0)):
-        level(col(name, c), value)
-    level(V("rr"), 0.0)
-    act(V("own", 16, 32), io(16))
-    ts(V("vs", 8, 15), io(7, 16), 16.0, OP.mult, pq, OP.add)
-    act(V("yc"), V("yc"), AF.Identity, -STEP, TOP)
-    act(V("tc"), V("ib"), AF.Identity, -STEP, 15 * STEP)
+    for name, c in (("own", 32), ("pay", 32), ("vs", 0), ("vs", 16), ("vp", 16), ("dp", 0), ("eb", 128), ("eb", 272), ("rq", 128)):
+        level(col(name, c), 0.0)
+    for name, n in (("rr", 256), ("ki", 128), ("ini", 256)):
+        level(V(name, 0, n), 0.0)
+    level(col("ki", 128), 0.5)
+    ts(V("vs", 2, 9), io(7, 16), 16.0, OP.mult, pq, OP.add)
+    ts(V("vs", 2, 9), V("vs", 2, 9), 32.0, OP.mult)
     for r in range(ROUNDS):
-        act(V("ct%d" % r, 0, 16), io(16), AF.Identity, -STEP, TOP)
+        act(V("ct%d" % r, 0, 8), io(8), AF.Copy, 0.5)
+        level(V("ct%d" % r, 64, 80), 0.0)
     for b in range(4):
         quant(V("qe", 128 * b, 128 * b + 128), V("se", 128 * b, 128 * b + 128), V("ez", 3 - b, 515 - b))
 
@@ -239,61 +266,54 @@ def program():
     tp(V("nt"), V("nf"))
     cp(V("t3", 0, 48), G(V("nt"), L(LT3, 3)))
     par0, colv = V("t3", 16, 32), V("t3", 32, 48)
+    pk, en = V("own", 0, 16), V("own", 16, 32)
     cp(V("lg1"), V("t3", 0, 16))
-    act(V("own", 0, 16), colv)
-    tt(V("dcol"), colv, V("t3", 33, 49), OP.subtract)
-    act(V("dcolb"), G(V("dcol"), L(LO, 16)))
-    act(V("dca", 0, 15), V("dcol", 0, 15))
+    ts(V("sm", 0, 16), colv, 32.0, OP.mult)
+    tt(pk, V("sm", 0, 16), io(16), OP.add)
+    tt(V("dpk", 0, 15), V("own", 0, 15), V("own", 1, 16), OP.subtract)
+    act(col("dpk", 15), col("own", 15))
+    act(V("dpkb"), G(V("dpk"), L(LO, 8)))
+    act(V("dca", 0, 15), V("dpk", 0, 15))
     quant(V("qu0"), V("su0"), V("ut"))
     add("v", "pickq", (V("qu"), V("qu0"), L(LU, 8)), [V("qu0"), L(LU, 8)], [V("qu")], 50 + 1.5 * 128 * CYC)
     add("a", "picks", (V("su"), V("su0"), L(LU, 8)), [V("su0"), L(LU, 8)], [V("su")], 65 + 1.5 * 128 * CYC)
     quant(V("qv"), V("sv"), V("vt"))
 
-    def ancestors(cur, nxt, win):
+    def aim(cur):
+        ts(V("p1"), cur, 1 / PTR, OP.mult)
+        ts(V("hh"), V("p1"), PTR, OP.mult, lifts, OP.add)
+        tt(last16("aa"), cur, V("hh"), OP.subtract)
+
+    def ancestors(first):
         for k in range(4):
-            mask = V("m2") if k else V("pm")
-            tt(mask, win, V("jb"), OP.is_lt)
-            tt(V("dd"), cur, nxt, OP.subtract)
-            act(V("ddb"), G(V("dd"), L(LO, 16)))
-            scan(V("hop"), mask, V("ddb"))
-            if BUF[cur[0]][0] != I:
-                cp(V("low", 16, 32), cur)
-                cur = V("low", 16, 32)
-            ts(V("low", 0, 16), cur, 65535, OP.bitwise_and)
-            if k == 0:
-                ts(V("dv", 64, 80), cur, 16, OP.logical_shift_right)
-                tt(V("df", 16, 32), V("own", 16, 32), V("dv", 64, 80), OP.subtract)
-                scan(V("cp"), V("pm"), V("dcolb"))
-                tt(V("df", 0, 16), V("own", 0, 16), last16("cp"), OP.subtract)
-            if k == 3:
-                tt(V("low", 16, 32), V("low", 0, 16), V("pw2"), OP.add)
-                tt(V("w4", 0, 16), last16("hop"), V("low", 16, 32), OP.add)
-            else:
-                at = 32 * (k % 2)
-                cur, nxt = V("dv", at, at + 16), V("dv", at + 1, at + 17)
-                win = G(cur, L(LI, 16))
-                tt(cur, last16("hop"), V("low", 0, 16), OP.add)
+            act(V("ddb"), G(V("cu"), V("p1") if k else first), AF.Identity, 1.0, LIFT)
+            scan(V("hop"), V("ddb"), V("aa"), OP.max, OP.add)
+            if k < 3:
+                act(V("cu"), last16("hop"))
+                aim(last16("hop"))
+        cp(V("w4", 0, 16), last16("hop"))
         ts(V("w4", 16, 32), V("w4", 0, 16), 1, OP.logical_shift_right)
         ts(V("w4", 32, 64), V("w4", 0, 32), 2, OP.logical_shift_right)
         for j in range(4):
             ts(V("bits", 64 * j, 64 * j + 64), V("w4"), 4 * j, OP.logical_shift_right, 1, OP.bitwise_and)
 
-    ts(V("ve", 0, 16), par0, 65536.0, OP.mult)
-    tt(V("m2"), G(V("ve", 0, 16), L(LI, 16)), V("jb"), OP.is_lt)
-    tt(V("dp"), par0, V("t3", 17, 33), OP.subtract)
-    act(V("dpb"), G(V("dp"), L(LO, 16)))
-    scan(V("ep", 0, 256), V("m2"), V("dpb"))
-    act(V("w"), par0, AF.Exp, LN2)
-    ts(V("sm", 0, 16), io(16), col("t3", 32), OP.subtract)
+    cp(V("p0"), par0)
+    act(V("dstb"), G(par0, V("p0")), AF.Identity, 1.0, 16.0)
+    scan(V("sp"), V("dstb"), V("a2"), OP.max, OP.add)
+    act(V("ddb"), G(pk, V("p0")), AF.Identity, 1.0, LIFT)
+    scan(V("hop"), V("ddb"), V("aa"), OP.max, OP.add)
+    tt(V("df", 0, 16), pk, last16("hop"), OP.subtract)
+    ts(V("sm", 16, 32), par0, PTR, OP.mult)
+    tt(V("sm", 32, 48), V("sm", 16, 32), V("pw2"), OP.add)
+    act(V("sm", 48, 64), io(16), AF.Copy, PTR)
+    tt(V("sm", 64, 80), V("sm", 32, 48), V("sm", 48, 64), OP.subtract)
     tt(V("sm", 16, 32), par0, io(16), OP.is_lt)
-    tt(V("ve", 16, 32), V("ve", 0, 16), V("w"), OP.add)
-    act(V("sm", 32, 48), io(16), AF.Copy, 65536.0)
-    tt(V("sm", 64, 80), V("sm", 32, 48), V("ve", 16, 32), OP.subtract)
     tt(V("sm", 80, 96), V("sm", 64, 80), V("sm", 16, 32), OP.mult)
-    tt(V("sm", 48, 64), last16("ep"), V("sm", 0, 16), OP.is_equal)
-    tt(V("sm", 32, 48), V("sm", 48, 64), V("sm", 80, 96), OP.mult)
-    tt(V("dv", 32, 48), V("sm", 32, 48), V("ve", 16, 32), OP.add)
-    ancestors(V("dv", 32, 48), V("dv", 33, 49), G(V("dv", 32, 48), L(LI, 16)))
+    tt(V("sm", 48, 64), last16("sp"), io(16), OP.is_equal)
+    tt(V("sm", 64, 80), V("sm", 48, 64), V("sm", 80, 96), OP.mult)
+    tt(V("cu"), V("sm", 32, 48), V("sm", 64, 80), OP.subtract)
+    aim(V("cu"))
+    ancestors(V("p1"))
 
     cp(V("lnod"), V("ni", 0, 16))
     cp(G(V("rr"), V("lnod")), V("scv"))
@@ -304,7 +324,6 @@ def program():
 
     bank = lambda b, n: V("pa", 512 * b, 512 * b + n)
     eq = lambda b: (V("qe", 128 * b, 128 * b + 128), V("se", 128 * b, 128 * b + 128))
-    st = V("own", 32, 48)
 
     def state_product(lq, ls):
         for h in range(2):
@@ -327,32 +346,31 @@ def program():
         act(V("gb"), G(V("tr"), L(LB, 16)))
         tt(V("c1"), G(V("tr"), L(LA, 16)), V("gb"), OP.is_gt)
         scan(V("s1"), V("ms"), V("c1"))
-        tt(st, last16("s1"), io(16), OP.add)
+        tt(en, io(16, 32), last16("s1"), OP.subtract)
         for b in range(4):
             act(V("fw", 384 * b, 384 * b + 256), bank(b, 256))
-        act(V("w"), st, AF.Exp, LN2)
-        tt(V("dst"), st, V("own", 33, 49), OP.subtract)
-        act(V("dstb"), G(V("dst"), L(LO, 16)))
+        act(V("w"), en, AF.Exp, -LN2, 16 * LN2)
+        act(V("dstb"), G(en, V("p0")), AF.Identity, 1.0, 16.0)
         tt(V("pr"), G(V("w"), L(LO, 16)), V("bits"), OP.mult)
         scan(V("bm"), V("rm"), V("pr"))
         act(V("gg"), last16("bm"), AF.Abs, 1.0, -HALF)
         act(V("ai"), G(V("bm"), L(LO16, 16)), AF.Abs, 1.0, -HALF)
         tt(V("c2"), G(V("gg"), L(LO, 16)), V("ai"), OP.is_gt)
         scan(V("posm"), V("rm"), V("c2"))
-        scan(V("sp"), V("pm"), V("dstb"))
-        tt(V("df", 32, 48), st, last16("sp"), OP.subtract)
-        ts(V("fl", 0, 48), G(V("bm"), L(LE, 3)), HALF, OP.is_lt)
-        tt(V("fl", 48, 96), V("df"), V("fl", 0, 48), OP.mult)
-        tt(V("pay", 0, 48), V("own", 0, 48), V("fl", 48, 96), OP.subtract)
-        tt(V("d3"), V("pay", 0, 48), V("pay", 1, 49), OP.subtract)
-        act(V("db", 0, 128), G(V("d3"), L(LO + 32, 8)))
-        act(V("db", 128, 256), G(V("d3"), L(LO, 8)))
-        tt(V("mk", 128, 256), G(V("posm"), L(LE, 8)), V("ib", 128, 256), OP.not_equal)
-        scan(V("eb", 0, 128), V("mk", 128, 256), V("db", 0, 128))
-        ts(V("ws%d" % r), last16("eb", 0, 128), -STEP, OP.mult, TOP, OP.add)
-        send(r, "aw", V(ct, 24, 32), V("ws%d" % r), 1800.0)
-        scan(V("ef", 128, 256), V("mk", 128, 256), V("db", 128, 256))
-        ts(V("vl", 0, 7), last16("ef", 128, 112), col("pay", 16), OP.add)
+        scan(V("sp"), V("dstb"), V("a2"), OP.max, OP.add)
+        tt(V("df", 16, 32), en, last16("sp"), OP.subtract)
+        ts(V("fl", 0, 32), G(V("bm"), L(LE, 2)), HALF, OP.is_lt)
+        tt(V("fl", 32, 64), V("df"), V("fl", 0, 32), OP.mult)
+        tt(V("pay", 0, 32), V("own", 0, 32), V("fl", 32, 64), OP.subtract)
+        tt(V("d3"), V("pay", 0, 32), V("pay", 1, 33), OP.subtract)
+        act(V("dbe"), G(V("d3"), L(LO + 16, 8)))
+        act(V("dbp"), G(V("d3"), L(LO, 8)))
+        tt(V("mk", 0, 128), G(V("posm"), L(LE, 8)), V("ib", 0, 128), OP.not_equal)
+        scan(V("eb", 0, 128), V("mk", 0, 128), V("dbe"))
+        cp(V("ws%d" % r), G(V("eb", 0, 129), L(LS, 4)))
+        send(r, "aw", V(ct, 8, 64), V("ws%d" % r, 0, 56), 1900.0)
+        scan(V("ef", 0, 128), V("mk", 0, 128), V("dbp"))
+        ts(V("vl", 0, 7), last16("ef", 16, 112), col("pay", 16), OP.add, 1 / 32, OP.mult)
         for b in range(4):
             src = G(V("fw", 384 * b, 384 * b + 256), V("vl", 0, 7))
             if b % 2:
@@ -362,43 +380,46 @@ def program():
         quant(V("qo%d" % r), V("so%d" % r), V("give"))
         send(r, "av", V("lq", at, at + 112), V("qo%d" % r, 0, 112), 3600.0 if last else 2300.0)
         send(r, "av", V("ls", at, at + 112), V("so%d" % r, 0, 112), 3300.0 if last else 2000.0)
-        act(V("db", 256, 384), G(V("d3"), L(LO + 16, 8)))
-        act(V("sto"), G(st, L(LO, 8)), AF.Identity, -STEP, TOP)
-        act(V("sti"), G(st, L(LI, 16)), AF.Identity, -STEP, TOP)
-        tt(V("mk", 0, 128), G(V("posm"), L(LE, 8)), V("ib", 0, 128), OP.not_equal)
-        scan(V("eb", 128, 256), V("mk", 0, 128), V("db", 0, 128))
-        ts(V(ct, 16, 24), last16("eb", 128, 128), -STEP, OP.mult, TOP, OP.add)
-        scan(V("ef", 0, 128), V("mk", 0, 128), V("db", 128, 256))
-        ts(V("vs", 0, 8), last16("ef", 0, 128), col("pay", 16), OP.add)
-        ts(col("vs", 15), col("ef", 255), col("pay", 16), OP.add)
+        act(V("sto"), G(en, L(LO, 8)))
+        act(V("sti"), G(V("own", 16, 33), L(LSTI, 16)))
+        act(V("ini", 0, 256, 16), en, AF.Exp, 2 * LN2, -LN2)
+        act(V("ba", 32, 48), en, AF.Identity, 1.0, -2.0)
+        tt(V("mk", 128, 256), G(V("posm"), L(LE, 8)), V("ib", 128, 256), OP.not_equal)
+        scan(V("eb", 144, 272), V("mk", 128, 256), V("dbe"))
+        act(V(ct, 80, 144), G(V("eb", 144, 273), L(LOWN, 4)))
+        act(V("ki", 64, 128, 8), last16("eb", 144, 128))
+        tt(V("oq"), G(V("ki", 64, 129), L(LTO, 4)), V(ct, 80, 144), OP.not_equal)
+        scan(V("ro"), V("oq"), V("ki", 64, 128))
+        act(V("ki", 64, 128, 8), V("ro", 7, 64, 8))
+        scan(V("ef", 128, 256), V("mk", 128, 256), V("dbp"))
+        ts(V("vs", 9, 16), last16("ef", 128, 112), col("pay", 16), OP.add)
+        act(V("vp", 9, 16), last16("ef", 128, 112), AF.Identity, 1.0, col("pay", 16))
+        ts(col("vs", 1), col("ef", 15), col("pay", 16), OP.add)
         tt(V("ds"), V("vs", 0, 16), V("vs", 1, 17), OP.subtract)
         act(V("dsb"), G(V("ds"), L(LO, 16)))
-        act(col("dca", 15), col("vs", 1), AF.Identity, -1.0, col("t3", 47))
-        scan(V("eb", 256, 384), V("mk", 0, 128), V("db", 256, 384))
-        ts(V("vp", 1, 8), V("eb", 256 + 31, 384, 16), col("pay", 32), OP.add)
-        tt(V("qq", 0, 128), G(V(ct, 0, 24), L(L8, 8)), V("yc"), OP.not_equal)
-        scan(V("rq", 0, 128), V("qq", 0, 128), V("rd", 0, 128))
-        act(V("rd", 128, 256, 8), V("rq", 7, 128, 8))
-        tt(V("qq", 128, 256), G(V(ct), L(L8B, 8)), V("yc"), OP.not_equal)
-        scan(V("rq", 128, 256), V("qq", 128, 256), V("rd", 128, 256))
-        tt(V("av", 0, 240), G(V("rq", 128, 256), L(LR, 15)), V("tc", 0, 240), OP.is_ge)
-        scan(V("n1", 0, 240), V("ns", 0, 240), V("av", 0, 240), OP.min, OP.add)
-        scan(V("n3", 16, 256), V("dn", 0, 240), V("n1", 0, 240), OP.add, OP.max)
-        tt(V("px", 0, 15), last16("n3", 16, 240), last16("n3", 0, 240), OP.is_lt)
-        tt(V("px", 16, 31), V(ct, 16, 31), V("px", 0, 15), OP.subtract)
-        tt(V("vv", 1, 16), last16("n3", 16, 240), V("px", 16, 31), OP.max)
-        tt(col("ma", 48), col("n3", 255), col(ct, 30), OP.max)
-        ts(V("ma", 0, 16), V("sto", 0, 16), col("ma", 48), OP.not_equal)
+        act(col("dca", 15), col("vs", 1), AF.Identity, -1.0, col("own", 15))
+        if not last:
+            ts(V("ba", 16, 32), en, 1.0, OP.not_equal)
+            tt(V("ba", 0, 16), V("ba", 16, 32), V("pw2"), OP.mult)
+            act(last16("aa"), V("ba", 0, 16), AF.Identity, 1.0, drop)
+        act(V("ki", 0, 56, 8), V(ct, 8, 15))
+        tt(V("qq"), G(V(ct, 0, 16), L(LTR, 8)), V(ct, 16, 144), OP.not_equal)
+        scan(V("rq", 0, 128), V("qq"), V("ki", 0, 128))
+        tt(V("dd"), G(V("rq", 0, 129), L(LK, 16)), V("sti"), OP.subtract)
+        ts(V("fi"), V("dd"), 1.0, OP.min, -0.25, OP.max)
+        scan(V("mg"), V("fi"), V("ini"))
+        ts(V("mm"), V("mg"), ROUGH, OP.add, ROUGH, OP.is_equal)
+        act(col("ma", 32), col(ct, 14), AF.Relu, 1.0, -2.0)
+        ts(V("ma", 0, 16), V("ba", 32, 48), col("ma", 32), OP.not_equal)
         scan(V("ma", 16, 32), V("ma", 0, 16), V("dca"))
         act(V("dsb", 0, 256, 16), z(16), AF.Identity, 1.0, col("ma", 31))
-        tt(V("mm"), G(V("vv"), L(LO, 16)), V("sti"), OP.not_equal)
         scan(V("sr"), V("mm"), V("dsb"))
-        cp(V("sl"), last16("sr"))
+        ts(V("sl"), last16("sr"), 1 / 32, OP.mult)
         for b in range(4):
             mx(bank(b, 128), eq(b)[0], eq(b)[1], V("lq", at, at + 128), V("ls", at, at + 128))
             act(V("fw", 384 * b + 256, 384 * b + 368), bank(b, 112))
         for b in range(4):
-            (cp if last and b == 0 else act)(V("hn", 256 * b, 256 * b + 256), G(V("fw", 384 * b, 384 * b + 368), V("sl")))
+            (cp if b == 0 else act)(V("hn", 256 * b, 256 * b + 256), G(V("fw", 384 * b, 384 * b + 368), V("sl")))
             tt(V("zt", b, 1024, 4), G(V("hn", 256 * b, 256 * b + 256), V("inv")), V("fw", 384 * b, 384 * b + 256), OP.add)
         quant(V("qz"), V("sz"), V("zt"))
         for b in range(4):
@@ -412,26 +433,25 @@ def program():
                 act(V("xt", b, 1024, 4), x32, AF.Copy, 0.03125)
             else:
                 ts(V("xt", b, 1024, 4), x32, 0.03125, OP.mult)
-        tt(V("mo", 0, 128), G(V(ct, 16, 32), L(LI + 8, 8)), V("sto"), OP.not_equal)
-        scan(V("mo", 128, 256), V("mo", 0, 128), V("didb"))
-        act(V("vp", 8, 16), last16("mo", 128, 128))
-        if last:
-            scan(V("ma", 32, 48), V("ma", 0, 16), V("didb", 0, 16))
-            act(col("vp", 0), col("ma", 47))
-            tt(V("dp"), V("vp", 0, 16), V("vp", 1, 17), OP.subtract)
-        else:
-            act(V("v0", 1, 16), V("vp", 1, 16), AF.Exp, LN2)
-            act(V("ve", 1, 16), V("vp", 1, 16), AF.Copy, 65536.0)
-            act(col("ve", 32), col("vp", 15), AF.Copy, 65536.0)
-            tt(V("ve", 33, 48), V("ve", 1, 16), V("v0", 1, 16), OP.add)
-            tt(V("dp"), V("ve", 32, 48), V("ve", 33, 49), OP.subtract)
+        tt(V("mo"), G(V(ct, 0, 16), L(LMO, 8)), V("sto"), OP.not_equal)
+        scan(V("mp"), V("mo"), V("dpkb"))
+        act(V("vp", 1, 9), last16("mp", 0, 128))
+        tt(V("dp", 1, 16), V("vp", 1, 16), V("vp", 2, 17), OP.subtract)
         act(V("dpb"), G(V("dp"), L(LO, 16)))
-        scan(V("ep", 0, 256), V("mm"), V("dpb"))
         if last:
-            act(V("lk"), last16("ep"))
+            act(V("dpb", 0, 256, 16), z(16), AF.Identity, 1.0, col("ma", 31))
+        scan(V("ep"), V("mm"), V("dpb"))
+        cp(V("li", 0, 16), last16("ep"))
+        ts(V("li", 16, 32), V("li", 0, 16), 31, OP.bitwise_and)
+        if last:
+            cp(V("lk"), V("li", 16, 32))
             store("s", "op", V("lk"))
         else:
-            ancestors(last16("ep"), last16("ep", 16), G(V("ep", 0, 256), L(LO16, 16)))
+            cp(V("p0"), V("li", 16, 32))
+            ts(V("hh"), V("li", 16, 32), PTR, OP.mult)
+            tt(V("cu"), V("hh"), V("ba", 0, 16), OP.add)
+            tt(V("df", 0, 16), pk, last16("ep"), OP.subtract)
+            ancestors(V("p0"))
     state_product(V("qv"), V("sv"))
     store("s", "oc", V("qx"))
     act(V("ysb", 0, 128), V("ps", 0, 128))

@@ -10,7 +10,7 @@ BUF = {
     "vt": (B, 512), "qv": (Q4, 128), "sv": (S1, 128), "qw": (Q4, 512), "sw": (S1, 512), "ez": (B, 520), "qe": (Q4, 512), "se": (S1, 512),
     "fw": (B, 1536), "give": (B, 512), "hn": (B, 1024), "zt": (B, 1024), "z32": (B, 1024), "x32": (B, 1024), "qz": (Q4, 256), "sz": (S1, 256),
     "ysb": (F, 256), "lq": (Q4, 352), "ls": (S1, 352),
-    "pi": (I, 8), "pf": (F, 32), "iof": (F, 48), "lc": (U, 196), "la": (I, 96), "lb": (I, 96), "rm": (B, 256), "ms": (B, 256), "ib": (B, 256),
+    "pi": (I, 8), "pf": (F, 32), "iof": (F, 48), "lc": (U, 196), "la": (I, 96), "lb": (I, 96), "rm": (B, 256), "rh": (B, 256), "ms": (B, 256), "ib": (B, 256),
     "scv": (B, 256), "z16": (F, 16), "pw2": (B, 16), "un": (F, 48), "a2": (B, 256), "aa": (F, 256),
     "ni": (I, 32), "nf": (F, 64), "nt": (F, 64), "t3": (F, 48), "lg1": (U, 16), "lnod": (U, 16), "rr": (B, 256), "r5": (B, 512), "t5": (B, 512),
     "sel": (F, 16), "inv": (U, 16), "dpk": (F, 16), "dpkb": (F, 128), "dca": (F, 16), "sm": (F, 112),
@@ -28,7 +28,8 @@ for _r in range(ROUNDS):
     BUF["ct%d" % _r] = (B, 144)
     BUF["qo%d" % _r] = (Q4, 128)
     BUF["so%d" % _r] = (S1, 128)
-PS = {"pa": 2048, "ps": 1024}
+PS = {"pa": 2048, "ps": 1024, "pb": 1024}
+HN0, ZSPLIT, HALVES, GSPLIT = 0, 3, 1, 1
 HOME, _fill = {}, {"shortf": 0, "shortb": 0}
 for _k in ("pf", "sel", "sm", "gg", "df", "fl", "pay", "vs", "ds", "vp", "pw2", "dpk", "dca", "w", "d3", "ma", "dp", "un", "cu", "hh", "ba", "oq", "ro"):
     _h = "shortf" if BUF[_k][0] == F else "shortb"
@@ -43,12 +44,11 @@ QUEUES = ["v", "a", "p", "g", "s"]
 NDMA = 16
 SEMAPHORES = ["q" + q for q in QUEUES] + ["d%d" % i for i in range(NDMA)] + ["sent"] + ["aw%d" % r for r in range(ROUNDS)] + ["av%d" % r for r in range(ROUNDS)]
 
-CYC = 1.0
-WAKES = ((120.0, 120.0), (180.0, 180.0), (120.0, 300.0))
-PLANS = [(p, k) for p in (200.0, 400.0, 800.0) for k in range(6)]
-MOVES, SLACK = 40000, 40.0
+PACES = ((0.9, 190.0), (1.0, 150.0), (1.2, 250.0))
+PLANS = [(p, k) for p in (200.0, 400.0, 800.0) for k in range(3)]
+MOVES, SLACK = 40000, 150.0
 LN2 = math.log(2.0)
-HALF = 32767.5
+HALF = 32767.5 / 32768
 PTR, LIFT = 2.0 ** 17, 2.0 ** 21
 ROUGH = 1.5 * 2.0 ** 24
 LD, LO, LE, LO16, LA, LB, LU, LT3, LSEL, LS, LOWN, LTR, LMO, LK, LSTI, LTO = 0, 32, 64, 72, 88, 104, 120, 128, 132, 136, 140, 144, 152, 160, 176, 192
@@ -90,7 +90,7 @@ def narrow(*vs):
     return all(v[0] in BUF and SIZE[BUF[v[0]][0]] == 2 for v in vs)
 
 
-def program():
+def program(CYC):
     ops = []
 
     def add(q, kind, args, reads, writes, cost, late=0.0):
@@ -171,9 +171,9 @@ def program():
     iota(V("lb", 32, 64), [[16, 2], [0, 16]], 0, 0)
     ts(L(LD, 64), V("lb", 0, 64), pq, OP.add)
     ts(col("pf", 7), ph, 8.0, OP.mult, pj, OP.add)
-    ts(L(LT3, 1), p2, 16.0, OP.mult, col("pf", 7), OP.add)
-    ts(L(LT3 + 1, 1), p32, 32.0, OP.add)
-    cp(L(LT3 + 2, 1), p32)
+    cp(L(LT3, 1), p32)
+    ts(L(LT3 + 1, 1), p2, 16.0, OP.mult, col("pf", 7), OP.add)
+    ts(L(LT3 + 2, 1), p32, 32.0, OP.add)
     ts(col("pf", 8), pq, 16.0, OP.mult, 15.0, OP.add)
     ts(L(LE, 8), z(8), col("pf", 8), OP.add)
     ts(L(LO16, 16), io(16), 16.0, OP.mult, 15.0, OP.add)
@@ -237,6 +237,8 @@ def program():
     ts(V("w4", 0, 32), V("la", 48, 80), 32.0, OP.mult)
     tt(V("fl", 0, 32), V("w4", 0, 32), V("w4", 32, 64), OP.add)
     cp(L(LA, 32), V("fl", 0, 32))
+    fill(V("rh"), 0.5)
+    fill(V("rh", 0, 256, 16), 0.0)
     fill(V("rm"), 1.0)
     fill(V("rm", 0, 256, 16), 0.0)
     fill(V("ms"), 1.0)
@@ -265,9 +267,9 @@ def program():
     cp(V("nf"), G(V("ni"), L(LD, 4)))
     tp(V("nt"), V("nf"))
     cp(V("t3", 0, 48), G(V("nt"), L(LT3, 3)))
-    par0, colv = V("t3", 16, 32), V("t3", 32, 48)
+    par0, colv = V("t3", 32, 48), V("t3", 0, 16)
     pk, en = V("own", 0, 16), V("own", 16, 32)
-    cp(V("lg1"), V("t3", 0, 16))
+    cp(V("lg1"), V("t3", 16, 32))
     ts(V("sm", 0, 16), colv, 32.0, OP.mult)
     tt(pk, V("sm", 0, 16), io(16), OP.add)
     tt(V("dpk", 0, 15), V("own", 0, 15), V("own", 1, 16), OP.subtract)
@@ -291,13 +293,12 @@ def program():
             if k < 3:
                 act(V("cu"), last16("hop"))
                 aim(last16("hop"))
-        cp(V("w4", 0, 16), last16("hop"))
-        ts(V("w4", 16, 32), V("w4", 0, 16), 1, OP.logical_shift_right)
-        ts(V("w4", 32, 64), V("w4", 0, 32), 2, OP.logical_shift_right)
+        for j in range(4):
+            ts(V("w4", 16 * j, 16 * j + 16), last16("hop"), 0.5 ** j, OP.mult, 0.5 ** (j + 1) - 0.5, OP.add)
         for j in range(4):
             ts(V("bits", 64 * j, 64 * j + 64), V("w4"), 4 * j, OP.logical_shift_right, 1, OP.bitwise_and)
 
-    cp(V("p0"), par0)
+    cp(V("p0"), G(V("nt"), L(LT3 + 2, 1)))
     act(V("dstb"), G(par0, V("p0")), AF.Identity, 1.0, 16.0)
     scan(V("sp"), V("dstb"), V("a2"), OP.max, OP.add)
     act(V("ddb"), G(pk, V("p0")), AF.Identity, 1.0, LIFT)
@@ -343,19 +344,22 @@ def program():
             act(V("ssb", 128 * h, 128 * h + 128), V("ps", 512 * h, 512 * h + 128))
         act(V("g1"), G(V("ssb"), V("lg1")))
         tp(V("tr"), V("g1"))
-        act(V("gb"), G(V("tr"), L(LB, 16)))
-        tt(V("c1"), G(V("tr"), L(LA, 16)), V("gb"), OP.is_gt)
+        parts = ((0, 8), (8, 16)) if GSPLIT else ((0, 16),)
+        for lo, hi in parts:
+            act(V("gb", 16 * lo, 16 * hi), G(V("tr"), L(LB + lo, hi - lo)))
+            tt(V("c1", 16 * lo, 16 * hi), G(V("tr"), L(LA + lo, hi - lo)), V("gb", 16 * lo, 16 * hi), OP.is_gt)
         scan(V("s1"), V("ms"), V("c1"))
         tt(en, io(16, 32), last16("s1"), OP.subtract)
         for b in range(4):
             act(V("fw", 384 * b, 384 * b + 256), bank(b, 256))
-        act(V("w"), en, AF.Exp, -LN2, 16 * LN2)
+        act(V("w"), last16("s1"), AF.Exp, LN2)
         act(V("dstb"), G(en, V("p0")), AF.Identity, 1.0, 16.0)
         tt(V("pr"), G(V("w"), L(LO, 16)), V("bits"), OP.mult)
-        scan(V("bm"), V("rm"), V("pr"))
+        scan(V("bm"), V("rh"), V("pr"))
         act(V("gg"), last16("bm"), AF.Abs, 1.0, -HALF)
-        act(V("ai"), G(V("bm"), L(LO16, 16)), AF.Abs, 1.0, -HALF)
-        tt(V("c2"), G(V("gg"), L(LO, 16)), V("ai"), OP.is_gt)
+        for lo, hi in parts:
+            act(V("ai", 16 * lo, 16 * hi), G(V("bm"), L(LO16 + lo, hi - lo)), AF.Abs, 1.0, -HALF)
+            tt(V("c2", 16 * lo, 16 * hi), G(V("gg"), L(LO, hi - lo)), V("ai", 16 * lo, 16 * hi), OP.is_gt)
         scan(V("posm"), V("rm"), V("c2"))
         scan(V("sp"), V("dstb"), V("a2"), OP.max, OP.add)
         tt(V("df", 16, 32), en, last16("sp"), OP.subtract)
@@ -419,20 +423,21 @@ def program():
             mx(bank(b, 128), eq(b)[0], eq(b)[1], V("lq", at, at + 128), V("ls", at, at + 128))
             act(V("fw", 384 * b + 256, 384 * b + 368), bank(b, 112))
         for b in range(4):
-            (cp if b == 0 else act)(V("hn", 256 * b, 256 * b + 256), G(V("fw", 384 * b, 384 * b + 368), V("sl")))
-            tt(V("zt", b, 1024, 4), G(V("hn", 256 * b, 256 * b + 256), V("inv")), V("fw", 384 * b, 384 * b + 256), OP.add)
-        quant(V("qz"), V("sz"), V("zt"))
-        for b in range(4):
-            act(V("z32", 256 * b, 256 * b + 256), V("zt", b, 1024, 4), AF.Copy, 32.0)
-        for b in range(4):
-            mx(bank(b, 256), V("qw", 128 * b, 128 * b + 128), V("sw", 128 * b, 128 * b + 128), V("qz"), V("sz"))
-        for b in range(4):
-            x32 = V("x32", 256 * b, 256 * b + 256)
-            tt(x32, bank(b, 256), V("z32", 256 * b, 256 * b + 256), OP.add)
-            if b < 3:
-                act(V("xt", b, 1024, 4), x32, AF.Copy, 0.03125)
-            else:
-                ts(V("xt", b, 1024, 4), x32, 0.03125, OP.mult)
+            (cp if b == 0 and (last or HN0) else act)(V("hn", 256 * b, 256 * b + 256), G(V("fw", 384 * b, 384 * b + 368), V("sl")))
+            for lo, hi in (((0, 128), (128, 256)) if b >= ZSPLIT else ((0, 256),)):
+                tt(V("zt", 4 * lo + b, 4 * hi, 4), G(V("hn", 256 * b, 256 * b + 256), V("inv", lo // 16, hi // 16)), V("fw", 384 * b + lo, 384 * b + hi), OP.add)
+                act(V("z32", 256 * b + lo, 256 * b + hi), V("zt", 4 * lo + b, 4 * hi, 4), AF.Copy, 32.0)
+        for h, (lo, hi) in enumerate(((0, 128), (128, 256)) if HALVES else ((0, 256),)):
+            quant(V("qz", lo, hi), V("sz", lo, hi), V("zt", 4 * lo, 4 * hi))
+            for b in range(4):
+                out = (bank(b, hi - lo) if h == 0 else V("pb" if b < 2 else "ps", 512 * (b % 2), 512 * (b % 2) + 128))
+                mx(out, V("qw", 128 * b, 128 * b + 128), V("sw", 128 * b, 128 * b + 128), V("qz", lo, hi), V("sz", lo, hi))
+                x32 = V("x32", 256 * b + lo, 256 * b + hi)
+                tt(x32, out, V("z32", 256 * b + lo, 256 * b + hi), OP.add)
+                if b < 3 or (HALVES and h == 0):
+                    act(V("xt", 4 * lo + b, 4 * hi, 4), x32, AF.Copy, 0.03125)
+                else:
+                    ts(V("xt", 4 * lo + b, 4 * hi, 4), x32, 0.03125, OP.mult)
         tt(V("mo"), G(V(ct, 0, 16), L(LMO, 8)), V("sto"), OP.not_equal)
         scan(V("mp"), V("mo"), V("dpkb"))
         act(V("vp", 1, 9), last16("mp", 0, 128))
@@ -477,6 +482,24 @@ def replay(table, seq):
     return top, end
 
 
+def blocked(table, seq):
+    top, end = replay(table, seq)
+    before, last = {}, {}
+    for n in seq:
+        before[n] = last.get(table[n][0])
+        last[table[n][0]] = n
+    n = max(seq, key=lambda m: end[m] + table[m][2])
+    pairs = []
+    while n is not None:
+        start, m = end[n] - table[n][1], before[n]
+        if m is not None and abs(end[m] - start) < 1e-6:
+            pairs.append((m, n))
+            n = m
+        else:
+            n = next((d for d, lag in table[n][3] if abs(end[d] + lag - start) < 1e-6), None)
+    return pairs
+
+
 def order(ops):
     writer, readers = {}, {}
     for n, o in enumerate(ops):
@@ -498,8 +521,15 @@ def order(ops):
             readers.setdefault(c, set()).add(n)
         deps.discard(n)
         o["deps"] = deps
-    flat = [[(QUEUES.index(o["q"]), o["cost"], o["late"], [(d, ops[d]["late"] + (a if ops[d]["q"] == o["q"] else b)) for d in sorted(o["deps"])]) for o in ops]
-            for a, b in WAKES]
+    above = []
+    for n, o in enumerate(ops):
+        far = 0
+        for d in o["deps"]:
+            far |= above[d]
+        o["near"] = sorted(d for d in o["deps"] if not far >> d & 1)
+        above.append(far | sum(1 << d for d in o["deps"]))
+    flat = [[(QUEUES.index(o["q"]), t["cost"], o["late"], [(d, ops[d]["late"] + wake) for d in o["near"]]) for o, t in zip(ops, program(cycle))]
+            for cycle, wake in PACES]
     score = lambda s: sum(replay(t, s)[0] for t in flat)
     tail = [o["cost"] + o["late"] for o in ops]
     users = [[] for o in ops]
@@ -511,7 +541,7 @@ def order(ops):
     for patience, grain in PLANS:
         noise = np.random.default_rng(grain).random(len(ops)).tolist()
         weight = [t + (300.0 * e if grain else 0.0) for t, e in zip(tail, noise)]
-        left = [len(o["deps"]) for o in ops]
+        left = [len(o["near"]) for o in ops]
         ready = {n: 0.0 for n in range(len(ops)) if left[n] == 0}
         free = {q: 0.0 for q in QUEUES}
         end, seq = {}, []
@@ -542,10 +572,16 @@ def order(ops):
         if best is None or total < best[0]:
             best = (total, seq)
     total, seq = best
-    for turn, (a, b, c) in enumerate(np.random.default_rng(7).random((MOVES, 3)).tolist()):
-        i = int(a * len(seq))
-        n = seq[i]
-        step, hops, j, to = (1 if b < 0.5 else -1), 1 + int(c * c * 8), i, None
+    held = None
+    for turn, (a, b, c, e) in enumerate(np.random.default_rng(7).random((MOVES, 4)).tolist()):
+        if held is None:
+            end = replay(flat[0], seq)[1]
+            seq.sort(key=lambda m: end[m] - ops[m]["cost"])
+            held = blocked(flat[turn % len(flat)], seq)
+        step = 1 if b < 0.5 else -1
+        n = held[int(a * len(held))][step < 0] if e < 0.7 and held else seq[int(a * len(seq))]
+        i = seq.index(n)
+        hops, j, to = 1 + int(c * c * 8), i, None
         stop = set(users[n]) if step > 0 else ops[n]["deps"]
         while hops and 0 <= j + step < len(seq) and seq[j + step] not in stop:
             j += step
@@ -557,11 +593,11 @@ def order(ops):
         new = seq[:i] + seq[i + 1:]
         new.insert(to, n)
         t = score(new)
-        if t <= total + SLACK * (1.0 - turn / MOVES):
-            total, seq = t, new
-            if turn % 8 == 0:
-                end = replay(flat[0], seq)[1]
-                seq.sort(key=lambda m: end[m] - ops[m]["cost"])
+        if t <= total + SLACK * (1.0 - turn / MOVES) ** 2 * c:
+            total, seq, held = t, new, None
+            if t < best[0]:
+                best = (t, list(new))
+    seq = best[1]
     end = replay(flat[0], seq)[1]
     for n, o in enumerate(ops):
         o["at"] = end[n] - o["cost"]
@@ -594,7 +630,7 @@ def order(ops):
     return seq
 
 
-OPS = program()
+OPS = program(PACES[0][0])
 SEQ = order(OPS)
 
 

@@ -8,30 +8,33 @@ SIZE = {F: 4, B: 2, I: 4, U: 2, Q4: 4, S1: 1}
 BUF = {
     "xt": (B, 1024), "qx": (Q4, 256), "sx": (S1, 256), "ut": (B, 512), "qu0": (Q4, 128), "su0": (S1, 128), "qu": (Q4, 128), "su": (S1, 128),
     "vt": (B, 512), "qv": (Q4, 128), "sv": (S1, 128), "qw": (Q4, 512), "sw": (S1, 512), "ez": (B, 520), "qe": (Q4, 512), "se": (S1, 512),
-    "fw": (B, 1536), "give": (B, 512), "hn": (B, 1024), "zt": (B, 1024), "z32": (B, 1024), "x32": (B, 1024), "qz": (Q4, 256), "sz": (S1, 256),
-    "ysb": (F, 256), "lq": (Q4, 352), "ls": (S1, 352),
-    "pi": (I, 8), "pf": (F, 32), "iof": (F, 48), "lc": (U, 196), "la": (I, 96), "lb": (I, 96), "rm": (B, 256), "rh": (B, 256), "ms": (B, 256), "ib": (B, 256),
-    "scv": (B, 256), "z16": (F, 16), "pw2": (B, 16), "un": (F, 48), "a2": (B, 256), "aa": (F, 256),
-    "ni": (I, 32), "nf": (F, 64), "nt": (F, 64), "t3": (F, 48), "lg1": (U, 16), "lnod": (U, 16), "rr": (B, 256), "r5": (B, 512), "t5": (B, 512),
-    "sel": (F, 16), "inv": (U, 16), "dpk": (F, 16), "dpkb": (F, 128), "dca": (F, 16), "sm": (F, 112),
+    "fw": (B, 1536), "fp": (B, 1024), "give": (B, 512), "hn": (B, 1024), "zt": (B, 1024), "z32": (B, 1024), "x32": (B, 1024), "qz": (Q4, 256), "sz": (S1, 256),
+    "ysb": (F, 256), "qo": (Q4, 128), "so": (S1, 128), "qg": (Q4, 128), "sg": (S1, 128),
+    "pi": (I, 8), "pf": (F, 32), "iof": (F, 48), "lc": (U, 200), "la": (I, 96), "lb": (I, 96), "rm": (B, 256), "rh": (B, 256), "ms": (B, 256), "ib": (B, 256),
+    "scv": (F, 256), "z16": (F, 16), "pw2": (B, 16), "un": (F, 48), "a2": (B, 256), "aa": (F, 256),
+    "ni": (I, 32), "nf": (F, 64), "nt": (F, 64), "t3": (F, 48), "lg1": (U, 16), "lnod": (U, 16), "rr": (F, 256),
+    "inv": (U, 16), "pe": (F, 48), "dnb": (B, 128), "a3": (B, 256), "dca": (F, 16), "sm": (F, 128),
     "ssb": (F, 256), "g1": (F, 256), "tr": (F, 256), "gb": (F, 256), "c1": (B, 256), "s1": (B, 256), "own": (F, 48), "w": (B, 16),
     "dstb": (B, 256), "sti": (B, 256), "sto": (B, 128), "pr": (B, 256), "bm": (F, 256), "gg": (F, 16),
-    "ai": (F, 256), "c2": (B, 256), "posm": (B, 256), "sp": (B, 256), "df": (F, 32), "fl": (F, 64), "pay": (F, 48), "d3": (F, 32),
-    "dbp": (F, 128), "dbe": (B, 128), "mk": (B, 256), "eb": (B, 288), "ef": (F, 256), "vl": (U, 8), "vs": (F, 32), "ds": (F, 16), "dsb": (F, 256),
+    "ai": (F, 256), "c2": (B, 256), "posm": (B, 256), "sp": (B, 256), "df": (F, 32), "fl": (F, 64), "pay": (F, 48), "d3": (F, 48),
+    "dbp": (F, 128), "dbe": (B, 128), "mk": (B, 256), "eb": (B, 400), "dbc": (B, 112), "ef": (F, 256), "vl": (U, 8), "vs": (F, 32), "ds": (F, 16), "dsb": (F, 256),
     "vp": (F, 32), "oq": (B, 64), "ro": (B, 64), "ki": (B, 144), "qq": (B, 128), "rq": (B, 144), "dd": (B, 256), "fi": (B, 256), "ini": (B, 256),
-    "mg": (B, 256), "ma": (F, 48), "mm": (B, 256), "sr": (F, 256), "sl": (U, 16), "mo": (B, 128), "mp": (F, 128), "dp": (F, 16), "dpb": (F, 256),
-    "ep": (F, 256), "li": (I, 32), "p0": (U, 16), "p1": (U, 16), "cu": (F, 16), "hh": (F, 16), "ba": (F, 48), "ddb": (F, 256), "hop": (F, 256),
+    "mg": (B, 256), "ma": (F, 64), "mm": (B, 256), "sr": (F, 256), "sl": (U, 16), "mo": (B, 128), "mp": (B, 128), "dp": (F, 16), "dpb": (F, 256),
+    "ep": (F, 256), "p0": (U, 16), "p1": (U, 16), "cu": (F, 32), "hh": (F, 16), "ba": (F, 64), "pwd": (F, 16), "ddb": (F, 256), "hop": (F, 256),
     "w4": (I, 64), "bits": (I, 256), "lk": (F, 16),
 }
 for _r in range(ROUNDS):
     BUF["ws%d" % _r] = (B, 64)
     BUF["ct%d" % _r] = (B, 144)
-    BUF["qo%d" % _r] = (Q4, 128)
-    BUF["so%d" % _r] = (S1, 128)
+    BUF["pq%d" % _r] = (Q4, 256)
+    BUF["pp%d" % _r] = (S1, 256)
 PS = {"pa": 2048, "ps": 1024, "pb": 1024}
-HN0, ZSPLIT, HALVES, GSPLIT = 0, 3, 1, 1
+HN0, ZSPLIT, HALVES, GSPLIT = 1, 3, 1, 1
+ZLAST = 0
+EARLY = (0, 1, 2)
+ASPLIT, CSPLIT, MERGE, HINT = 1, 30, 0, 0
 HOME, _fill = {}, {"shortf": 0, "shortb": 0}
-for _k in ("pf", "sel", "sm", "gg", "df", "fl", "pay", "vs", "ds", "vp", "pw2", "dpk", "dca", "w", "d3", "ma", "dp", "un", "cu", "hh", "ba", "oq", "ro"):
+for _k in ("pf", "sm", "gg", "df", "fl", "pay", "vs", "ds", "vp", "pw2", "pe", "dca", "w", "d3", "ma", "dp", "un", "cu", "hh", "ba", "pwd", "oq", "ro"):
     _h = "shortf" if BUF[_k][0] == F else "shortb"
     HOME[_k] = (_h, _fill[_h])
     _fill[_h] += BUF[_k][1]
@@ -41,17 +44,20 @@ SCRATCH["shortb"] = ("sbuf", [128, _fill["shortb"]], B)
 for _k, _n in PS.items():
     SCRATCH[_k] = ("psum", [128, _n], F)
 QUEUES = ["v", "a", "p", "g", "s"]
-NDMA = 16
-SEMAPHORES = ["q" + q for q in QUEUES] + ["d%d" % i for i in range(NDMA)] + ["sent"] + ["aw%d" % r for r in range(ROUNDS)] + ["av%d" % r for r in range(ROUNDS)]
+NDMA = 20
+SEMAPHORES = ["q" + q for q in QUEUES] + ["d%d" % i for i in range(NDMA)] + ["sent"] + ["%s%d" % (s, r) for s in ("aw", "av", "left") for r in range(ROUNDS)]
 
-PACES = ((0.9, 190.0), (1.0, 150.0), (1.2, 250.0))
+ISSUE, START = 0.0, 220.0
+PACES = ((0.87, 195.0, 0.0, 1.2, 1.55), (1.05, 200.0, 0.0, 1.5, 1.25), (1.15, 250.0, 0.0, 1.7, 1.9))
 PLANS = [(p, k) for p in (200.0, 400.0, 800.0) for k in range(3)]
-MOVES, SLACK = 40000, 150.0
+TRIES, STRETCHES = 41, 8
+MOVES, SLACK = 80000, 400.0
 LN2 = math.log(2.0)
 HALF = 32767.5 / 32768
-PTR, LIFT = 2.0 ** 17, 2.0 ** 21
+PTR, LIFT = 2.0 ** 17, 2.0 ** 22
+COL, NODE = 2048.0, 32.0
 ROUGH = 1.5 * 2.0 ** 24
-LD, LO, LE, LO16, LA, LB, LU, LT3, LSEL, LS, LOWN, LTR, LMO, LK, LSTI, LTO = 0, 32, 64, 72, 88, 104, 120, 128, 132, 136, 140, 144, 152, 160, 176, 192
+LD, LO, LE, LO16, LA, LB, LU, LT3, LSEL, LS, LOWN, LTR, LMO, LK, LSTI, LTO, LSE = 0, 32, 64, 72, 88, 104, 120, 128, 132, 136, 140, 144, 152, 160, 176, 192, 196
 
 
 def V(name, lo=0, hi=None, step=1):
@@ -90,7 +96,12 @@ def narrow(*vs):
     return all(v[0] in BUF and SIZE[BUF[v[0]][0]] == 2 for v in vs)
 
 
-def program(CYC):
+def real(*vs):
+    names = [v[1][0] if v[0] == "@" else v[0] for v in vs]
+    return all(n in PS or BUF[n][0] in (F, B) for n in names)
+
+
+def program(CYC, SLOW, PICK):
     ops = []
 
     def add(q, kind, args, reads, writes, cost, late=0.0):
@@ -98,12 +109,31 @@ def program(CYC):
 
     def vcost(n, src, per):
         if src[0] == "@":
-            return 50 + 1.5 * n * CYC
+            return 50 + PICK * n * CYC
         return max(64, n * per) * CYC
+
+    def acost(n, src):
+        return 65 + PICK * n * CYC if src[0] == "@" else max(64, n) * CYC
+
+    def either(first, out, src, scale=1.0, bias=None):
+        n = count(out)
+        if scale == 0.0:
+            form = ("fill", (out, bias))
+        elif bias is None:
+            form = ("copy", (out, src)) if scale == 1.0 else ("ts", (out, src, scale, None, OP.mult, None))
+        else:
+            form = ("ts", (out, src, scale, bias, OP.mult, OP.add))
+        forms = [("v",) + form + (vcost(n, src, 0.5 if narrow(out, src) else 1),),
+                 ("a", "act", (out, src, AF.Copy if bias is None else AF.Identity, scale, bias), acost(n, src))]
+        q, kind, args, cost = forms[first == "a"]
+        add(q, kind, args, [src, bias], [out], cost)
+        ops[-1]["other"] = forms[first == "v"]
 
     def cp(out, src):
         if out[0] == "@":
             add("v", "copy", (out, src), [src, out[2]], [out[1]], 50 + 3.0 * count(src) * CYC)
+        elif real(out, src):
+            either("v", out, src)
         else:
             add("v", "copy", (out, src), [src], [out], vcost(count(out), src, 0.5 if narrow(out, src) else 1))
 
@@ -111,6 +141,10 @@ def program(CYC):
         add("v", "tt", (out, a, b, op), [a, b], [out], vcost(count(out), a, 1 if a[0] in PS else 2))
 
     def ts(out, a, s1, op0, s2=None, op1=None):
+        if real(out, a) and op0 == OP.mult and op1 in (None, OP.add) and not isinstance(s1, tuple):
+            return either("v", out, a, s1, s2)
+        if real(out, a) and op0 == OP.add and op1 is None:
+            return either("v", out, a, 1.0, s1)
         add("v", "ts", (out, a, s1, s2, op0, op1), [a, s1, s2], [out], vcost(count(out), a, 0.5 if narrow(out, a) else 1))
 
     def scan(out, d0, d1, op0=OP.mult, op1=OP.add, init=0.0):
@@ -126,23 +160,31 @@ def program(CYC):
         add("v", "quant", (q, s, src), [src], [q, s], 12 + 0.22 * count(src) * 1.2)
 
     def act(out, src, func=AF.Copy, scale=1.0, bias=None):
-        n = count(out)
-        add("a", "act", (out, src, func, scale, bias), [src, bias], [out], 65 + 1.5 * n * CYC if src[0] == "@" else max(64, n) * CYC)
+        if func in (AF.Copy, AF.Identity):
+            return either("a", out, src, scale, bias)
+        add("a", "act", (out, src, func, scale, bias), [src, bias], [out], acost(count(out), src))
+
+    def vact(out, src, func=AF.Copy, scale=1.0, bias=None):
+        either("v", out, src, scale, bias)
 
     def mx(out, lq, ls, rq, rs):
-        add("p", "mx", (out, lq, ls, rq, rs), [lq, ls, rq, rs], [out], (count(out) + 16) * CYC)
+        add("p", "mx", (out, lq, ls, rq, rs), [lq, ls, rq, rs], [out], (count(out) + 16) * CYC * SLOW)
 
     def iota(out, pattern, base, chan):
         add("g", "iota", (out, pattern, base, chan), [], [out], 130 + 2 * count(out) * CYC)
 
     def load(q, out, name, after=()):
-        add(q, "load", (out, name), [name] + list(after), [out], 60, 2000.0)
+        add(q, "load", (out, name), [name] + list(after), [out], START, 1900.0)
 
     def store(q, name, src, part=None):
-        add(q, "store", (name, src, part), [src], [], 60, 2000.0 if part is not None else 2400.0)
+        add(q, "store", (name, src, part), [src], [], START, 1800.0 if part is not None else 2000.0)
+        ops[-1]["other"] = ("s" if q == "a" else "a", "store", (name, src, part), START)
 
     def send(r, sem, out, src, late):
         add("g", "send", (r, sem, out, src), [src], [out], 300, late)
+
+    def whole(out, src, unit):
+        ts(out, src, 1.5 * 2.0 ** 23 * unit, OP.add, 1.5 * 2.0 ** 23 * unit, OP.subtract)
 
     def level(out, c):
         act(out, V("ib", 0, count(out)), AF.Identity, 0.0, c)
@@ -177,8 +219,6 @@ def program(CYC):
     ts(col("pf", 8), pq, 16.0, OP.mult, 15.0, OP.add)
     ts(L(LE, 8), z(8), col("pf", 8), OP.add)
     ts(L(LO16, 16), io(16), 16.0, OP.mult, 15.0, OP.add)
-    ts(col("pf", 10), ph, 16.0, OP.mult)
-    ts(L(LSEL, 1), pq, 32.0, OP.mult, col("pf", 10), OP.add)
     ts(col("pf", 11), p2, 16.0, OP.mult)
     iota(V("la", 32, 40), [[32, 4], [0, 2]], 0, 0)
     ts(L(LU, 8), V("la", 32, 40), col("pf", 11), OP.add)
@@ -186,46 +226,38 @@ def program(CYC):
     ts(V("un", 32, 48), io(16, 1), pq, OP.is_equal, -2.0, OP.mult)
     tt(V("un", 0, 15), V("un", 16, 31), V("un", 32, 47), OP.add)
     ts(col("un", 15), pq, 15.0, OP.is_equal, -2.0, OP.add)
-    ts(V("a2"), G(V("un", 0, 16), L(LO, 16)), 16.0, OP.mult)
-    act(V("aa"), V("a2"), AF.Copy, LIFT / 16)
-    drop, lifts = col("pf", 16), col("pf", 17)
-    ts(drop, col("un", 15), LIFT, OP.mult)
+    ts(V("a2"), G(V("un", 0, 16), L(LO, 16)), 32.0, OP.mult)
+    act(V("aa"), V("a2"), AF.Copy, LIFT / 32)
+    act(V("a3"), V("a2"), AF.Copy, LIFT / 32)
+    lifts = col("pf", 17)
     ts(lifts, col("un", 15), -LIFT, OP.mult)
-    ts(V("la", 0, 8), io(8), 2.0, OP.mult, pe, OP.add)
-    later, head = col("pf", 13), col("pf", 12)
+    ts(col("pf", 16), col("un", 15), LIFT, OP.mult, 1.5 * 2.0 ** 23 * PTR, OP.add)
+    ts(V("sm", 96, 100), io(4), 2.0, OP.mult, pe, OP.add)
+    later, head, end = col("pf", 13), col("pf", 12), col("pf", 14)
     ts(later, p8, 0.0, OP.is_gt)
     ts(head, p8, 0.0, OP.is_equal, 128.0, OP.mult)
-    act(V("sm", 96, 100), io(4), AF.Identity, 32.0, 15.0)
-    ts(col("pf", 14), pe, 16.0, OP.mult)
-    ts(V("la", 8, 12), V("sm", 96, 100), col("pf", 14), OP.add, later, OP.mult)
-    ts(L(LOWN, 4), V("la", 8, 12), head, OP.add)
-    ts(V("la", 12, 16), V("la", 8, 12), 16.0, OP.add, 127.0, OP.min)
-    ts(V("sm", 100, 104), V("la", 12, 16), later, OP.mult, head, OP.add)
-    act(col("pf", 15), p8, AF.Identity, 16.0, 16.0)
-    ts(col("pf", 22), p8, 5.0, OP.is_le, col("pf", 15), OP.mult)
-    ts(col("pf", 23), col("sm", 100), col("pf", 22), OP.subtract, -31.0, OP.add)
-    ts(col("sm", 104), col("pf", 23), pe, OP.mult, col("pf", 22), OP.add)
-    ts(L(LS, 1), col("sm", 104), 31.0, OP.add)
-    cp(L(LS + 1, 3), V("sm", 101, 104))
+    ts(end, p8, 7.0, OP.is_equal, 112.0, OP.mult)
+    ts(V("sm", 100, 104), V("sm", 96, 100), 16.0, OP.mult, 15.0, OP.add)
+    ts(L(LOWN, 4), V("sm", 100, 104), later, OP.mult, head, OP.add)
+    ts(V("sm", 104, 107), V("sm", 100, 103), 32.0, OP.add, later, OP.mult)
+    ts(L(LS, 3), V("sm", 104, 107), head, OP.add, end, OP.add)
+    ts(col("pf", 15), p8, 16.0, OP.mult, 31.0, OP.add)
+    ts(L(LS + 3, 1), col("pf", 15), end, OP.add)
     act(col("pf", 24), p8, AF.Identity, 8.0, -72.0)
-    ts(V("la", 16, 20), V("la", 0, 4), p8, OP.is_ge, col("pf", 24), OP.mult)
-    ts(V("la", 20, 24), V("la", 16, 20), 63.0, OP.add, later, OP.mult)
-    ts(L(LTO, 4), V("la", 20, 24), 1.0, OP.add)
-    ts(col("pf", 25), p8, 1.0, OP.is_equal, 7.0, OP.mult)
-    ts(col("pf", 26), col("pf", 25), p8, OP.add, 5.0, OP.add)
-    ts(V("la", 24, 32), V("la", 0, 8), 6.0, OP.not_equal)
-    ts(V("la", 40, 48), V("la", 0, 8), 1.0, OP.add, p8, OP.is_ge)
-    tt(V("la", 80, 88), V("la", 24, 32), V("la", 40, 48), OP.mult)
-    ts(V("la", 88, 96), V("la", 80, 88), col("pf", 26), OP.mult, 1.0, OP.add)
-    ts(L(LTR, 8), V("la", 88, 96), later, OP.mult)
-    ts(L(LMO + 2, 6), io(6), 8.0, OP.add)
-    fill(L(LMO, 1), 2)
-    fill(L(LMO + 1, 1), 14)
-    ts(col("pf", 18), pq, 9.0, OP.is_ge, 2.0, OP.mult)
-    ts(col("pf", 27), pq, 2.0, OP.is_equal, 7.0, OP.mult)
-    ts(col("pf", 28), col("pf", 18), col("pf", 27), OP.add, pq, OP.add)
-    act(col("pf", 19), col("pf", 28), AF.Identity, 8.0, -145.0)
-    ts(col("pf", 29), pq, 2.0, OP.is_ge, col("pf", 19), OP.mult)
+    ts(V("sm", 108, 112), V("sm", 96, 100), p8, OP.is_ge, col("pf", 24), OP.mult)
+    ts(V("sm", 112, 116), V("sm", 108, 112), 63.0, OP.add, later, OP.mult)
+    ts(L(LTO, 4), V("sm", 112, 116), 1.0, OP.add)
+    ts(col("pf", 25), head, 9 / 128, OP.mult, p8, OP.add)
+    ts(L(LTR, 4), z(4), col("pf", 25), OP.add, -1.0, OP.add)
+    ts(col("pf", 26), col("pf", 25), -10.0, OP.add)
+    ts(V("sm", 116, 120), V("sm", 96, 100), p8, OP.is_gt, col("pf", 26), OP.mult)
+    ts(L(LTR + 4, 4), V("sm", 116, 120), 9.0, OP.add)
+    cp(L(LMO + 1, 7), io(7))
+    fill(L(LMO, 1), 10)
+    ts(col("pf", 18), pq, 9.0, OP.is_ge, -128.0, OP.mult)
+    ts(col("pf", 27), pq, 8.0, OP.mult, col("pf", 18), OP.add)
+    ts(col("pf", 28), pq, 2.0, OP.is_ge)
+    ts(col("pf", 29), col("pf", 27), -65.0, OP.add, col("pf", 28), OP.mult)
     ts(L(LK, 16), z(16), col("pf", 29), OP.add, 128.0, OP.add)
     ts(col("pf", 20), pq, 0.0, OP.is_gt)
     ts(col("pf", 21), pq, 0.0, OP.is_equal, 16.0, OP.mult)
@@ -247,19 +279,25 @@ def program(CYC):
     fill(V("give", 448, 512), 0.0)
     act(V("pw2"), io(16), AF.Exp, LN2)
     ops[-1]["cost"] += 1500.0
+    ts(V("pwd"), V("pw2"), lifts, OP.subtract)
+    fill(col("cu", 16), 16 * PTR)
+    fill(col("vp", 0), 16 * PTR)
     fill(V("ez"), 0.5)
     iota(V("ib"), [[-1, 16], [0, 16]], 15, 0)
     add("g", "select", (V("ez"), [[1, 520]], OP.is_equal, 0.0, -3, -4), [V("ez")], [V("ez")], 170 + 1040 * CYC)
-    iota(V("scv"), [[1, 16], [16, 16]], 0, 0)
-    for name, c in (("own", 32), ("pay", 32), ("vs", 0), ("vs", 16), ("vp", 16), ("dp", 0), ("eb", 128), ("eb", 272), ("rq", 128)):
+    iota(V("scv"), [[1, 16], [16, 16]], int(LIFT), 0)
+    for name, c in (("own", 32), ("pay", 32), ("vs", 0), ("vs", 16), ("vp", 16), ("eb", 384), ("rq", 128)):
         level(col(name, c), 0.0)
-    for name, n in (("rr", 256), ("ki", 128), ("ini", 256)):
+    for name, n in (("ki", 128), ("ini", 256)):
         level(V(name, 0, n), 0.0)
-    level(col("ki", 128), 0.5)
+    level(col("ki", 64), 0.5)
+    level(V("eb", 128, 144), 0.0)
     ts(V("vs", 2, 9), io(7, 16), 16.0, OP.mult, pq, OP.add)
-    ts(V("vs", 2, 9), V("vs", 2, 9), 32.0, OP.mult)
+    ts(V("vs", 2, 9), V("vs", 2, 9), COL, OP.mult)
+    level(V("dnb"), -PTR)
+    level(last16("dnb", 0, 128), 15 * PTR)
     for r in range(ROUNDS):
-        act(V("ct%d" % r, 0, 8), io(8), AF.Copy, 0.5)
+        act(V("ct%d" % r, 136, 144), io(8), AF.Copy, 0.5)
         level(V("ct%d" % r, 64, 80), 0.0)
     for b in range(4):
         quant(V("qe", 128 * b, 128 * b + 128), V("se", 128 * b, 128 * b + 128), V("ez", 3 - b, 515 - b))
@@ -270,12 +308,11 @@ def program(CYC):
     par0, colv = V("t3", 32, 48), V("t3", 0, 16)
     pk, en = V("own", 0, 16), V("own", 16, 32)
     cp(V("lg1"), V("t3", 16, 32))
-    ts(V("sm", 0, 16), colv, 32.0, OP.mult)
-    tt(pk, V("sm", 0, 16), io(16), OP.add)
-    tt(V("dpk", 0, 15), V("own", 0, 15), V("own", 1, 16), OP.subtract)
-    act(col("dpk", 15), col("own", 15))
-    act(V("dpkb"), G(V("dpk"), L(LO, 8)))
-    act(V("dca", 0, 15), V("dpk", 0, 15))
+    ts(V("sm", 0, 16), colv, COL, OP.mult)
+    act(V("pe", 32, 48), io(16), AF.Copy, NODE)
+    tt(pk, V("sm", 0, 16), V("pe", 32, 48), OP.add)
+    act(V("pe", 16, 32), pk)
+    tt(V("dca", 0, 15), V("own", 0, 15), V("own", 1, 16), OP.subtract)
     quant(V("qu0"), V("su0"), V("ut"))
     add("v", "pickq", (V("qu"), V("qu0"), L(LU, 8)), [V("qu0"), L(LU, 8)], [V("qu")], 50 + 1.5 * 128 * CYC)
     add("a", "picks", (V("su"), V("su0"), L(LU, 8)), [V("su0"), L(LU, 8)], [V("su")], 65 + 1.5 * 128 * CYC)
@@ -283,15 +320,17 @@ def program(CYC):
 
     def aim(cur):
         ts(V("p1"), cur, 1 / PTR, OP.mult)
-        ts(V("hh"), V("p1"), PTR, OP.mult, lifts, OP.add)
+        ts(V("hh"), cur, 1.5 * 2.0 ** 23 * PTR, OP.add, col("pf", 16), OP.subtract)
         tt(last16("aa"), cur, V("hh"), OP.subtract)
 
-    def ancestors(first):
+    def ancestors(first, parts):
         for k in range(4):
-            act(V("ddb"), G(V("cu"), V("p1") if k else first), AF.Identity, 1.0, LIFT)
-            scan(V("hop"), V("ddb"), V("aa"), OP.max, OP.add)
+            for lo, hi in parts:
+                rows = lambda name: V(name, 16 * lo, 16 * hi)
+                (act if lo == 0 else vact)(rows("ddb"), G(V("cu", 0, 17), V("p1" if k else first, lo, hi)), AF.Identity, 1.0, LIFT)
+                scan(rows("hop"), rows("ddb"), rows("aa"), OP.max, OP.add)
             if k < 3:
-                act(V("cu"), last16("hop"))
+                act(V("cu", 0, 16), last16("hop"))
                 aim(last16("hop"))
         for j in range(4):
             ts(V("w4", 16 * j, 16 * j + 16), last16("hop"), 0.5 ** j, OP.mult, 0.5 ** (j + 1) - 0.5, OP.add)
@@ -299,29 +338,31 @@ def program(CYC):
             ts(V("bits", 64 * j, 64 * j + 64), V("w4"), 4 * j, OP.logical_shift_right, 1, OP.bitwise_and)
 
     cp(V("p0"), G(V("nt"), L(LT3 + 2, 1)))
-    act(V("dstb"), G(par0, V("p0")), AF.Identity, 1.0, 16.0)
+    ONE, TWO = ((0, 16),), ((0, 8), (8, 16))
+    for lo, hi in (TWO if ASPLIT & 1 else ONE):
+        (act if lo == 0 else vact)(V("dstb", 16 * lo, 16 * hi), G(par0, V("p0", lo, hi)), AF.Identity, 1.0, 32.0)
     scan(V("sp"), V("dstb"), V("a2"), OP.max, OP.add)
-    act(V("ddb"), G(pk, V("p0")), AF.Identity, 1.0, LIFT)
-    scan(V("hop"), V("ddb"), V("aa"), OP.max, OP.add)
-    tt(V("df", 0, 16), pk, last16("hop"), OP.subtract)
     ts(V("sm", 16, 32), par0, PTR, OP.mult)
     tt(V("sm", 32, 48), V("sm", 16, 32), V("pw2"), OP.add)
-    act(V("sm", 48, 64), io(16), AF.Copy, PTR)
-    tt(V("sm", 64, 80), V("sm", 32, 48), V("sm", 48, 64), OP.subtract)
-    tt(V("sm", 16, 32), par0, io(16), OP.is_lt)
-    tt(V("sm", 80, 96), V("sm", 64, 80), V("sm", 16, 32), OP.mult)
+    ts(V("sm", 64, 80), par0, PTR, OP.mult, -16 * PTR, OP.add)
+    tt(V("ba", 48, 64), par0, io(16), OP.is_lt)
+    tt(V("sm", 80, 96), V("sm", 64, 80), V("ba", 48, 64), OP.mult)
     tt(V("sm", 48, 64), last16("sp"), io(16), OP.is_equal)
     tt(V("sm", 64, 80), V("sm", 48, 64), V("sm", 80, 96), OP.mult)
-    tt(V("cu"), V("sm", 32, 48), V("sm", 64, 80), OP.subtract)
-    aim(V("cu"))
-    ancestors(V("p1"))
+    tt(V("cu", 0, 16), V("sm", 32, 48), V("sm", 64, 80), OP.subtract)
+    act(V("w"), par0, AF.Exp, LN2)
+    act(V("hh"), io(16, 32), AF.Copy, PTR)
+    tt(V("ba", 0, 16), V("hh"), V("w"), OP.subtract)
+    tt(V("ba", 16, 32), V("ba", 0, 16), V("ba", 48, 64), OP.mult)
+    tt(V("ba", 32, 48), V("sm", 48, 64), V("ba", 16, 32), OP.mult)
+    tt(last16("aa"), V("pwd"), V("ba", 32, 48), OP.add)
+    ancestors("p0", TWO if ASPLIT & 1 else ONE)
 
     cp(V("lnod"), V("ni", 0, 16))
-    cp(G(V("rr"), V("lnod")), V("scv"))
-    act(V("r5"), G(V("rr"), L(LD, 32)))
-    tp(V("t5"), V("r5"))
-    cp(V("sel"), G(V("t5"), L(LSEL, 1)))
-    cp(V("inv"), V("sel"))
+    for lo, hi in TWO:
+        cp(G(V("rr"), V("lnod", lo, hi)), V("scv", 16 * lo, 16 * hi))
+    scan(V("sr"), V("rr"), V("a3"), OP.max, OP.add)
+    cp(V("inv"), last16("sr"))
 
     bank = lambda b, n: V("pa", 512 * b, 512 * b + n)
     eq = lambda b: (V("qe", 128 * b, 128 * b + 128), V("se", 128 * b, 128 * b + 128))
@@ -333,157 +374,215 @@ def program(CYC):
             mx(V("ps", 512 * h, 512 * h + 128), lq, ls, q, s)
 
     for r in range(ROUNDS):
-        ct, last, at = "ct%d" % r, r == ROUNDS - 1, 112 * (ROUNDS - 1 - r)
+        ct, last = "ct%d" % r, r == ROUNDS - 1
         state_product(V("qu"), V("su"))
+        early = r in EARLY
+        if early:
+            send(r, "av", V("pq%d" % r), V("qx"), 6500.0 if last else 5000.0)
+            ops[-1]["cost"] += 0.0 if r else 1500.0
+            send(r, "av", V("pp%d" % r), V("sx"), 6500.0 if last else 5000.0)
         if r == 0:
-            load("s", V("lq", 336, 352), V("qx", 0, 16))
-            load("s", V("ls", 336, 352), V("sx", 0, 16))
+            for k in range(ROUNDS):
+                if k not in EARLY:
+                    load("s", V("pq%d" % k, 112, 128), V("qx", 0, 16))
+                    load("s", V("pp%d" % k, 112, 128), V("sx", 0, 16))
         for b in range(4):
             mx(bank(b, 256), eq(b)[0], eq(b)[1], V("qx"), V("sx"))
         for h in range(2):
             act(V("ssb", 128 * h, 128 * h + 128), V("ps", 512 * h, 512 * h + 128))
-        act(V("g1"), G(V("ssb"), V("lg1")))
-        tp(V("tr"), V("g1"))
+        for lo, hi in (TWO if CSPLIT & 8 else ONE):
+            act(V("g1", 16 * lo, 16 * hi), G(V("ssb"), V("lg1", lo, hi)))
+            tp(V("tr", 16 * lo, 16 * hi), V("g1", 16 * lo, 16 * hi))
         parts = ((0, 8), (8, 16)) if GSPLIT else ((0, 16),)
         for lo, hi in parts:
             act(V("gb", 16 * lo, 16 * hi), G(V("tr"), L(LB + lo, hi - lo)))
             tt(V("c1", 16 * lo, 16 * hi), G(V("tr"), L(LA + lo, hi - lo)), V("gb", 16 * lo, 16 * hi), OP.is_gt)
-        scan(V("s1"), V("ms"), V("c1"))
+        cuts = [(16 * lo, 16 * hi) for lo, hi in (TWO if CSPLIT & 1 else ONE)]
+        for lo, hi in cuts:
+            scan(V("s1", lo, hi), V("ms", lo, hi), V("c1", lo, hi))
         tt(en, io(16, 32), last16("s1"), OP.subtract)
         for b in range(4):
             act(V("fw", 384 * b, 384 * b + 256), bank(b, 256))
+        for b in range(4 if early else 0):
+            mx(bank(b, 256), eq(b)[0], eq(b)[1], V("pq%d" % r), V("pp%d" % r))
+            act(V("fp", 256 * b, 256 * b + 256), bank(b, 256))
+        act(V("dpb"), G(V("pe", 16, 33), V("p0")), AF.Identity, 1.0, LIFT)
         act(V("w"), last16("s1"), AF.Exp, LN2)
-        act(V("dstb"), G(en, V("p0")), AF.Identity, 1.0, 16.0)
-        tt(V("pr"), G(V("w"), L(LO, 16)), V("bits"), OP.mult)
-        scan(V("bm"), V("rh"), V("pr"))
+        ops[-1]["r"] += [V("dpb")] if HINT else []
+        act(V("dstb"), G(V("own", 16, 33), V("p0")), AF.Identity, 1.0, 32.0)
+        for lo, hi in [(16 * lo, 16 * hi) for lo, hi in (TWO if CSPLIT & 2 else ONE)]:
+            tt(V("pr", lo, hi), G(V("w"), L(LO, (hi - lo) // 16)), V("bits", lo, hi), OP.mult)
+            scan(V("bm", lo, hi), V("rh", lo, hi), V("pr", lo, hi))
         act(V("gg"), last16("bm"), AF.Abs, 1.0, -HALF)
         for lo, hi in parts:
-            act(V("ai", 16 * lo, 16 * hi), G(V("bm"), L(LO16 + lo, hi - lo)), AF.Abs, 1.0, -HALF)
+            act(V("ai", 16 * lo, 16 * hi), G(V("bm", 16 * lo, 16 * hi), L(LO16, hi - lo)), AF.Abs, 1.0, -HALF)
             tt(V("c2", 16 * lo, 16 * hi), G(V("gg"), L(LO, hi - lo)), V("ai", 16 * lo, 16 * hi), OP.is_gt)
-        scan(V("posm"), V("rm"), V("c2"))
+        for lo, hi in cuts:
+            scan(V("posm", lo, hi), V("rm", lo, hi), V("c2", lo, hi))
         scan(V("sp"), V("dstb"), V("a2"), OP.max, OP.add)
         tt(V("df", 16, 32), en, last16("sp"), OP.subtract)
+        scan(V("ep"), V("dpb"), V("a3"), OP.max, OP.add)
+        tt(V("df", 0, 16), pk, last16("ep"), OP.subtract)
         ts(V("fl", 0, 32), G(V("bm"), L(LE, 2)), HALF, OP.is_lt)
         tt(V("fl", 32, 64), V("df"), V("fl", 0, 32), OP.mult)
         tt(V("pay", 0, 32), V("own", 0, 32), V("fl", 32, 64), OP.subtract)
-        tt(V("d3"), V("pay", 0, 32), V("pay", 1, 33), OP.subtract)
-        act(V("dbe"), G(V("d3"), L(LO + 16, 8)))
-        act(V("dbp"), G(V("d3"), L(LO, 8)))
+        tt(V("d3", 0, 32), V("pay", 0, 32), V("pay", 1, 33), OP.subtract)
+        act(V("dbe"), G(V("d3", 16, 32), L(LO, 8)))
+        act(V("dbp"), G(V("d3", 0, 16), L(LO, 8)))
         tt(V("mk", 0, 128), G(V("posm"), L(LE, 8)), V("ib", 0, 128), OP.not_equal)
         scan(V("eb", 0, 128), V("mk", 0, 128), V("dbe"))
-        cp(V("ws%d" % r), G(V("eb", 0, 129), L(LS, 4)))
-        send(r, "aw", V(ct, 8, 64), V("ws%d" % r, 0, 56), 1900.0)
-        scan(V("ef", 0, 128), V("mk", 0, 128), V("dbp"))
-        ts(V("vl", 0, 7), last16("ef", 16, 112), col("pay", 16), OP.add, 1 / 32, OP.mult)
+        if early:
+            whole(V("d3", 32, 48), V("d3", 0, 16), COL)
+            act(V("dbc"), G(V("d3", 32, 48), L(LO, 7)), AF.Copy, 1 / COL)
+            scan(V("eb", 144, 256), V("mk", 16, 128), V("dbc"))
+            scan(V("ef", 0, 16), V("mk", 0, 16), V("d3", 0, 16))
+        else:
+            scan(V("ef", 0, 128), V("mk", 0, 128), V("dbp"))
+            ts(V("vl", 0, 7), last16("ef", 16, 112), col("pay", 16), OP.add, 1 / COL, OP.mult)
+        cp(V("ws%d" % r), G(V("eb", 0, 256), L(LS, 4)))
+        send(r, "aw", V(ct, 80, 136), V("ws%d" % r, 0, 56), 1900.0 if last else 1600.0)
+        if early:
+            cp(V("vl", 0, 7), V(ct, 87, 136, 8))
         for b in range(4):
-            src = G(V("fw", 384 * b, 384 * b + 256), V("vl", 0, 7))
-            if b % 2:
-                act(V("give", b, 448, 4), src, AF.Copy, 2.0)
-            else:
-                ts(V("give", b, 448, 4), src, 2.0, OP.mult)
-        quant(V("qo%d" % r), V("so%d" % r), V("give"))
-        send(r, "av", V("lq", at, at + 112), V("qo%d" % r, 0, 112), 3600.0 if last else 2300.0)
-        send(r, "av", V("ls", at, at + 112), V("so%d" % r, 0, 112), 3300.0 if last else 2000.0)
+            src = G(V("fp", 256 * b, 256 * b + 256) if early else V("fw", 384 * b, 384 * b + 256), V("vl", 0, 7))
+            (act if early or b % 2 else vact)(V("give", b, 448, 4), src, AF.Copy, 2.0)
+        made = (V("qo"), V("so")) if early else (V("qg"), V("sg"))
+        quant(made[0], made[1], V("give"))
+        if not early:
+            send(r, "av", V("pq%d" % r, 0, 112), V("qg", 0, 112), 2300.0)
+            send(r, "av", V("pp%d" % r, 0, 112), V("sg", 0, 112), 2000.0)
+            made = V("pq%d" % r, 0, 128), V("pp%d" % r, 0, 128)
         act(V("sto"), G(en, L(LO, 8)))
         act(V("sti"), G(V("own", 16, 33), L(LSTI, 16)))
         act(V("ini", 0, 256, 16), en, AF.Exp, 2 * LN2, -LN2)
-        act(V("ba", 32, 48), en, AF.Identity, 1.0, -2.0)
         tt(V("mk", 128, 256), G(V("posm"), L(LE, 8)), V("ib", 128, 256), OP.not_equal)
-        scan(V("eb", 144, 272), V("mk", 128, 256), V("dbe"))
-        act(V(ct, 80, 144), G(V("eb", 144, 273), L(LOWN, 4)))
-        act(V("ki", 64, 128, 8), last16("eb", 144, 128))
-        tt(V("oq"), G(V("ki", 64, 129), L(LTO, 4)), V(ct, 80, 144), OP.not_equal)
-        scan(V("ro"), V("oq"), V("ki", 64, 128))
-        act(V("ki", 64, 128, 8), V("ro", 7, 64, 8))
+        scan(V("eb", 256, 384), V("mk", 128, 256), V("dbe"))
+        act(V(ct, 0, 64), G(V("eb", 256, 385), L(LOWN, 4)))
+        act(V("ki", 0, 64, 8), last16("eb", 256, 128))
+        tt(V("oq"), G(V("ki", 0, 65), L(LTO, 4)), V(ct, 0, 64), OP.not_equal)
+        scan(V("ro"), V("oq"), V("ki", 0, 64))
+        act(V("ki", 0, 64, 8), V("ro", 7, 64, 8))
         scan(V("ef", 128, 256), V("mk", 128, 256), V("dbp"))
         ts(V("vs", 9, 16), last16("ef", 128, 112), col("pay", 16), OP.add)
-        act(V("vp", 9, 16), last16("ef", 128, 112), AF.Identity, 1.0, col("pay", 16))
+        whole(V("vp", 17, 24), V("vs", 9, 16), COL)
+        tt(V("vp", 24, 31), V("vs", 9, 16), V("vp", 17, 24), OP.subtract)
+        act(V("vp", 9, 16), V("vp", 24, 31), AF.Copy, PTR / NODE)
         ts(col("vs", 1), col("ef", 15), col("pay", 16), OP.add)
         tt(V("ds"), V("vs", 0, 16), V("vs", 1, 17), OP.subtract)
         act(V("dsb"), G(V("ds"), L(LO, 16)))
         act(col("dca", 15), col("vs", 1), AF.Identity, -1.0, col("own", 15))
         if not last:
-            ts(V("ba", 16, 32), en, 1.0, OP.not_equal)
-            tt(V("ba", 0, 16), V("ba", 16, 32), V("pw2"), OP.mult)
-            act(last16("aa"), V("ba", 0, 16), AF.Identity, 1.0, drop)
-        act(V("ki", 0, 56, 8), V(ct, 8, 15))
-        tt(V("qq"), G(V(ct, 0, 16), L(LTR, 8)), V(ct, 16, 144), OP.not_equal)
+            act(last16("aa"), V("pwd"))
+        act(V("ki", 72, 128, 8), V(ct, 128, 135))
+        tt(V("qq"), G(V(ct, 128, 144), L(LTR, 8)), V(ct, 0, 128), OP.not_equal)
+        ops[-1]["r"] += [V("inv"), V("dsb")] + ([V("fp")] if early and not last else [])
         scan(V("rq", 0, 128), V("qq"), V("ki", 0, 128))
-        tt(V("dd"), G(V("rq", 0, 129), L(LK, 16)), V("sti"), OP.subtract)
-        ts(V("fi"), V("dd"), 1.0, OP.min, -0.25, OP.max)
-        scan(V("mg"), V("fi"), V("ini"))
-        ts(V("mm"), V("mg"), ROUGH, OP.add, ROUGH, OP.is_equal)
-        act(col("ma", 32), col(ct, 14), AF.Relu, 1.0, -2.0)
-        ts(V("ma", 0, 16), V("ba", 32, 48), col("ma", 32), OP.not_equal)
+        cuts = [(16 * lo, 16 * hi) for lo, hi in (TWO if CSPLIT & 4 else ONE)]
+        for lo, hi in cuts:
+            tt(V("dd", lo, hi), G(V("rq", 0, 129), L(LK, (hi - lo) // 16)), V("sti", lo, hi), OP.subtract)
+            ts(V("fi", lo, hi), V("dd", lo, hi), 1.0, OP.min, -0.25, OP.max)
+            scan(V("mg", lo, hi), V("fi", lo, hi), V("ini", lo, hi))
+            ts(V("mm", lo, hi), V("mg", lo, hi), ROUGH, OP.add, ROUGH, OP.is_equal)
+        act(col("ma", 32), col(ct, 128), AF.Relu, 1.0, -2.0)
+        ts(V("ma", 0, 16), en, -2.0, OP.add, col("ma", 32), OP.not_equal)
         scan(V("ma", 16, 32), V("ma", 0, 16), V("dca"))
         act(V("dsb", 0, 256, 16), z(16), AF.Identity, 1.0, col("ma", 31))
-        scan(V("sr"), V("mm"), V("dsb"))
-        ts(V("sl"), last16("sr"), 1 / 32, OP.mult)
+        for lo, hi in cuts:
+            scan(V("sr", lo, hi), V("mm", lo, hi), V("dsb", lo, hi))
+        for lo, hi in (TWO if CSPLIT & 16 else ONE):
+            ts(V("sl", lo, hi), last16("sr", 16 * lo, 16 * (hi - lo)), 1 / COL, OP.mult)
         for b in range(4):
-            mx(bank(b, 128), eq(b)[0], eq(b)[1], V("lq", at, at + 128), V("ls", at, at + 128))
+            mx(bank(b, 128), eq(b)[0], eq(b)[1], made[0], made[1])
             act(V("fw", 384 * b + 256, 384 * b + 368), bank(b, 112))
         for b in range(4):
-            (cp if b == 0 and (last or HN0) else act)(V("hn", 256 * b, 256 * b + 256), G(V("fw", 384 * b, 384 * b + 368), V("sl")))
-            for lo, hi in (((0, 128), (128, 256)) if b >= ZSPLIT else ((0, 256),)):
+            for lo, hi in (TWO if CSPLIT & 16 and b == 0 else ONE):
+                (cp if b == 0 and lo == 0 and (last or HN0) else act)(V("hn", 256 * b + 16 * lo, 256 * b + 16 * hi), G(V("fw", 384 * b, 384 * b + 368), V("sl", lo, hi)))
+            for lo, hi in (((0, 128), (128, 256)) if b >= (ZLAST if last else ZSPLIT) else ((0, 256),)):
                 tt(V("zt", 4 * lo + b, 4 * hi, 4), G(V("hn", 256 * b, 256 * b + 256), V("inv", lo // 16, hi // 16)), V("fw", 384 * b + lo, 384 * b + hi), OP.add)
-                act(V("z32", 256 * b + lo, 256 * b + hi), V("zt", 4 * lo + b, 4 * hi, 4), AF.Copy, 32.0)
+                if not MERGE & 1:
+                    act(V("z32", 4 * lo + b, 4 * hi, 4), V("zt", 4 * lo + b, 4 * hi, 4), AF.Copy, 32.0)
         for h, (lo, hi) in enumerate(((0, 128), (128, 256)) if HALVES else ((0, 256),)):
             quant(V("qz", lo, hi), V("sz", lo, hi), V("zt", 4 * lo, 4 * hi))
+            if MERGE & 1:
+                act(V("z32", 4 * lo, 4 * hi), V("zt", 4 * lo, 4 * hi), AF.Copy, 32.0)
             for b in range(4):
                 out = (bank(b, hi - lo) if h == 0 else V("pb" if b < 2 else "ps", 512 * (b % 2), 512 * (b % 2) + 128))
                 mx(out, V("qw", 128 * b, 128 * b + 128), V("sw", 128 * b, 128 * b + 128), V("qz", lo, hi), V("sz", lo, hi))
-                x32 = V("x32", 256 * b + lo, 256 * b + hi)
-                tt(x32, out, V("z32", 256 * b + lo, 256 * b + hi), OP.add)
-                if b < 3 or (HALVES and h == 0):
-                    act(V("xt", 4 * lo + b, 4 * hi, 4), x32, AF.Copy, 0.03125)
-                else:
-                    ts(V("xt", 4 * lo + b, 4 * hi, 4), x32, 0.03125, OP.mult)
-        tt(V("mo"), G(V(ct, 0, 16), L(LMO, 8)), V("sto"), OP.not_equal)
-        scan(V("mp"), V("mo"), V("dpkb"))
+                x32 = V("x32", 4 * lo + b, 4 * hi, 4)
+                tt(x32, out, V("z32", 4 * lo + b, 4 * hi, 4), OP.add)
+                if not MERGE & (2 << h):
+                    (act if b < 3 or h == 0 else vact)(V("xt", 4 * lo + b, 4 * hi, 4), x32, AF.Copy, 0.03125)
+            if MERGE & (2 << h):
+                (vact if h else act)(V("xt", 4 * lo, 4 * hi), V("x32", 4 * lo, 4 * hi), AF.Copy, 0.03125)
+        tt(V("mo"), G(V(ct, 128, 144), L(LMO, 8)), V("sto"), OP.not_equal)
+        scan(V("mp"), V("mo"), V("dnb"))
         act(V("vp", 1, 9), last16("mp", 0, 128))
-        tt(V("dp", 1, 16), V("vp", 1, 16), V("vp", 2, 17), OP.subtract)
+        tt(V("dp"), V("vp", 0, 16), V("vp", 1, 17), OP.subtract)
         act(V("dpb"), G(V("dp"), L(LO, 16)))
         if last:
-            act(V("dpb", 0, 256, 16), z(16), AF.Identity, 1.0, col("ma", 31))
+            scan(V("ma", 48, 64), V("ma", 0, 16), V("dnb", 0, 16))
+            ts(V("dpb", 0, 256, 16), z(16), col("ma", 63), OP.add, col("vp", 1), OP.subtract)
+        else:
+            act(last16("dpb"), V("pw2"), AF.Identity, 1.0, col("vp", 15))
         scan(V("ep"), V("mm"), V("dpb"))
-        cp(V("li", 0, 16), last16("ep"))
-        ts(V("li", 16, 32), V("li", 0, 16), 31, OP.bitwise_and)
         if last:
-            cp(V("lk"), V("li", 16, 32))
+            act(V("lk"), last16("ep"), AF.Copy, 1 / PTR)
             store("s", "op", V("lk"))
         else:
-            cp(V("p0"), V("li", 16, 32))
-            ts(V("hh"), V("li", 16, 32), PTR, OP.mult)
-            tt(V("cu"), V("hh"), V("ba", 0, 16), OP.add)
-            tt(V("df", 0, 16), pk, last16("ep"), OP.subtract)
-            ancestors(V("p0"))
+            act(V("cu", 0, 16), last16("ep"))
+            ts(V("p0"), last16("ep"), 1 / PTR, OP.mult)
+            ancestors("p0", TWO if ASPLIT & 2 else ONE)
     state_product(V("qv"), V("sv"))
-    store("s", "oc", V("qx"))
-    act(V("ysb", 0, 128), V("ps", 0, 128))
-    cp(V("ysb", 128, 256), V("ps", 512, 640))
-    store("a", "y", V("ysb"))
+    for h in range(2):
+        store("s", "oc", V("qx", 128 * h, 128 * h + 128))
+        act(V("ysb", 128 * h, 128 * h + 128), V("ps", 512 * h, 512 * h + 128))
+        store("a", "y", V("ysb", 128 * h, 128 * h + 128))
     for k in range(4):
-        store("s", "osc", V("sx"), k)
+        store("sa"[k % 2], "osc", V("sx"), k)
     return ops
 
 
 def replay(table, seq):
     free, end, top = [0.0] * len(QUEUES), [0.0] * len(seq), 0.0
     for n in seq:
-        q, cost, late, deps = table[n]
-        t = free[q]
+        q, cost, late, deps, wake = table[n]
+        t = t0 = free[q]
         for d, lag in deps:
             if end[d] + lag > t:
                 t = end[d] + lag
-        t += cost
+        t += cost + wake if t > t0 else cost
         end[n] = free[q] = t
         if late and t + late > top:
             top = t + late
     return top, end
 
 
-def blocked(table, seq):
-    top, end = replay(table, seq)
+def shift(table, seq, run, lo, hi):
+    top, old = run
+    end, free, same, last = old[:], [0.0] * len(QUEUES), 0, None
+    for n in seq[max(lo - 60, 0):lo]:
+        free[table[n][0]] = old[n]
+    for i in range(lo, len(seq)):
+        n = seq[i]
+        q, cost, late, deps, wake = table[n]
+        t = t0 = free[q]
+        for d, lag in deps:
+            if end[d] + lag > t:
+                t = end[d] + lag
+        t += cost + wake if t > t0 else cost
+        end[n] = free[q] = t
+        if i > hi:
+            t -= old[n]
+            if last is not None and -1e-6 < t - last < 1e-6:
+                same += 1
+                if same == 30:
+                    return t, end, i + 1
+            else:
+                same, last = 0, t
+    return max(end[n] + table[n][2] for n in seq[-40:]) - top, end, len(seq)
+
+
+def blocked(table, seq, end):
     before, last = {}, {}
     for n in seq:
         before[n] = last.get(table[n][0])
@@ -496,7 +595,7 @@ def blocked(table, seq):
             pairs.append((m, n))
             n = m
         else:
-            n = next((d for d, lag in table[n][3] if abs(end[d] + lag - start) < 1e-6), None)
+            n = next((d for d, lag in table[n][3] if abs(end[d] + lag + table[n][4] - start) < 1e-6), None)
     return pairs
 
 
@@ -528,8 +627,17 @@ def order(ops):
             far |= above[d]
         o["near"] = sorted(d for d in o["deps"] if not far >> d & 1)
         above.append(far | sum(1 << d for d in o["deps"]))
-    flat = [[(QUEUES.index(o["q"]), t["cost"], o["late"], [(d, ops[d]["late"] + wake) for d in o["near"]]) for o, t in zip(ops, program(cycle))]
-            for cycle, wake in PACES]
+    timed = [program(pace[0], pace[3], pace[4]) for pace in PACES]
+    flat = [[(QUEUES.index(o["q"]), t["cost"] + ISSUE, o["late"], [(d, ops[d]["late"] + lag) for d in o["near"]], wake) for o, t in zip(ops, same)]
+            for same, (cycle, lag, wake, slow, pick) in zip(timed, PACES)]
+    spare = [{n: (QUEUES.index(t["other"][0]), t["other"][3] + ISSUE) + table[n][2:] for n, t in enumerate(same) if "other" in t} for same, table in zip(timed, flat)]
+
+    def swap(n):
+        o = ops[n]
+        o["q"], o["kind"], o["args"], o["cost"], o["other"] = o["other"] + ((o["q"], o["kind"], o["args"], o["cost"]),)
+        for table, rest in zip(flat, spare):
+            table[n], rest[n] = rest[n], table[n]
+
     score = lambda s: sum(replay(t, s)[0] for t in flat)
     tail = [o["cost"] + o["late"] for o in ops]
     users = [[] for o in ops]
@@ -571,32 +679,58 @@ def order(ops):
         total = score(seq)
         if best is None or total < best[0]:
             best = (total, seq)
-    total, seq = best
-    held = None
-    for turn, (a, b, c, e) in enumerate(np.random.default_rng(7).random((MOVES, 4)).tolist()):
-        if held is None:
-            end = replay(flat[0], seq)[1]
-            seq.sort(key=lambda m: end[m] - ops[m]["cost"])
-            held = blocked(flat[turn % len(flat)], seq)
-        step = 1 if b < 0.5 else -1
-        n = held[int(a * len(held))][step < 0] if e < 0.7 and held else seq[int(a * len(seq))]
-        i = seq.index(n)
-        hops, j, to = 1 + int(c * c * 8), i, None
-        stop = set(users[n]) if step > 0 else ops[n]["deps"]
-        while hops and 0 <= j + step < len(seq) and seq[j + step] not in stop:
-            j += step
-            if ops[seq[j]]["q"] == ops[n]["q"]:
-                hops -= 1
-                to = j
-        if to is None:
-            continue
-        new = seq[:i] + seq[i + 1:]
-        new.insert(to, n)
-        t = score(new)
-        if t <= total + SLACK * (1.0 - turn / MOVES) ** 2 * c:
-            total, seq, held = t, new, None
-            if t < best[0]:
-                best = (t, list(new))
+    def improve(seq, seed, moves, span):
+        taken, pool = 0, seq[max(span[0], 0):span[1]]
+        free = set(pool)
+        for turn, (a, b, c, e) in enumerate(np.random.default_rng(seed).random((moves, 4)).tolist()):
+            if taken % 16 == 0:
+                runs = [replay(t, seq) for t in flat]
+                end = runs[0][1]
+                seq.sort(key=lambda m: end[m] - ops[m]["cost"])
+                held = [p for p in blocked(flat[turn % len(flat)], seq, runs[turn % len(flat)][1]) if p[1] in free]
+                taken += 1
+            step = 1 if b < 0.5 else -1
+            n = held[int(a * len(held))][step < 0] if e < 0.8 and held else pool[int(a * len(pool))]
+            i = seq.index(n)
+            turned = "other" in ops[n] and turn % 3 == 0
+            if turned:
+                swap(n)
+            hops, j, to = int(c ** 3 * 30) + (0 if turned else 1), i, i
+            stop = set(users[n]) if step > 0 else ops[n]["deps"]
+            while hops and 0 <= j + step < len(seq) and seq[j + step] not in stop:
+                j += step
+                if ops[seq[j]]["q"] == ops[n]["q"]:
+                    hops -= 1
+                    to = j
+            if to == i and not turned:
+                continue
+            new = seq[:i] + seq[i + 1:]
+            new.insert(to, n)
+            moved = [shift(t, new, run, min(i, to), max(i, to)) for t, run in zip(flat, runs)]
+            if sum(m[0] for m in moved) <= SLACK * (1.0 - turn / moves) ** 2 * c:
+                for by, end, rest in moved:
+                    if by:
+                        for m in new[rest:]:
+                            end[m] += by
+                seq, runs, taken = new, [(run[0] + m[0], m[1]) for run, m in zip(runs, moved)], taken + 1
+            elif turned:
+                swap(n)
+        return seq
+
+    def queues(want):
+        for n, q in enumerate(want):
+            if ops[n]["q"] != q:
+                swap(n)
+
+    best += ([o["q"] for o in ops],)
+    for seed in range(TRIES):
+        queues(best[2])
+        part = (seed - 1) % STRETCHES * len(ops) // STRETCHES
+        span = (part - 30, part + len(ops) // STRETCHES + 30) if seed else (0, len(ops))
+        seq = improve(list(best[1]), seed, MOVES // (8 if seed else 1), span)
+        if score(seq) < best[0]:
+            best = (score(seq), seq, [o["q"] for o in ops])
+    queues(best[2])
     seq = best[1]
     end = replay(flat[0], seq)[1]
     for n, o in enumerate(ops):
@@ -609,16 +743,20 @@ def order(ops):
         need = {}
         for d in o["deps"]:
             kind = ops[d]["kind"]
-            key = ("in",) + ops[d]["args"][:2] if kind == "send" else ("dma", d) if kind in ("load", "store") else ops[d]["q"]
+            if kind == "send":
+                side = "out" if any(cells(ops[d]["r"][0]) & cells(v) for v in o["w"]) else "in"
+                key = (side,) + ops[d]["args"][:2]
+            else:
+                key = ("dma", d) if kind in ("load", "store") else ops[d]["q"]
             if k.get(key, -1) < place[d] and place[d] > place.get(need.get(key, -1), -1):
                 need[key] = d
         waits = []
         for key, d in sorted(need.items(), key=lambda e: -place[e[1]]):
             if k.get(key, -1) >= place[d]:
                 continue
-            waits.append(d)
+            waits.append((d, key[0] == "out"))
             ops[d]["inc"] = True
-            if key[0] == "in":
+            if key[0] in ("in", "out"):
                 k[key] = len(seq)
                 continue
             k[key] = place[d]
@@ -630,7 +768,7 @@ def order(ops):
     return seq
 
 
-OPS = program(PACES[0][0])
+OPS = program(PACES[0][0], PACES[0][3], PACES[0][4])
 SEQ = order(OPS)
 
 
@@ -654,28 +792,30 @@ def rank_program(g, core, T, topo):
         return ap(v).bitcast(dt.uint8) if BUF[v[0]][0] == Q4 else ap(v)
 
     partner = [T.cores[rank ^ (1 << r)] for r in range(ROUNDS)]
-    common = [e for e in topo.engines(core, partner[0]) if all(e in topo.engines(core, c) for c in partner)]
-    mask = sum(1 << e for e in common)
-    lanes = len(common)
     done = {q: 0 for q in QUEUES}
-    mark, ndma, sent, stores = {}, [0], [0], []
+    mark, ndma, sent, stores = {}, [0], {}, []
     for n in SEQ:
         o = OPS[n]
         e, kind, a = eng[o["q"]], o["kind"], o["args"]
-        for d in o["waits"]:
-            e.wait_ge(T.sem[mark[d][0]], mark[d][1])
+        for d, left in o["waits"]:
+            e.wait_ge(T.sem["left%d" % OPS[d]["args"][0] if left else mark[d][0]], mark[d][1])
         if kind == "send":
             r, sem, out, src = a
             rid, pid, sengine = topo.addr(partner[r])
-            g.remote_dma(raw(out), raw(src), T.sem["%s%d" % (sem, r)], T.sem.sent, pid, rid, mask)
-            sent[0] += lanes
+            local = "left%d" % r if sem == "av" else "sent"
+            lanes = len(topo.engines(core, partner[r]))
+            g.remote_dma(raw(out), raw(src), T.sem["%s%d" % (sem, r)], T.sem[local], pid, rid, topo.mask(core, partner[r]))
+            sent[local] = sent.get(local, 0) + lanes
             mark[n] = ("%s%d" % (sem, r), lanes * (1 if sem == "aw" else 2))
             continue
         if kind in ("load", "store"):
             if kind == "load":
                 ins = e.dma_start(raw(a[0]), raw(a[1]) if isinstance(a[1], tuple) else T[a[1]][:])
-            elif a[2] is None:
+            elif a[0] == "op":
                 ins = e.dma_start(T[a[0]][:], raw(a[1]))
+            elif a[2] is None:
+                wide = 4 if a[0] == "oc" else 1
+                ins = e.dma_start(T[a[0]][:, wide * a[1][1]:wide * a[1][2]], raw(a[1]))
             else:
                 ins = e.dma_start(T[a[0]][4 * a[2]:4 * a[2] + 4, :], T[a[1][0]][32 * a[2]:32 * a[2] + 4, :])
             mark[n] = ("d%d" % ndma[0], 16)
@@ -723,6 +863,7 @@ def rank_program(g, core, T, topo):
             done[o["q"]] += 1
             mark[n] = ("q" + o["q"], done[o["q"]])
             ins.then_inc(T.sem[mark[n][0]], 1)
-    g.wait_ge(T.sem.sent, sent[0])
+    for local, total in sent.items():
+        g.wait_ge(T.sem[local], total)
     for e, m in stores:
         e.wait_ge(T.sem[m[0]], m[1])

@@ -8,19 +8,19 @@ SIZE = {F: 4, B: 2, I: 4, U: 2, Q4: 4, S1: 1}
 BUF = {
     "xt": (B, 1024), "qx": (Q4, 256), "sx": (S1, 256), "ut": (B, 512), "qu0": (Q4, 128), "su0": (S1, 128), "qu": (Q4, 128), "su": (S1, 128),
     "vt": (B, 512), "qv": (Q4, 128), "sv": (S1, 128), "qw": (Q4, 512), "sw": (S1, 512), "ez": (B, 520), "qe": (Q4, 512), "se": (S1, 512),
-    "fw": (B, 1536), "fp": (B, 1024), "give": (B, 512), "hn": (B, 1024), "zt": (B, 1024), "z32": (B, 1024), "x32": (B, 1024), "qz": (Q4, 256), "sz": (S1, 256),
-    "ysb": (F, 256), "qo": (Q4, 128), "so": (S1, 128), "qg": (Q4, 128), "sg": (S1, 128),
+    "fw": (B, 2048), "ft": (B, 1024), "fn": (B, 1024), "lcol": (U, 16), "hn": (B, 1024), "zt": (B, 1024), "z32": (B, 1024), "x32": (B, 1024), "qz": (Q4, 256), "sz": (S1, 256),
+    "ysb": (F, 256), "qf": (Q4, 256), "sf": (S1, 256),
     "pi": (I, 8), "pf": (F, 32), "iof": (F, 48), "lc": (U, 200), "la": (I, 96), "lb": (I, 96), "rm": (B, 256), "rh": (B, 256), "ms": (B, 256), "ib": (B, 256),
     "scv": (F, 256), "z16": (F, 16), "pw2": (B, 16), "un": (F, 48), "a2": (B, 256), "aa": (F, 256),
     "ni": (I, 32), "nf": (F, 64), "nt": (F, 64), "t3": (F, 48), "lg1": (U, 16), "lnod": (U, 16), "rr": (F, 256),
-    "inv": (U, 16), "pe": (F, 48), "dnb": (B, 128), "a3": (B, 256), "dca": (F, 16), "sm": (F, 128),
-    "ssb": (F, 256), "g1": (F, 256), "tr": (F, 256), "gb": (F, 256), "c1": (B, 256), "s1": (B, 256), "own": (F, 48), "w": (B, 16),
+    "inv": (U, 16), "pe": (F, 48), "dnb": (F, 112), "dca": (F, 32), "sm": (F, 128), "wd": (F, 48), "dsx": (F, 32), "ex": (F, 64), "pp": (F, 32), "p16": (U, 16),
+    "ssb": (F, 256), "g1": (F, 256), "tr": (F, 256), "gb": (F, 256), "c1": (B, 256), "s1": (B, 272), "own": (F, 48), "w": (B, 16),
     "dstb": (B, 256), "sti": (B, 256), "sto": (B, 128), "pr": (B, 256), "bm": (F, 256), "gg": (F, 16),
     "ai": (F, 256), "c2": (B, 256), "posm": (B, 256), "sp": (B, 256), "df": (F, 32), "fl": (F, 64), "pay": (F, 48), "d3": (F, 48),
-    "dbp": (F, 128), "dbe": (B, 128), "mk": (B, 256), "eb": (B, 400), "dbc": (B, 112), "ef": (F, 256), "vl": (U, 8), "vs": (F, 32), "ds": (F, 16), "dsb": (F, 256),
-    "vp": (F, 32), "oq": (B, 64), "ro": (B, 64), "ki": (B, 144), "qq": (B, 128), "rq": (B, 144), "dd": (B, 256), "fi": (B, 256), "ini": (B, 256),
-    "mg": (B, 256), "ma": (F, 64), "mm": (B, 256), "sr": (F, 256), "sl": (U, 16), "mo": (B, 128), "mp": (B, 128), "dp": (F, 16), "dpb": (F, 256),
-    "ep": (F, 256), "p0": (U, 16), "p1": (U, 16), "cu": (F, 32), "hh": (F, 16), "ba": (F, 64), "pwd": (F, 16), "ddb": (F, 256), "hop": (F, 256),
+    "dbp": (F, 112), "dbe": (B, 128), "mk": (B, 256), "eb": (B, 400), "dbc": (B, 112), "ef": (F, 256), "dsb": (F, 128),
+    "oq": (B, 64), "ro": (B, 64), "ki": (B, 144), "qq": (B, 128), "rq": (B, 144), "dd": (B, 256), "fi": (B, 256), "ini": (B, 256),
+    "mg": (B, 256), "ma": (F, 64), "mm": (B, 256), "sr": (F, 256), "sl": (U, 16), "mo": (B, 112), "dpb": (F, 256),
+    "ep": (F, 256), "p0": (U, 16), "p1": (U, 16), "cu": (F, 72), "eight": (B, 64), "hh": (F, 16), "ba": (F, 64), "pwd": (F, 16), "ddb": (F, 256), "hop": (F, 256),
     "w4": (I, 64), "bits": (I, 256), "lk": (F, 16),
 }
 for _r in range(ROUNDS):
@@ -29,12 +29,16 @@ for _r in range(ROUNDS):
     BUF["pq%d" % _r] = (Q4, 256)
     BUF["pp%d" % _r] = (S1, 256)
 PS = {"pa": 2048, "ps": 1024, "pb": 1024}
-HN0, ZSPLIT, HALVES, GSPLIT = 1, 3, 1, 1
-ZLAST = 0
-EARLY = (0, 1, 2)
+HALVES, GSPLIT = 1, 1
+BYNODE, FIRST, ZSPLIT, ZLAST = (2, 3), (0, 2), (0, 1, 2, 3), (0, 1, 2, 3)
+HOME_MADE = ()
+DIRECT, DSPLIT = 1, 0
+MASKS, PLAIN, WIDE = 0, 1, 1
+PIECES = (2,)
+NEAR, FAR = 5000.0, 6500.0
 ASPLIT, CSPLIT, MERGE, HINT = 1, 30, 0, 0
 HOME, _fill = {}, {"shortf": 0, "shortb": 0}
-for _k in ("pf", "sm", "gg", "df", "fl", "pay", "vs", "ds", "vp", "pw2", "pe", "dca", "w", "d3", "ma", "dp", "un", "cu", "hh", "ba", "pwd", "oq", "ro"):
+for _k in ("pf", "sm", "gg", "df", "fl", "pay", "pw2", "pe", "dca", "w", "d3", "ma", "un", "cu", "hh", "ba", "pwd", "oq", "ro", "wd", "dsx", "ex", "pp"):
     _h = "shortf" if BUF[_k][0] == F else "shortb"
     HOME[_k] = (_h, _fill[_h])
     _fill[_h] += BUF[_k][1]
@@ -45,17 +49,18 @@ for _k, _n in PS.items():
     SCRATCH[_k] = ("psum", [128, _n], F)
 QUEUES = ["v", "a", "p", "g", "s"]
 NDMA = 20
-SEMAPHORES = ["q" + q for q in QUEUES] + ["d%d" % i for i in range(NDMA)] + ["sent"] + ["%s%d" % (s, r) for s in ("aw", "av", "left") for r in range(ROUNDS)]
+SEMAPHORES = ["q" + q for q in QUEUES] + ["d%d" % i for i in range(NDMA)] + ["sent"] + ["%s%d" % (s, r) for s in ("aw", "av0", "av1", "leftav0", "leftav1") for r in range(ROUNDS)]
 
 ISSUE, START = 0.0, 220.0
 PACES = ((0.87, 195.0, 0.0, 1.2, 1.55), (1.05, 200.0, 0.0, 1.5, 1.25), (1.15, 250.0, 0.0, 1.7, 1.9))
-PLANS = [(p, k) for p in (200.0, 400.0, 800.0) for k in range(3)]
-TRIES, STRETCHES = 41, 8
-MOVES, SLACK = 80000, 400.0
+PLANS, SWEEPS, TOLL, GRAIN = 30, 4, 2.0, 400.0
+STARTS, REBUILDS, SPAN, LOOSE, STAY = 3, 25000, 25, 900.0, 500.0
+TRIES, STRETCHES = 9, 8
+MOVES, SLACK = 24000, 150.0
 LN2 = math.log(2.0)
 HALF = 32767.5 / 32768
 PTR, LIFT = 2.0 ** 17, 2.0 ** 22
-COL, NODE = 2048.0, 32.0
+COL, TAKE = 64.0, 2.0 ** 15
 ROUGH = 1.5 * 2.0 ** 24
 LD, LO, LE, LO16, LA, LB, LU, LT3, LSEL, LS, LOWN, LTR, LMO, LK, LSTI, LTO, LSE = 0, 32, 64, 72, 88, 104, 120, 128, 132, 136, 140, 144, 152, 160, 176, 192, 196
 
@@ -187,7 +192,11 @@ def program(CYC, SLOW, PICK):
         ts(out, src, 1.5 * 2.0 ** 23 * unit, OP.add, 1.5 * 2.0 ** 23 * unit, OP.subtract)
 
     def level(out, c):
-        act(out, V("ib", 0, count(out)), AF.Identity, 0.0, c)
+        iota(out, [[0, count(out)]], c, 0)
+        ops[-1]["other"] = ("v", "fill", (out, float(c)), vcost(count(out), out, 0.5 if narrow(out) else 1))
+
+    def select(out, src, pattern, op, other, base, chan):
+        add("g", "select", (out, src, pattern, op, other, base, chan), [src], [out], 170 + 2 * count(out) * CYC)
 
     last16 = lambda name, lo=0, n=256: V(name, lo + 15, lo + n, 16)
     z = lambda n: V("z16", 0, n)
@@ -196,7 +205,9 @@ def program(CYC, SLOW, PICK):
     load("s", V("ni", 16, 32), "par")
     load("a", V("ni", 0, 16), "nod")
     load("s", V("xt"), "x")
+    ops[-1]["behind"] = len(ops) - 3
     load("a", V("ut"), "u")
+    ops[-1]["behind"] = len(ops) - 3
     for out, name in (("qw", "wc"), ("sw", "ws"), ("vt", "v")):
         load("s", V(out), name, (col("xt", 0), col("ut", 0)))
 
@@ -204,18 +215,17 @@ def program(CYC, SLOW, PICK):
     iota(V("iof", 0, 32), [[1, 32]], 0, 0)
     iota(V("iof", 32, 48), [[-1, 16]], 16, 0)
     p0 = col("pi", 0)
-    for i, (shift, mask) in enumerate(((0, 15), (4, 1), (0, 7), (0, 1), (0, 31), (1, 7), (3, 1))):
+    for i, (shift, mask) in enumerate(((0, 15), (4, 1), (0, 7), (0, 1), (0, 31), (3, 1))):
         ts(col("pi", 1 + i), p0, shift, OP.logical_shift_right, mask, OP.bitwise_and)
-    cp(V("pf", 0, 7), V("pi", 1, 8))
-    pq, ph, p8, p2, p32, pj, pe = [col("pf", i) for i in range(7)]
+    cp(V("pf", 0, 6), V("pi", 1, 7))
+    pq, ph, p8, p2, p32, pe = [col("pf", i) for i in range(6)]
     fill(V("z16"), 0.0)
-    iota(V("lb", 0, 32), [[16, 16], [0, 2]], 0, 0)
-    iota(V("lb", 32, 64), [[16, 2], [0, 16]], 0, 0)
-    ts(L(LD, 64), V("lb", 0, 64), pq, OP.add)
-    ts(col("pf", 7), ph, 8.0, OP.mult, pj, OP.add)
-    cp(L(LT3, 1), p32)
-    ts(L(LT3 + 1, 1), p2, 16.0, OP.mult, col("pf", 7), OP.add)
-    ts(L(LT3 + 2, 1), p32, 32.0, OP.add)
+    iota(V("lb", 0, 64), [[16, 4], [0, 16]], 0, 0)
+    ts(V("lc", LD, LD + 4), V("lb", 0, 32, 8), pq, OP.add)
+    ts(L(LO, 16), z(16), pq, OP.add)
+    ts(col("pf", 7), p2, 15.0, OP.mult, pq, OP.add)
+    ts(V("lc", LT3, LT3 + 3, 2), V("lb", 0, 33, 32), p32, OP.add)
+    ts(L(LT3 + 1, 1), col("pf", 7), ph, OP.add)
     ts(col("pf", 8), pq, 16.0, OP.mult, 15.0, OP.add)
     ts(L(LE, 8), z(8), col("pf", 8), OP.add)
     ts(L(LO16, 16), io(16), 16.0, OP.mult, 15.0, OP.add)
@@ -228,10 +238,7 @@ def program(CYC, SLOW, PICK):
     ts(col("un", 15), pq, 15.0, OP.is_equal, -2.0, OP.add)
     ts(V("a2"), G(V("un", 0, 16), L(LO, 16)), 32.0, OP.mult)
     act(V("aa"), V("a2"), AF.Copy, LIFT / 32)
-    act(V("a3"), V("a2"), AF.Copy, LIFT / 32)
-    lifts = col("pf", 17)
-    ts(lifts, col("un", 15), -LIFT, OP.mult)
-    ts(col("pf", 16), col("un", 15), LIFT, OP.mult, 1.5 * 2.0 ** 23 * PTR, OP.add)
+    act(col("pf", 16), col("un", 15), AF.Copy, LIFT)
     ts(V("sm", 96, 100), io(4), 2.0, OP.mult, pe, OP.add)
     later, head, end = col("pf", 13), col("pf", 12), col("pf", 14)
     ts(later, p8, 0.0, OP.is_gt)
@@ -252,8 +259,7 @@ def program(CYC, SLOW, PICK):
     ts(col("pf", 26), col("pf", 25), -10.0, OP.add)
     ts(V("sm", 116, 120), V("sm", 96, 100), p8, OP.is_gt, col("pf", 26), OP.mult)
     ts(L(LTR + 4, 4), V("sm", 116, 120), 9.0, OP.add)
-    cp(L(LMO + 1, 7), io(7))
-    fill(L(LMO, 1), 10)
+    cp(L(LMO, 7), io(7))
     ts(col("pf", 18), pq, 9.0, OP.is_ge, -128.0, OP.mult)
     ts(col("pf", 27), pq, 8.0, OP.mult, col("pf", 18), OP.add)
     ts(col("pf", 28), pq, 2.0, OP.is_ge)
@@ -262,43 +268,40 @@ def program(CYC, SLOW, PICK):
     ts(col("pf", 20), pq, 0.0, OP.is_gt)
     ts(col("pf", 21), pq, 0.0, OP.is_equal, 16.0, OP.mult)
     ts(L(LSTI, 16), io(16), col("pf", 20), OP.mult, col("pf", 21), OP.add)
-    ts(V("la", 48, 64), io(16), pq, OP.max)
-    ts(V("la", 64, 80), io(16), pq, OP.min)
-    ts(V("w4", 0, 32), V("la", 48, 80), 3, OP.logical_shift_right)
-    ts(V("w4", 32, 64), V("w4", 0, 32), -240.0, OP.mult, ph, OP.add)
-    ts(V("w4", 0, 32), V("la", 48, 80), 32.0, OP.mult)
-    tt(V("fl", 0, 32), V("w4", 0, 32), V("w4", 32, 64), OP.add)
-    cp(L(LA, 32), V("fl", 0, 32))
-    fill(V("rh"), 0.5)
-    fill(V("rh", 0, 256, 16), 0.0)
-    fill(V("rm"), 1.0)
-    fill(V("rm", 0, 256, 16), 0.0)
-    fill(V("ms"), 1.0)
-    fill(V("ms", 0, 256, 16), 0.0)
-    fill(V("ms", 17, 256, 17), -1.0)
-    fill(V("give", 448, 512), 0.0)
+    iota(V("la", 48, 64), [[16, 16]], 0, 0)
+    ts(col("pf", 6), pq, 16.0, OP.mult)
+    ts(L(LA, 16), V("la", 48, 64), col("pf", 6), OP.max, ph, OP.add)
+    ts(L(LB, 16), V("la", 48, 64), col("pf", 6), OP.min, ph, OP.add)
+    if MASKS:
+        iota(V("ms"), [[0, 16], [1, 16]], 0, 0)
+        select(V("rh"), V("ms"), [[0, 16], [1, 16]], OP.is_equal, 0.5, 0, 0)
+        select(V("rm"), V("ms"), [[0, 16], [1, 16]], OP.is_equal, 1.0, 0, 0)
+        select(V("ms"), V("ms"), [[0, 16], [1, 16]], OP.is_equal, 1.0, 0, 0)
+    else:
+        for name, c in (("rh", 0.5), ("rm", 1.0), ("ms", 1.0)):
+            fill(V(name), c)
+            level(V(name, 0, 256, 16), 0)
+    level(V("ms", 17, 256, 17), -1)
     act(V("pw2"), io(16), AF.Exp, LN2)
     ops[-1]["cost"] += 1500.0
-    ts(V("pwd"), V("pw2"), lifts, OP.subtract)
-    fill(col("cu", 16), 16 * PTR)
-    fill(col("vp", 0), 16 * PTR)
+    ts(V("pwd"), V("pw2"), col("pf", 16), OP.add)
+    act(V("pp", 0, 16), V("pw2"), AF.Copy, 1 / PTR)
+    act(V("pp", 16, 32), io(16), AF.Copy, PTR)
+    level(col("cu", 16), 16)
     fill(V("ez"), 0.5)
-    iota(V("ib"), [[-1, 16], [0, 16]], 15, 0)
-    add("g", "select", (V("ez"), [[1, 520]], OP.is_equal, 0.0, -3, -4), [V("ez")], [V("ez")], 170 + 1040 * CYC)
+    iota(V("ib", 16, 240), [[-1, 14], [0, 16]], 14, 0)
+    level(V("ib", 240, 256), 15)
+    select(V("ez"), V("ez"), [[1, 520]], OP.is_equal, 0.0, -3, -4)
     iota(V("scv"), [[1, 16], [16, 16]], int(LIFT), 0)
-    for name, c in (("own", 32), ("pay", 32), ("vs", 0), ("vs", 16), ("vp", 16), ("eb", 384), ("rq", 128)):
-        level(col(name, c), 0.0)
+    for name, c in (("own", 16), ("pay", 33), ("fl", 32), ("cu", 40), ("ef", 255), ("eb", 384), ("rq", 128)) + ((("s1", 271),) if DIRECT else ()):
+        level(col(name, c), 0)
     for name, n in (("ki", 128), ("ini", 256)):
-        level(V(name, 0, n), 0.0)
-    level(col("ki", 64), 0.5)
-    level(V("eb", 128, 144), 0.0)
-    ts(V("vs", 2, 9), io(7, 16), 16.0, OP.mult, pq, OP.add)
-    ts(V("vs", 2, 9), V("vs", 2, 9), COL, OP.mult)
-    level(V("dnb"), -PTR)
-    level(last16("dnb", 0, 128), 15 * PTR)
+        level(V(name, 0, n), 0)
+    level(col("ki", 64), 99)
+    level(V("eb", 128, 144), 0)
     for r in range(ROUNDS):
-        act(V("ct%d" % r, 136, 144), io(8), AF.Copy, 0.5)
-        level(V("ct%d" % r, 64, 80), 0.0)
+        iota(V("ct%d" % r, 136, 144), [[-1, 8]], 0, 0)
+        level(V("ct%d" % r, 64, 80), 0)
     for b in range(4):
         quant(V("qe", 128 * b, 128 * b + 128), V("se", 128 * b, 128 * b + 128), V("ez", 3 - b, 515 - b))
 
@@ -306,62 +309,91 @@ def program(CYC, SLOW, PICK):
     tp(V("nt"), V("nf"))
     cp(V("t3", 0, 48), G(V("nt"), L(LT3, 3)))
     par0, colv = V("t3", 32, 48), V("t3", 0, 16)
-    pk, en = V("own", 0, 16), V("own", 16, 32)
+    en, pk = V("own", 0, 16), V("own", 17, 33)
     cp(V("lg1"), V("t3", 16, 32))
+    cp(V("lcol"), colv)
     ts(V("sm", 0, 16), colv, COL, OP.mult)
-    act(V("pe", 32, 48), io(16), AF.Copy, NODE)
-    tt(pk, V("sm", 0, 16), V("pe", 32, 48), OP.add)
-    act(V("pe", 16, 32), pk)
-    tt(V("dca", 0, 15), V("own", 0, 15), V("own", 1, 16), OP.subtract)
+    tt(V("pe", 16, 32), V("sm", 0, 16), io(16), OP.add)
+    act(pk, V("pe", 16, 32))
+    tt(V("pe", 0, 15), V("pe", 16, 31), V("pe", 17, 32), OP.subtract)
+    act(col("pe", 15), col("pe", 31), AF.Identity, 1.0, 256 * TAKE)
+    act(V("dnb"), G(V("pe", 0, 16), L(LO, 7)))
+    act(V("pe", 32, 48), colv, AF.Copy, TAKE + COL)
+    tt(V("dca", 0, 15), V("pe", 32, 47), V("pe", 33, 48), OP.subtract)
+    act(V("dca", 16, 31), V("dca", 0, 15), AF.Identity, 1.0, -1.0)
+    act(col("pf", 9), col("pe", 47), AF.Identity, 1.0, 16.0)
+    act(col("pf", 10), col("pe", 47), AF.Identity, 1.0, 15.0)
     quant(V("qu0"), V("su0"), V("ut"))
     add("v", "pickq", (V("qu"), V("qu0"), L(LU, 8)), [V("qu0"), L(LU, 8)], [V("qu")], 50 + 1.5 * 128 * CYC)
     add("a", "picks", (V("su"), V("su0"), L(LU, 8)), [V("su0"), L(LU, 8)], [V("su")], 65 + 1.5 * 128 * CYC)
     quant(V("qv"), V("sv"), V("vt"))
 
-    def aim(cur):
+    def aim(cur, plain):
         ts(V("p1"), cur, 1 / PTR, OP.mult)
-        ts(V("hh"), cur, 1.5 * 2.0 ** 23 * PTR, OP.add, col("pf", 16), OP.subtract)
-        tt(last16("aa"), cur, V("hh"), OP.subtract)
+        if plain:
+            act(V("cu", 48, 64), cur)
+            ts(V("hh"), cur, 1.5 * 2.0 ** 23 * PTR, OP.add, col("pf", 17), OP.subtract)
+            tt(last16("aa"), cur, V("hh"), OP.subtract)
+        else:
+            tt(V("cu", 24, 40), cur, V("pp", 16, 32), OP.subtract)
+            act(last16("aa"), cur, AF.Identity, 1.0, col("pf", 16))
 
-    def ancestors(first, parts):
+    def ancestors(unit, parts, plain):
         for k in range(4):
             for lo, hi in parts:
                 rows = lambda name: V(name, 16 * lo, 16 * hi)
-                (act if lo == 0 else vact)(rows("ddb"), G(V("cu", 0, 17), V("p1" if k else first, lo, hi)), AF.Identity, 1.0, LIFT)
+                src = G(V("cu", 48, 65) if plain else V("cu", 24, 41), V("p1", lo, hi)) if k else G(V("cu", 0, 17), V("p0", lo, hi))
+                (act if lo == 0 else vact)(rows("ddb"), src, AF.Identity, 1.0 if k else unit, LIFT)
                 scan(rows("hop"), rows("ddb"), rows("aa"), OP.max, OP.add)
             if k < 3:
-                act(V("cu", 0, 16), last16("hop"))
-                aim(last16("hop"))
-        for j in range(4):
+                aim(last16("hop"), plain)
+        if WIDE:
+            tt(V("w4"), G(V("hop"), L(LE, 4)), V("eight"), OP.mult)
+        for j in range(0 if WIDE else 4):
             ts(V("w4", 16 * j, 16 * j + 16), last16("hop"), 0.5 ** j, OP.mult, 0.5 ** (j + 1) - 0.5, OP.add)
         for j in range(4):
-            ts(V("bits", 64 * j, 64 * j + 64), V("w4"), 4 * j, OP.logical_shift_right, 1, OP.bitwise_and)
+            ts(V("bits", 64 * j, 64 * j + 64), V("w4"), 4 * j + 3 * WIDE, OP.logical_shift_right, 1, OP.bitwise_and)
 
     cp(V("p0"), G(V("nt"), L(LT3 + 2, 1)))
     ONE, TWO = ((0, 16),), ((0, 8), (8, 16))
     for lo, hi in (TWO if ASPLIT & 1 else ONE):
-        (act if lo == 0 else vact)(V("dstb", 16 * lo, 16 * hi), G(par0, V("p0", lo, hi)), AF.Identity, 1.0, 32.0)
+        (act if lo == 0 else vact)(V("dstb", 16 * lo, 16 * hi), G(par0, V("p0", lo, hi)), AF.Identity, 1.0, 33.0)
     scan(V("sp"), V("dstb"), V("a2"), OP.max, OP.add)
-    ts(V("sm", 16, 32), par0, PTR, OP.mult)
-    tt(V("sm", 32, 48), V("sm", 16, 32), V("pw2"), OP.add)
-    ts(V("sm", 64, 80), par0, PTR, OP.mult, -16 * PTR, OP.add)
+    tt(V("sm", 16, 32), par0, V("pp", 0, 16), OP.add)
+    act(V("sm", 32, 48), V("sm", 16, 32), AF.Copy, 1 / 16)
     tt(V("ba", 48, 64), par0, io(16), OP.is_lt)
-    tt(V("sm", 80, 96), V("sm", 64, 80), V("ba", 48, 64), OP.mult)
-    tt(V("sm", 48, 64), last16("sp"), io(16), OP.is_equal)
-    tt(V("sm", 64, 80), V("sm", 48, 64), V("sm", 80, 96), OP.mult)
-    tt(V("cu", 0, 16), V("sm", 32, 48), V("sm", 64, 80), OP.subtract)
+    tt(V("sm", 80, 96), V("ba", 48, 64), io(16, 1), OP.mult)
+    tt(V("sm", 48, 64), last16("sp"), V("sm", 80, 96), OP.is_equal)
+    tt(V("cu", 0, 16), V("sm", 32, 48), V("sm", 48, 64), OP.max)
     act(V("w"), par0, AF.Exp, LN2)
     act(V("hh"), io(16, 32), AF.Copy, PTR)
-    tt(V("ba", 0, 16), V("hh"), V("w"), OP.subtract)
-    tt(V("ba", 16, 32), V("ba", 0, 16), V("ba", 48, 64), OP.mult)
+    tt(V("ba", 0, 16), V("hh"), V("pw2"), OP.subtract)
+    tt(V("ba", 16, 32), V("ba", 0, 16), V("w"), OP.subtract)
     tt(V("ba", 32, 48), V("sm", 48, 64), V("ba", 16, 32), OP.mult)
     tt(last16("aa"), V("pwd"), V("ba", 32, 48), OP.add)
-    ancestors("p0", TWO if ASPLIT & 1 else ONE)
+    for j in range(4 * WIDE):
+        level(V("eight", 16 * j, 16 * j + 16), 8 >> j)
+    if PLAIN:
+        level(col("cu", 64), int(16 * PTR))
+        act(col("pf", 17), col("un", 15), AF.Identity, LIFT, 1.5 * 2.0 ** 23 * PTR)
+    ancestors(16 * PTR, TWO if ASPLIT & 1 else ONE, PLAIN & 1)
+    act(V("dpb"), G(V("pe", 16, 32), V("p0")), AF.Identity, 1.0, LIFT)
+    act(last16("aa"), z(16), AF.Identity, 1.0, col("pf", 16))
+    scan(V("ep"), V("dpb"), V("aa"), OP.max, OP.add)
+    tt(V("df", 0, 16), pk, last16("ep"), OP.subtract)
+
+    def beside(link):
+        ts(V("p16"), link, 16.0, OP.mult, 15.0, OP.add)
+        act(last16("a2"), link, AF.Identity, 1.0, col("pf", 19))
+
+    if DIRECT:
+        ts(col("pf", 19), col("un", 15), 32.0, OP.mult, -16.0, OP.add)
+        beside(par0)
 
     cp(V("lnod"), V("ni", 0, 16))
     for lo, hi in TWO:
         cp(G(V("rr"), V("lnod", lo, hi)), V("scv", 16 * lo, 16 * hi))
-    scan(V("sr"), V("rr"), V("a3"), OP.max, OP.add)
+    scan(V("sr"), V("rr"), V("aa"), OP.max, OP.add)
     cp(V("inv"), last16("sr"))
 
     bank = lambda b, n: V("pa", 512 * b, 512 * b + n)
@@ -376,16 +408,26 @@ def program(CYC, SLOW, PICK):
     for r in range(ROUNDS):
         ct, last = "ct%d" % r, r == ROUNDS - 1
         state_product(V("qu"), V("su"))
-        early = r in EARLY
-        if early:
-            send(r, "av", V("pq%d" % r), V("qx"), 6500.0 if last else 5000.0)
-            ops[-1]["cost"] += 0.0 if r else 1500.0
-            send(r, "av", V("pp%d" % r), V("sx"), 6500.0 if last else 5000.0)
-        if r == 0:
-            for k in range(ROUNDS):
-                if k not in EARLY:
-                    load("s", V("pq%d" % k, 112, 128), V("qx", 0, 16))
-                    load("s", V("pp%d" % k, 112, 128), V("sx", 0, 16))
+        home = r in HOME_MADE
+
+        pieces = ((0, 128), (128, 256)) if r in PIECES else ((0, 256),)
+
+        def cross(q, s):
+            for k, (lo, hi) in enumerate(pieces):
+                late = (FAR if last else NEAR) * (0.6 if hi < 256 else 1.0) - 600.0 * k
+                send(r, "av%d" % k, V("pq%d" % r, lo, hi), V(q, lo, hi), late)
+                ops[-1]["cost"] += 0.0 if r or k else 1500.0
+                if k:
+                    ops[-1]["behind"] = len(ops) - 2
+                send(r, "av%d" % k, V("pp%d" % r, lo, hi), V(s, lo, hi), late)
+                ops[-1]["behind"] = len(ops) - 2
+
+        def again():
+            for h in range(2):
+                quant(V("qf", 128 * h, 128 * h + 128), V("sf", 128 * h, 128 * h + 128), V("ft", 512 * h, 512 * h + 512))
+
+        if not home:
+            cross("qx", "sx")
         for b in range(4):
             mx(bank(b, 256), eq(b)[0], eq(b)[1], V("qx"), V("sx"))
         for h in range(2):
@@ -402,14 +444,31 @@ def program(CYC, SLOW, PICK):
             scan(V("s1", lo, hi), V("ms", lo, hi), V("c1", lo, hi))
         tt(en, io(16, 32), last16("s1"), OP.subtract)
         for b in range(4):
-            act(V("fw", 384 * b, 384 * b + 256), bank(b, 256))
-        for b in range(4 if early else 0):
-            mx(bank(b, 256), eq(b)[0], eq(b)[1], V("pq%d" % r), V("pp%d" % r))
-            act(V("fp", 256 * b, 256 * b + 256), bank(b, 256))
-        act(V("dpb"), G(V("pe", 16, 33), V("p0")), AF.Identity, 1.0, LIFT)
+            act(V("fw", 512 * b, 512 * b + 256), bank(b, 256))
+        for b in BYNODE:
+            act(V("fn", 256 * b, 256 * b + 256), G(V("fw", 512 * b, 512 * b + 256), V("lcol")))
+        made = "pq%d" % r, "pp%d" % r
+        if home:
+            for b in range(4):
+                vact(V("ft", b, 1024, 4), V("fw", 512 * b, 512 * b + 256), AF.Copy, 2.0)
+            again()
+            cross("qf", "sf")
+        else:
+            for lo, hi in pieces:
+                for b in range(4):
+                    mx(bank(b, hi - lo), eq(b)[0], eq(b)[1], V(made[0], lo, hi), V(made[1], lo, hi))
+                    act(V("ft", 4 * lo + b, 4 * hi, 4), bank(b, hi - lo), AF.Copy, 2.0)
+            again()
+            made = "qf", "sf"
+        for lo, hi in pieces:
+            for b in range(4):
+                out = V("pb", 512 * (b % 2), 512 * (b % 2) + hi - lo) if lo == 0 and hi < 256 else bank(b, hi - lo)
+                mx(out, eq(b)[0], eq(b)[1], V(made[0], lo, hi), V(made[1], lo, hi))
+                act(V("fw", 512 * b + 256 + lo, 512 * b + 256 + hi), out)
         act(V("w"), last16("s1"), AF.Exp, LN2)
-        ops[-1]["r"] += [V("dpb")] if HINT else []
-        act(V("dstb"), G(V("own", 16, 33), V("p0")), AF.Identity, 1.0, 32.0)
+        for lo, hi in (TWO if DSPLIT else ONE):
+            src = G(V("s1"), V("p16", lo, hi)) if DIRECT else G(V("own", 0, 17), V("p0", lo, hi))
+            act(V("dstb", 16 * lo, 16 * hi), src, AF.Identity, 1.0, 32.0)
         for lo, hi in [(16 * lo, 16 * hi) for lo, hi in (TWO if CSPLIT & 2 else ONE)]:
             tt(V("pr", lo, hi), G(V("w"), L(LO, (hi - lo) // 16)), V("bits", lo, hi), OP.mult)
             scan(V("bm", lo, hi), V("rh", lo, hi), V("pr", lo, hi))
@@ -420,40 +479,25 @@ def program(CYC, SLOW, PICK):
         for lo, hi in cuts:
             scan(V("posm", lo, hi), V("rm", lo, hi), V("c2", lo, hi))
         scan(V("sp"), V("dstb"), V("a2"), OP.max, OP.add)
-        tt(V("df", 16, 32), en, last16("sp"), OP.subtract)
-        scan(V("ep"), V("dpb"), V("a3"), OP.max, OP.add)
-        tt(V("df", 0, 16), pk, last16("ep"), OP.subtract)
-        ts(V("fl", 0, 32), G(V("bm"), L(LE, 2)), HALF, OP.is_lt)
-        tt(V("fl", 32, 64), V("df"), V("fl", 0, 32), OP.mult)
-        tt(V("pay", 0, 32), V("own", 0, 32), V("fl", 32, 64), OP.subtract)
-        tt(V("d3", 0, 32), V("pay", 0, 32), V("pay", 1, 33), OP.subtract)
-        act(V("dbe"), G(V("d3", 16, 32), L(LO, 8)))
-        act(V("dbp"), G(V("d3", 0, 16), L(LO, 8)))
-        tt(V("mk", 0, 128), G(V("posm"), L(LE, 8)), V("ib", 0, 128), OP.not_equal)
-        scan(V("eb", 0, 128), V("mk", 0, 128), V("dbe"))
-        if early:
-            whole(V("d3", 32, 48), V("d3", 0, 16), COL)
-            act(V("dbc"), G(V("d3", 32, 48), L(LO, 7)), AF.Copy, 1 / COL)
-            scan(V("eb", 144, 256), V("mk", 16, 128), V("dbc"))
-            scan(V("ef", 0, 16), V("mk", 0, 16), V("d3", 0, 16))
-        else:
-            scan(V("ef", 0, 128), V("mk", 0, 128), V("dbp"))
-            ts(V("vl", 0, 7), last16("ef", 16, 112), col("pay", 16), OP.add, 1 / COL, OP.mult)
+        tt(V("df", 16, 32), en, last16("sp"), OP.add if DIRECT else OP.subtract)
+        ts(V("fl", 0, 16), last16("bm"), HALF, OP.is_lt)
+        tt(V("fl", 16, 32), V("df", 16, 32), V("fl", 0, 16), OP.mult)
+        tt(V("fl", 33, 49), V("df", 0, 16), V("fl", 0, 16), OP.mult)
+        tt(V("pay", 0, 33), V("own", 0, 33), V("fl", 16, 49), OP.subtract)
+        tt(V("d3", 0, 33), V("pay", 0, 33), V("pay", 1, 34), OP.subtract)
+        act(V("dbe"), G(V("d3", 0, 16), L(LO, 8)))
+        whole(V("wd", 0, 16), V("d3", 17, 33), COL)
+        act(V("dbc"), G(V("wd", 0, 16), L(LO, 7)), AF.Copy, 1 / COL)
+        act(V("wd", 16, 32), V("wd", 0, 16), AF.Copy, TAKE / COL)
+        tt(V("wd", 32, 48), V("wd", 16, 32), V("d3", 17, 33), OP.add)
+        act(V("dbp"), G(V("wd", 32, 48), L(LO, 7)))
+        tt(V("mk", 16, 128), G(V("posm"), L(LE, 7)), V("ib", 16, 128), OP.not_equal)
+        scan(V("eb", 16, 128), V("mk", 16, 128), V("dbe", 0, 112))
+        scan(V("eb", 144, 256), V("mk", 16, 128), V("dbc"))
         cp(V("ws%d" % r), G(V("eb", 0, 256), L(LS, 4)))
         send(r, "aw", V(ct, 80, 136), V("ws%d" % r, 0, 56), 1900.0 if last else 1600.0)
-        if early:
-            cp(V("vl", 0, 7), V(ct, 87, 136, 8))
-        for b in range(4):
-            src = G(V("fp", 256 * b, 256 * b + 256) if early else V("fw", 384 * b, 384 * b + 256), V("vl", 0, 7))
-            (act if early or b % 2 else vact)(V("give", b, 448, 4), src, AF.Copy, 2.0)
-        made = (V("qo"), V("so")) if early else (V("qg"), V("sg"))
-        quant(made[0], made[1], V("give"))
-        if not early:
-            send(r, "av", V("pq%d" % r, 0, 112), V("qg", 0, 112), 2300.0)
-            send(r, "av", V("pp%d" % r, 0, 112), V("sg", 0, 112), 2000.0)
-            made = V("pq%d" % r, 0, 128), V("pp%d" % r, 0, 128)
-        act(V("sto"), G(en, L(LO, 8)))
-        act(V("sti"), G(V("own", 16, 33), L(LSTI, 16)))
+        act(V("sto", 0, 112), G(en, L(LO, 7)))
+        act(V("sti"), G(V("own", 0, 17), L(LSTI, 16)))
         act(V("ini", 0, 256, 16), en, AF.Exp, 2 * LN2, -LN2)
         tt(V("mk", 128, 256), G(V("posm"), L(LE, 8)), V("ib", 128, 256), OP.not_equal)
         scan(V("eb", 256, 384), V("mk", 128, 256), V("dbe"))
@@ -462,20 +506,15 @@ def program(CYC, SLOW, PICK):
         tt(V("oq"), G(V("ki", 0, 65), L(LTO, 4)), V(ct, 0, 64), OP.not_equal)
         scan(V("ro"), V("oq"), V("ki", 0, 64))
         act(V("ki", 0, 64, 8), V("ro", 7, 64, 8))
-        scan(V("ef", 128, 256), V("mk", 128, 256), V("dbp"))
-        ts(V("vs", 9, 16), last16("ef", 128, 112), col("pay", 16), OP.add)
-        whole(V("vp", 17, 24), V("vs", 9, 16), COL)
-        tt(V("vp", 24, 31), V("vs", 9, 16), V("vp", 17, 24), OP.subtract)
-        act(V("vp", 9, 16), V("vp", 24, 31), AF.Copy, PTR / NODE)
-        ts(col("vs", 1), col("ef", 15), col("pay", 16), OP.add)
-        tt(V("ds"), V("vs", 0, 16), V("vs", 1, 17), OP.subtract)
-        act(V("dsb"), G(V("ds"), L(LO, 16)))
-        act(col("dca", 15), col("vs", 1), AF.Identity, -1.0, col("own", 15))
+        scan(V("ef", 128, 240), V("mk", 128, 240), V("dbp"))
+        scan(V("ef", 0, 16), V("mk", 240, 256), V("wd", 32, 48))
+        dca = V("dca", 16 * last, 16 * last + 16)
+        act(col("dca", 16 * last + 15), col("ef", 15), AF.Identity, -1.0, col("pf", 9 + last))
         if not last:
             act(last16("aa"), V("pwd"))
         act(V("ki", 72, 128, 8), V(ct, 128, 135))
         tt(V("qq"), G(V(ct, 128, 144), L(LTR, 8)), V(ct, 0, 128), OP.not_equal)
-        ops[-1]["r"] += [V("inv"), V("dsb")] + ([V("fp")] if early and not last else [])
+        ops[-1]["r"] += [V("inv"), V("ef", 128, 240), V("sti"), V("sto", 0, 112)] if HINT else []
         scan(V("rq", 0, 128), V("qq"), V("ki", 0, 128))
         cuts = [(16 * lo, 16 * hi) for lo, hi in (TWO if CSPLIT & 4 else ONE)]
         for lo, hi in cuts:
@@ -485,20 +524,29 @@ def program(CYC, SLOW, PICK):
             ts(V("mm", lo, hi), V("mg", lo, hi), ROUGH, OP.add, ROUGH, OP.is_equal)
         act(col("ma", 32), col(ct, 128), AF.Relu, 1.0, -2.0)
         ts(V("ma", 0, 16), en, -2.0, OP.add, col("ma", 32), OP.not_equal)
-        scan(V("ma", 16, 32), V("ma", 0, 16), V("dca"))
-        act(V("dsb", 0, 256, 16), z(16), AF.Identity, 1.0, col("ma", 31))
-        for lo, hi in cuts:
-            scan(V("sr", lo, hi), V("mm", lo, hi), V("dsb", lo, hi))
+        scan(V("dsx", 1, 17), V("ma", 0, 16), dca)
+        act(last16("dnb", 0, 112), V(ct, 87, 136, 8), AF.Identity, TAKE, col("pe", 15))
+        tt(V("mo"), G(V(ct, 128, 144), L(LMO, 7)), V("sto", 0, 112), OP.not_equal)
+        scan(V("ef", 16, 128), V("mo"), V("dnb"))
+        tt(V("dsx", 17, 32), last16("ef", 0, 240), last16("ef", 16, 240), OP.subtract)
+        act(V("dsb"), G(V("dsx", 16, 32), L(LO, 8)))
+        for lo, hi in ((0, 128), (128, 256)):
+            scan(V("sr", lo, hi), V("mm", lo, hi), V("dsb"))
         for lo, hi in (TWO if CSPLIT & 16 else ONE):
-            ts(V("sl", lo, hi), last16("sr", 16 * lo, 16 * (hi - lo)), 1 / COL, OP.mult)
+            ts(V("sl", lo, hi), last16("sr", 16 * lo, 16 * (hi - lo)), 1 / TAKE, OP.mult)
         for b in range(4):
-            mx(bank(b, 128), eq(b)[0], eq(b)[1], made[0], made[1])
-            act(V("fw", 384 * b + 256, 384 * b + 368), bank(b, 112))
-        for b in range(4):
-            for lo, hi in (TWO if CSPLIT & 16 and b == 0 else ONE):
-                (cp if b == 0 and lo == 0 and (last or HN0) else act)(V("hn", 256 * b + 16 * lo, 256 * b + 16 * hi), G(V("fw", 384 * b, 384 * b + 368), V("sl", lo, hi)))
-            for lo, hi in (((0, 128), (128, 256)) if b >= (ZLAST if last else ZSPLIT) else ((0, 256),)):
-                tt(V("zt", 4 * lo + b, 4 * hi, 4), G(V("hn", 256 * b, 256 * b + 256), V("inv", lo // 16, hi // 16)), V("fw", 384 * b + lo, 384 * b + hi), OP.add)
+            for lo, hi in (TWO if b in FIRST else ONE):
+                out, src = V("hn", 256 * b + 16 * lo, 256 * b + 16 * hi), G(V("fw", 512 * b, 512 * b + 512), V("sl", lo, hi))
+                if b in BYNODE:
+                    tt(out, src, V("fn", 256 * b + 16 * lo, 256 * b + 16 * hi), OP.add)
+                else:
+                    act(out, src)
+            for lo, hi in (((0, 128), (128, 256)) if b in (ZLAST if last else ZSPLIT) else ((0, 256),)):
+                out, src = V("zt", 4 * lo + b, 4 * hi, 4), G(V("hn", 256 * b, 256 * b + 256), V("inv", lo // 16, hi // 16))
+                if b in BYNODE:
+                    act(out, src)
+                else:
+                    tt(out, src, V("fw", 512 * b + lo, 512 * b + hi), OP.add)
                 if not MERGE & 1:
                     act(V("z32", 4 * lo + b, 4 * hi, 4), V("zt", 4 * lo + b, 4 * hi, 4), AF.Copy, 32.0)
         for h, (lo, hi) in enumerate(((0, 128), (128, 256)) if HALVES else ((0, 256),)):
@@ -514,24 +562,19 @@ def program(CYC, SLOW, PICK):
                     (act if b < 3 or h == 0 else vact)(V("xt", 4 * lo + b, 4 * hi, 4), x32, AF.Copy, 0.03125)
             if MERGE & (2 << h):
                 (vact if h else act)(V("xt", 4 * lo, 4 * hi), V("x32", 4 * lo, 4 * hi), AF.Copy, 0.03125)
-        tt(V("mo"), G(V(ct, 128, 144), L(LMO, 8)), V("sto"), OP.not_equal)
-        scan(V("mp"), V("mo"), V("dnb"))
-        act(V("vp", 1, 9), last16("mp", 0, 128))
-        tt(V("dp"), V("vp", 0, 16), V("vp", 1, 17), OP.subtract)
-        act(V("dpb"), G(V("dp"), L(LO, 16)))
+        whole(V("ex", 0, 16), last16("sr"), COL)
+        tt(V("lk"), last16("sr"), V("ex", 0, 16), OP.subtract)
         if last:
-            scan(V("ma", 48, 64), V("ma", 0, 16), V("dnb", 0, 16))
-            ts(V("dpb", 0, 256, 16), z(16), col("ma", 63), OP.add, col("vp", 1), OP.subtract)
-        else:
-            act(last16("dpb"), V("pw2"), AF.Identity, 1.0, col("vp", 15))
-        scan(V("ep"), V("mm"), V("dpb"))
-        if last:
-            act(V("lk"), last16("ep"), AF.Copy, 1 / PTR)
             store("s", "op", V("lk"))
         else:
-            act(V("cu", 0, 16), last16("ep"))
-            ts(V("p0"), last16("ep"), 1 / PTR, OP.mult)
-            ancestors("p0", TWO if ASPLIT & 2 else ONE)
+            cp(V("p0"), V("lk"))
+            tt(V("cu", 0, 16), V("lk"), V("pp", 0, 16), OP.add)
+            whole(V("ex", 16, 32), last16("sr"), TAKE)
+            tt(V("ex", 32, 48), last16("sr"), V("ex", 16, 32), OP.subtract)
+            tt(V("df", 0, 16), pk, V("ex", 32, 48), OP.subtract)
+            if DIRECT:
+                beside(V("lk"))
+            ancestors(PTR, TWO if ASPLIT & 2 else ONE, PLAIN & 2)
     state_product(V("qv"), V("sv"))
     for h in range(2):
         store("s", "oc", V("qx", 128 * h, 128 * h + 128))
@@ -619,16 +662,16 @@ def order(ops):
         for c in rd:
             readers.setdefault(c, set()).add(n)
         deps.discard(n)
-        o["deps"] = deps
+        o["deps"] = deps | ({o["behind"]} if "behind" in o else set())
     above = []
     for n, o in enumerate(ops):
         far = 0
         for d in o["deps"]:
             far |= above[d]
         o["near"] = sorted(d for d in o["deps"] if not far >> d & 1)
-        above.append(far | sum(1 << d for d in o["deps"]))
+        above.append(far | sum(1 << d for d in o["deps"] - {o.get("behind")}))
     timed = [program(pace[0], pace[3], pace[4]) for pace in PACES]
-    flat = [[(QUEUES.index(o["q"]), t["cost"] + ISSUE, o["late"], [(d, ops[d]["late"] + lag) for d in o["near"]], wake) for o, t in zip(ops, same)]
+    flat = [[(QUEUES.index(o["q"]), t["cost"] + ISSUE, o["late"], [(d, 0.0 if d == o.get("behind") else ops[d]["late"] + lag) for d in o["near"]], wake) for o, t in zip(ops, same)]
             for same, (cycle, lag, wake, slow, pick) in zip(timed, PACES)]
     spare = [{n: (QUEUES.index(t["other"][0]), t["other"][3] + ISSUE) + table[n][2:] for n, t in enumerate(same) if "other" in t} for same, table in zip(timed, flat)]
 
@@ -645,40 +688,71 @@ def order(ops):
         for d, lag in flat[0][n][3]:
             tail[d] = max(tail[d], ops[d]["cost"] + lag + tail[n])
             users[d].append(n)
-    best = None
-    for patience, grain in PLANS:
-        noise = np.random.default_rng(grain).random(len(ops)).tolist()
-        weight = [t + (300.0 * e if grain else 0.0) for t, e in zip(tail, noise)]
-        left = [len(o["near"]) for o in ops]
-        ready = {n: 0.0 for n in range(len(ops)) if left[n] == 0}
-        free = {q: 0.0 for q in QUEUES}
-        end, seq = {}, []
-        while ready:
-            first = min(ready, key=lambda n: (max(ready[n], free[ops[n]["q"]]), n))
-            q = ops[first]["q"]
-            t = max(ready[first], free[q])
-            n, limit = None, None
-            for m in sorted([m for m in ready if ops[m]["q"] == q], key=lambda m: (-weight[m], m)):
-                if limit is None or max(ready[m], t) + ops[m]["cost"] <= limit:
-                    if ready[m] <= t:
-                        n = m
-                        break
-                    n = m if n is None or ready[m] < ready[n] else n
-                limit = ready[m] + patience if limit is None else min(limit, max(ready[m], t) + patience)
-            if ready[n] > t:
-                others = [max(ready[m], free[ops[m]["q"]]) for m in ready if ops[m]["q"] != q]
-                if others and min(others) < ready[n]:
-                    free[q] = min(others) + 1.0
-                    continue
-            end[n] = free[q] = max(ready.pop(n), free[q]) + ops[n]["cost"]
-            seq.append(n)
-            for m in users[n]:
-                left[m] -= 1
-                if left[m] == 0:
-                    ready[m] = max(end[d] + lag for d, lag in flat[0][m][3])
-        total = score(seq)
-        if best is None or total < best[0]:
-            best = (total, seq)
+    def queues(want):
+        for n, q in enumerate(want):
+            if ops[n]["q"] != q:
+                swap(n)
+
+    def lay(turns, forms, before, first):
+        starts, ends = [[] for q in QUEUES], [[] for q in QUEUES]
+        end, start, where = [0.0] * len(ops), [0.0] * len(ops), [0] * len(ops)
+        for n in turns:
+            ready = first[n]
+            for d, lag in before[n]:
+                if end[d] + lag > ready:
+                    ready = end[d] + lag
+            found = None
+            for q, cost, toll in forms[n]:
+                s, e, t = starts[q], ends[q], ready
+                i = len(e)
+                while i and e[i - 1] > t:
+                    i -= 1
+                while i < len(s) and s[i] < t + cost - 1e-6:
+                    t = max(t, e[i])
+                    i += 1
+                if found is None or t + cost + toll < found[0]:
+                    found = (t + cost + toll, q, i, t, cost)
+            key, q, i, t, cost = found
+            starts[q].insert(i, t)
+            ends[q].insert(i, t + cost)
+            start[n], end[n], where[n] = t, t + cost, q
+        return start, end, where
+
+    def turns_by(key, before, after):
+        key = list(key)
+        for n in (range(len(ops)) if before is ahead else range(len(ops) - 1, -1, -1)):
+            for d, lag in before[n]:
+                if key[d] >= key[n]:
+                    key[n] = key[d] + 1e-3
+        return sorted(range(len(ops)), key=lambda n: key[n])
+
+    best, rng = None, np.random.default_rng(0)
+    both = [[(table[n][:2],) + ((rest[n][:2],) if n in rest else ()) for n in range(len(ops))] for table, rest in zip(flat, spare)]
+    late, zero = [o["late"] for o in ops], [0.0] * len(ops)
+    for plan in range(PLANS):
+        pace = plan % len(flat)
+        ahead = [flat[pace][n][3] for n in range(len(ops))]
+        behind = [[] for o in ops]
+        for n in range(len(ops)):
+            for d, lag in ahead[n]:
+                behind[d].append((n, lag))
+        toll, grain = rng.random(2).tolist()
+        forms = [[(q, c, TOLL * toll * c * e if q == 0 else 0.0) for q, c in f] for f, e in zip(both[pace], (0.5 + rng.random(len(ops))).tolist())]
+        if best is None or plan % 4 == 0:
+            key = [-t for t in tail]
+        else:
+            key = best[3]
+        key = [k + GRAIN * grain * e for k, e in zip(key, rng.random(len(ops)).tolist())]
+        for sweep in range(SWEEPS):
+            start, end, where = lay(turns_by(key, ahead, behind), forms, ahead, zero)
+            queues([QUEUES[q] for q in where])
+            seq = sorted(range(len(ops)), key=lambda n: (start[n], n))
+            total = score(seq)
+            if best is None or total < best[0]:
+                best = (total, seq, [QUEUES[q] for q in where], start)
+            start, end, where = lay(turns_by([-e for e in end], behind, ahead), forms, behind, late)
+            key = [-e for e in end]
+    best = best[:3]
     def improve(seq, seed, moves, span):
         taken, pool = 0, seq[max(span[0], 0):span[1]]
         free = set(pool)
@@ -717,12 +791,90 @@ def order(ops):
                 swap(n)
         return seq
 
-    def queues(want):
-        for n, q in enumerate(want):
-            if ops[n]["q"] != q:
+    def rebuild(seq, seed, rounds):
+        stale = True
+        for turn, (a, b, c, e, f) in enumerate(np.random.default_rng(seed).random((rounds, 5)).tolist()):
+            if stale:
+                runs = [replay(t, seq) for t in flat]
+                seq.sort(key=lambda m: runs[0][1][m] - flat[0][m][1])
+                rests = []
+                for table in flat:
+                    rest, nxt = [0.0] * len(ops), [0.0] * len(QUEUES)
+                    for n in reversed(seq):
+                        q, cost, late, deps, wake = table[n]
+                        t = rest[n] = nxt[q] = max(rest[n], nxt[q], late) + cost
+                        for d, lag in deps:
+                            if rest[d] < t + lag:
+                                rest[d] = t + lag
+                    rests.append(rest)
+                stale = False
+            pace = turn % len(flat)
+            table, end, rest = flat[pace], runs[pace][1][:], rests[pace]
+            size = 12 + int(b * SPAN)
+            lo = int(a * (len(seq) - size))
+            part = seq[lo:lo + size]
+            inside = set(part)
+            free, after = [0.0] * len(QUEUES), [None] * len(QUEUES)
+            for n in seq[max(lo - 60, 0):lo]:
+                free[table[n][0]] = end[n]
+            for n in seq[lo + size:lo + size + 80]:
+                if after[table[n][0]] is None:
+                    after[table[n][0]] = rest[n]
+            noise = np.random.default_rng(seed * rounds + turn).random(2 * size).tolist()
+            chain = {}
+            for i, n in enumerate(sorted(part, reverse=True)):
+                t = max(table[n][2], after[table[n][0]] or 0.0)
+                for m in users[n]:
+                    lag = links[pace][n, m]
+                    t = max(t, (chain[m] if m in inside else rest[m]) + lag)
+                chain[n] = t + table[n][1]
+            key = {n: GRAIN * c * r - chain[n] for n, r in zip(part, noise)}
+            for n in sorted(part):
+                for d, lag in table[n][3]:
+                    if d in inside and key[d] >= key[n]:
+                        key[n] = key[d] + 1e-3
+            starts, ends, start, turned = [[] for q in QUEUES], [[] for q in QUEUES], {}, []
+            for n, r in zip(sorted(part, key=key.get), noise[size:]):
+                ready, found = 0.0, None
+                for d, lag in table[n][3]:
+                    if end[d] + lag > ready:
+                        ready = end[d] + lag
+                for q, cost in both[pace][n]:
+                    s, u, t = starts[q], ends[q], max(ready, free[q])
+                    i = len(u)
+                    while i and u[i - 1] > t:
+                        i -= 1
+                    while i < len(s) and s[i] < t + cost - 1e-6:
+                        t = max(t, u[i])
+                        i += 1
+                    mark = t + cost + (TOLL * e * cost * r if q == 0 else 0.0) + (STAY * f if q != table[n][0] else 0.0)
+                    if found is None or mark < found[0]:
+                        found = (mark, q, i, t, cost)
+                mark, q, i, t, cost = found
+                starts[q].insert(i, t)
+                ends[q].insert(i, t + cost)
+                start[n], end[n] = t, t + cost
+                if q != table[n][0]:
+                    turned.append(n)
+            new = seq[:lo] + sorted(part, key=lambda n: (start[n], n)) + seq[lo + size:]
+            if new == seq and not turned:
+                continue
+            for n in turned:
                 swap(n)
+            if sum(shift(t, new, run, lo, lo + size)[0] for t, run in zip(flat, runs)) <= LOOSE * (1.0 - turn / rounds) ** 2 * noise[0]:
+                seq, stale = new, True
+            else:
+                for n in turned:
+                    swap(n)
+        return seq
 
-    best += ([o["q"] for o in ops],)
+    links = [{(d, n): lag for n in range(len(ops)) for d, lag in table[n][3]} for table in flat]
+    begin = best
+    for seed in range(1, 1 + STARTS):
+        queues(begin[2])
+        seq = rebuild(list(begin[1]), seed, REBUILDS)
+        if score(seq) < best[0]:
+            best = (score(seq), seq, [o["q"] for o in ops])
     for seed in range(TRIES):
         queues(best[2])
         part = (seed - 1) % STRETCHES * len(ops) // STRETCHES
@@ -741,7 +893,7 @@ def order(ops):
         o = ops[n]
         k = known[o["q"]]
         need = {}
-        for d in o["deps"]:
+        for d in o["deps"] - {o.get("behind")}:
             kind = ops[d]["kind"]
             if kind == "send":
                 side = "out" if any(cells(ops[d]["r"][0]) & cells(v) for v in o["w"]) else "in"
@@ -798,11 +950,11 @@ def rank_program(g, core, T, topo):
         o = OPS[n]
         e, kind, a = eng[o["q"]], o["kind"], o["args"]
         for d, left in o["waits"]:
-            e.wait_ge(T.sem["left%d" % OPS[d]["args"][0] if left else mark[d][0]], mark[d][1])
+            e.wait_ge(T.sem[("left" if left else "") + mark[d][0]], mark[d][1])
         if kind == "send":
             r, sem, out, src = a
             rid, pid, sengine = topo.addr(partner[r])
-            local = "left%d" % r if sem == "av" else "sent"
+            local = "sent" if sem == "aw" else "left%s%d" % (sem, r)
             lanes = len(topo.engines(core, partner[r]))
             g.remote_dma(raw(out), raw(src), T.sem["%s%d" % (sem, r)], T.sem[local], pid, rid, topo.mask(core, partner[r]))
             sent[local] = sent.get(local, 0) + lanes
@@ -854,7 +1006,7 @@ def rank_program(g, core, T, topo):
             else:
                 ins = e.iota(ap(a[0]), a[1], a[2], a[3], allow_small_or_imprecise_dtypes=True)
         elif kind == "select":
-            ins = e.affine_select(ap(a[0]), ap(a[0]), a[1], a[2], a[3], a[4], a[5])
+            ins = e.affine_select(ap(a[0]), ap(a[1]), a[2], a[3], a[4], a[5], a[6])
         elif kind == "pickq":
             ins = e.tensor_copy(ap(a[0]).bitcast(dt.uint32), ap(a[1]).bitcast(dt.uint32).indirect(ap(a[2])))
         else:

@@ -9,36 +9,45 @@ BUF = {
     "xt": (B, 1024), "qx": (Q4, 256), "sx": (S1, 256), "ut": (B, 512), "qu0": (Q4, 128), "su0": (S1, 128), "qu": (Q4, 128), "su": (S1, 128),
     "vt": (B, 512), "qv": (Q4, 128), "sv": (S1, 128), "qw": (Q4, 512), "sw": (S1, 512), "ez": (B, 520), "qe": (Q4, 512), "se": (S1, 512),
     "fw": (B, 2048), "ft": (B, 1024), "fn": (B, 1024), "lcol": (U, 16), "hn": (B, 1024), "zt": (B, 1024), "z32": (B, 1024), "x32": (B, 1024), "qz": (Q4, 256), "sz": (S1, 256),
-    "ysb": (F, 256), "qf": (Q4, 256), "sf": (S1, 256),
-    "pi": (I, 8), "pf": (F, 32), "iof": (F, 48), "lc": (U, 200), "la": (I, 96), "lb": (I, 96), "rm": (B, 256), "rh": (B, 256), "ms": (B, 256), "ib": (B, 256),
+    "ysb": (F, 256), "qf": (Q4, 256), "sf": (S1, 256), "fh": (B, 1024), "qh": (Q4, 256), "sh": (S1, 256),
+    "pi": (I, 8), "pf": (F, 32), "iof": (F, 48), "lc": (U, 200), "lf": (F, 200), "la": (I, 96), "lb": (I, 96), "rm": (B, 256), "rh": (B, 256), "ms": (B, 256), "ib": (B, 256),
     "scv": (F, 256), "z16": (F, 16), "pw2": (B, 16), "un": (F, 48), "a2": (B, 256), "aa": (F, 256),
     "ni": (I, 32), "nf": (F, 64), "nt": (F, 64), "t3": (F, 48), "lg1": (U, 16), "lnod": (U, 16), "rr": (F, 256),
     "inv": (U, 16), "pe": (F, 48), "dnb": (F, 112), "dca": (F, 32), "sm": (F, 128), "wd": (F, 48), "dsx": (F, 32), "ex": (F, 64), "pp": (F, 32), "p16": (U, 16),
     "ssb": (F, 256), "g1": (F, 256), "tr": (F, 256), "gb": (F, 256), "c1": (B, 256), "s1": (B, 272), "own": (F, 48), "w": (B, 16),
     "dstb": (B, 256), "sti": (B, 256), "sto": (B, 128), "pr": (B, 256), "bm": (F, 256), "gg": (F, 16),
-    "ai": (F, 256), "c2": (B, 256), "posm": (B, 256), "sp": (B, 256), "df": (F, 32), "fl": (F, 64), "pay": (F, 48), "d3": (F, 48),
+    "ai": (F, 256), "c2": (B, 256), "posm": (B, 256), "sp": (B, 256), "df": (F, 48), "fl": (F, 72), "pay": (F, 56), "d3": (F, 48),
     "dbp": (F, 112), "dbe": (B, 128), "mk": (B, 256), "eb": (B, 400), "dbc": (B, 112), "ef": (F, 256), "dsb": (F, 128),
-    "oq": (B, 64), "ro": (B, 64), "ki": (B, 144), "qq": (B, 128), "rq": (B, 144), "dd": (B, 256), "fi": (B, 256), "ini": (B, 256),
+    "ki": (B, 176), "qq": (B, 176), "rq": (B, 192), "dd": (B, 256), "fi": (B, 256), "ini": (B, 256),
     "mg": (B, 256), "ma": (F, 64), "mm": (B, 256), "sr": (F, 256), "sl": (U, 16), "mo": (B, 112), "dpb": (F, 256),
     "ep": (F, 256), "p0": (U, 16), "p1": (U, 16), "cu": (F, 72), "eight": (B, 64), "hh": (F, 16), "ba": (F, 64), "pwd": (F, 16), "ddb": (F, 256), "hop": (F, 256),
     "w4": (I, 64), "bits": (I, 256), "lk": (F, 16),
 }
+TWICE = 1
+if TWICE:
+    BUF["nf"] = BUF["nt"] = (I, 64)
 for _r in range(ROUNDS):
     BUF["ws%d" % _r] = (B, 64)
-    BUF["ct%d" % _r] = (B, 144)
+    BUF["ct%d" % _r] = (B, 208)
     BUF["pq%d" % _r] = (Q4, 256)
     BUF["pp%d" % _r] = (S1, 256)
 PS = {"pa": 2048, "ps": 1024, "pb": 1024}
 HALVES, GSPLIT = 1, 1
 BYNODE, FIRST, ZSPLIT, ZLAST = (2, 3), (0, 2), (0, 1, 2, 3), (0, 1, 2, 3)
 HOME_MADE = ()
-DIRECT, DSPLIT = 1, 0
+BANKS, ROWS, SHORT = 1, 4, 1
+LISTS = ()
+APART = (2,)
+AFTER = ()
+COLS = 0
+DIRECT, DSPLIT = 1, 1
 MASKS, PLAIN, WIDE = 0, 1, 1
 PIECES = (2,)
-NEAR, FAR = 5000.0, 6500.0
-ASPLIT, CSPLIT, MERGE, HINT = 1, 30, 0, 0
+LANDS = (4500.0, 3000.0, 6200.0)
+LOAD, WORD = 1250.0, (750.0, 750.0, 1150.0)
+ASPLIT, CSPLIT, MERGE, HINT = 1, 31, 0, 0
 HOME, _fill = {}, {"shortf": 0, "shortb": 0}
-for _k in ("pf", "sm", "gg", "df", "fl", "pay", "pw2", "pe", "dca", "w", "d3", "ma", "un", "cu", "hh", "ba", "pwd", "oq", "ro", "wd", "dsx", "ex", "pp"):
+for _k in ("pf", "sm", "gg", "df", "fl", "pay", "pw2", "pe", "dca", "w", "d3", "ma", "un", "cu", "hh", "ba", "pwd", "wd", "dsx", "ex", "pp"):
     _h = "shortf" if BUF[_k][0] == F else "shortb"
     HOME[_k] = (_h, _fill[_h])
     _fill[_h] += BUF[_k][1]
@@ -52,9 +61,13 @@ NDMA = 20
 SEMAPHORES = ["q" + q for q in QUEUES] + ["d%d" % i for i in range(NDMA)] + ["sent"] + ["%s%d" % (s, r) for s in ("aw", "av0", "av1", "leftav0", "leftav1") for r in range(ROUNDS)]
 
 ISSUE, START = 0.0, 220.0
-PACES = ((0.87, 195.0, 0.0, 1.2, 1.55), (1.05, 200.0, 0.0, 1.5, 1.25), (1.15, 250.0, 0.0, 1.7, 1.9))
+PACES = ((0.85, 225.0, 0.0, 1.3, 1.55, 1.15), (1.03, 250.0, 0.0, 1.7, 1.3, 0.85), (1.2, 225.0, 0.0, 1.7, 1.9, 1.3))
 PLANS, SWEEPS, TOLL, GRAIN = 30, 4, 2.0, 400.0
-STARTS, REBUILDS, SPAN, LOOSE, STAY = 3, 25000, 25, 900.0, 500.0
+STARTS, REBUILDS, SPAN, LOOSE, STAY = 18, 48000, 25, 900.0, 500.0
+PART, FRESH, LOOSER = 0.15, 6, 300.0
+PULLS, EASE = 100, 100.0
+RUNS, MEND, CUTS = 1, 250, ()
+SOON = (("dstb", ("ez",)),)
 TRIES, STRETCHES = 9, 8
 MOVES, SLACK = 24000, 150.0
 LN2 = math.log(2.0)
@@ -62,7 +75,7 @@ HALF = 32767.5 / 32768
 PTR, LIFT = 2.0 ** 17, 2.0 ** 22
 COL, TAKE = 64.0, 2.0 ** 15
 ROUGH = 1.5 * 2.0 ** 24
-LD, LO, LE, LO16, LA, LB, LU, LT3, LSEL, LS, LOWN, LTR, LMO, LK, LSTI, LTO, LSE = 0, 32, 64, 72, 88, 104, 120, 128, 132, 136, 140, 144, 152, 160, 176, 192, 196
+LD, LO, LO17, LA, LB, LU, LT3, LE, LO16, LS, LTR, LMO, LK, LSTI, LOWN = 0, 32, 48, 64, 80, 96, 104, 112, 120, 136, 140, 152, 160, 176, 192
 
 
 def V(name, lo=0, hi=None, step=1):
@@ -103,10 +116,10 @@ def narrow(*vs):
 
 def real(*vs):
     names = [v[1][0] if v[0] == "@" else v[0] for v in vs]
-    return all(n in PS or BUF[n][0] in (F, B) for n in names)
+    return all(n in PS or BUF[n][0] in (F, B) or n in LISTS for n in names)
 
 
-def program(CYC, SLOW, PICK):
+def program(CYC, SLOW, PICK, WAY):
     ops = []
 
     def add(q, kind, args, reads, writes, cost, late=0.0):
@@ -131,7 +144,7 @@ def program(CYC, SLOW, PICK):
         forms = [("v",) + form + (vcost(n, src, 0.5 if narrow(out, src) else 1),),
                  ("a", "act", (out, src, AF.Copy if bias is None else AF.Identity, scale, bias), acost(n, src))]
         q, kind, args, cost = forms[first == "a"]
-        add(q, kind, args, [src, bias], [out], cost)
+        add(q, kind, args, [src, bias, scale], [out], cost)
         ops[-1]["other"] = forms[first == "v"]
 
     def cp(out, src):
@@ -146,7 +159,7 @@ def program(CYC, SLOW, PICK):
         add("v", "tt", (out, a, b, op), [a, b], [out], vcost(count(out), a, 1 if a[0] in PS else 2))
 
     def ts(out, a, s1, op0, s2=None, op1=None):
-        if real(out, a) and op0 == OP.mult and op1 in (None, OP.add) and not isinstance(s1, tuple):
+        if real(out, a) and op0 == OP.mult and (op1 == OP.add or op1 is None and not isinstance(s1, tuple)):
             return either("v", out, a, s1, s2)
         if real(out, a) and op0 == OP.add and op1 is None:
             return either("v", out, a, 1.0, s1)
@@ -162,7 +175,7 @@ def program(CYC, SLOW, PICK):
         add("v", "fill", (out, c), [], [out], vcost(count(out), out, 0.5 if narrow(out) else 1))
 
     def quant(q, s, src):
-        add("v", "quant", (q, s, src), [src], [q, s], 12 + 0.22 * count(src) * 1.2)
+        add("v", "quant", (q, s, src), [src], [q, s], (12 + 0.22 * count(src)) * CYC / 0.8)
 
     def act(out, src, func=AF.Copy, scale=1.0, bias=None):
         if func in (AF.Copy, AF.Identity):
@@ -179,7 +192,7 @@ def program(CYC, SLOW, PICK):
         add("g", "iota", (out, pattern, base, chan), [], [out], 130 + 2 * count(out) * CYC)
 
     def load(q, out, name, after=()):
-        add(q, "load", (out, name), [name] + list(after), [out], START, 1900.0)
+        add(q, "load", (out, name), [name] + list(after), [out], START, WAY * (LOAD if count(out) <= 16 else 1600.0))
 
     def store(q, name, src, part=None):
         add(q, "store", (name, src, part), [src], [], START, 1800.0 if part is not None else 2000.0)
@@ -202,12 +215,20 @@ def program(CYC, SLOW, PICK):
     z = lambda n: V("z16", 0, n)
     io = lambda n, lo=0: V("iof", lo, lo + n)
 
-    load("s", V("ni", 16, 32), "par")
-    load("a", V("ni", 0, 16), "nod")
+    if TWICE:
+        load("s", V("nf", 32, 48), "par")
+        load("a", V("nf", 48, 64), "par")
+        load("s", V("nf", 0, 16), "nod")
+        ops[-1]["behind"] = 0
+        load("s", V("nf", 16, 32), "nod")
+        ops[-1]["behind"] = len(ops) - 2
+    else:
+        load("s", V("ni", 16, 32), "par")
+        load("a", V("ni", 0, 16), "nod")
+    load("s", V("ut"), "u")
+    ops[-1]["behind"] = len(ops) - 2
     load("s", V("xt"), "x")
-    ops[-1]["behind"] = len(ops) - 3
-    load("a", V("ut"), "u")
-    ops[-1]["behind"] = len(ops) - 3
+    ops[-1]["behind"] = len(ops) - 2
     for out, name in (("qw", "wc"), ("sw", "ws"), ("vt", "v")):
         load("s", V(out), name, (col("xt", 0), col("ut", 0)))
 
@@ -217,18 +238,24 @@ def program(CYC, SLOW, PICK):
     p0 = col("pi", 0)
     for i, (shift, mask) in enumerate(((0, 15), (4, 1), (0, 7), (0, 1), (0, 31), (3, 1))):
         ts(col("pi", 1 + i), p0, shift, OP.logical_shift_right, mask, OP.bitwise_and)
-    cp(V("pf", 0, 6), V("pi", 1, 7))
+    cp(V("pf", 0, 1), V("pi", 1, 2))
+    cp(V("pf", 1, 6), V("pi", 2, 7))
     pq, ph, p8, p2, p32, pe = [col("pf", i) for i in range(6)]
     fill(V("z16"), 0.0)
     iota(V("lb", 0, 64), [[16, 4], [0, 16]], 0, 0)
-    ts(V("lc", LD, LD + 4), V("lb", 0, 32, 8), pq, OP.add)
+    if not TWICE:
+        ts(V("lc", LD, LD + 4), V("lb", 0, 32, 8), pq, OP.add)
     ts(L(LO, 16), z(16), pq, OP.add)
+    if COLS:
+        ts(L(LO17, 7), z(7), pq, OP.add, 17.0, OP.add)
     ts(col("pf", 7), p2, 15.0, OP.mult, pq, OP.add)
     ts(V("lc", LT3, LT3 + 3, 2), V("lb", 0, 33, 32), p32, OP.add)
     ts(L(LT3 + 1, 1), col("pf", 7), ph, OP.add)
     ts(col("pf", 8), pq, 16.0, OP.mult, 15.0, OP.add)
-    ts(L(LE, 8), z(8), col("pf", 8), OP.add)
-    ts(L(LO16, 16), io(16), 16.0, OP.mult, 15.0, OP.add)
+    M = lambda at, n: V("lf", at, at + n)
+    ts(M(LE, 8), z(8), col("pf", 8), OP.add)
+    ts(M(LO16, 16), io(16), 16.0, OP.mult, 15.0, OP.add)
+    cp(L(LE, LS - LE), M(LE, LS - LE))
     ts(col("pf", 11), p2, 16.0, OP.mult)
     iota(V("la", 32, 40), [[32, 4], [0, 2]], 0, 0)
     ts(L(LU, 8), V("la", 32, 40), col("pf", 11), OP.add)
@@ -244,30 +271,35 @@ def program(CYC, SLOW, PICK):
     ts(later, p8, 0.0, OP.is_gt)
     ts(head, p8, 0.0, OP.is_equal, 128.0, OP.mult)
     ts(end, p8, 7.0, OP.is_equal, 112.0, OP.mult)
-    ts(V("sm", 100, 104), V("sm", 96, 100), 16.0, OP.mult, 15.0, OP.add)
-    ts(L(LOWN, 4), V("sm", 100, 104), later, OP.mult, head, OP.add)
-    ts(V("sm", 104, 107), V("sm", 100, 103), 32.0, OP.add, later, OP.mult)
-    ts(L(LS, 3), V("sm", 104, 107), head, OP.add, end, OP.add)
+    ts(V("sm", 100, 103), V("sm", 96, 99), 16.0, OP.mult, 47.0, OP.add)
+    ts(col("sm", 104), head, end, OP.add)
+    ts(M(LS, 3), V("sm", 100, 103), later, OP.mult, col("sm", 104), OP.add)
     ts(col("pf", 15), p8, 16.0, OP.mult, 31.0, OP.add)
-    ts(L(LS + 3, 1), col("pf", 15), end, OP.add)
-    act(col("pf", 24), p8, AF.Identity, 8.0, -72.0)
-    ts(V("sm", 108, 112), V("sm", 96, 100), p8, OP.is_ge, col("pf", 24), OP.mult)
-    ts(V("sm", 112, 116), V("sm", 108, 112), 63.0, OP.add, later, OP.mult)
-    ts(L(LTO, 4), V("sm", 112, 116), 1.0, OP.add)
-    ts(col("pf", 25), head, 9 / 128, OP.mult, p8, OP.add)
-    ts(L(LTR, 4), z(4), col("pf", 25), OP.add, -1.0, OP.add)
-    ts(col("pf", 26), col("pf", 25), -10.0, OP.add)
-    ts(V("sm", 116, 120), V("sm", 96, 100), p8, OP.is_gt, col("pf", 26), OP.mult)
-    ts(L(LTR + 4, 4), V("sm", 116, 120), 9.0, OP.add)
-    cp(L(LMO, 7), io(7))
-    ts(col("pf", 18), pq, 9.0, OP.is_ge, -128.0, OP.mult)
-    ts(col("pf", 27), pq, 8.0, OP.mult, col("pf", 18), OP.add)
-    ts(col("pf", 28), pq, 2.0, OP.is_ge)
-    ts(col("pf", 29), col("pf", 27), -65.0, OP.add, col("pf", 28), OP.mult)
-    ts(L(LK, 16), z(16), col("pf", 29), OP.add, 128.0, OP.add)
+    ts(M(LS + 3, 1), col("pf", 15), end, OP.add)
     ts(col("pf", 20), pq, 0.0, OP.is_gt)
     ts(col("pf", 21), pq, 0.0, OP.is_equal, 16.0, OP.mult)
-    ts(L(LSTI, 16), io(16), col("pf", 20), OP.mult, col("pf", 21), OP.add)
+    ts(col("pf", 22), col("pf", 21), 8.0, OP.mult)
+    ts(M(LOWN, 7), M(LO16, 7), col("pf", 20), OP.mult, col("pf", 22), OP.add)
+    ts(col("pf", 23), pe, 9.0, OP.mult, pq, OP.add)
+    ts(col("pf", 24), col("pf", 21), 9 / 16, OP.mult, -10.0, OP.add)
+    ts(col("pf", 30), col("pf", 23), col("pf", 24), OP.add)
+    ts(col("pf", 31), pq, -8.0, OP.add)
+    ts(V("sm", 108, 115), io(7), col("pf", 31), OP.is_gt, col("pf", 30), OP.mult)
+    ts(M(LTR, 7), V("sm", 108, 115), 9.0, OP.add)
+    ts(col("pf", 25), head, 9 / 128, OP.mult, p8, OP.add)
+    ts(col("pf", 26), col("pf", 25), -10.0, OP.add)
+    ts(V("sm", 116, 120), V("sm", 96, 100), p8, OP.is_gt, col("pf", 26), OP.mult)
+    ts(M(LTR + 7, 4), V("sm", 116, 120), 9.0, OP.add)
+    iota(M(LMO - 1, 9), [[1, 9]], -1, 0)
+    ts(col("sm", 120), pq, 8.0, OP.mult, -240.0, OP.add)
+    ts(col("pf", 18), pq, 9.0, OP.is_ge, col("sm", 120), OP.mult)
+    ts(col("pf", 27), pq, 8.0, OP.mult, col("pf", 18), OP.add)
+    ts(col("pf", 28), pq, 2.0, OP.is_ge)
+    ts(col("sm", 121), col("pf", 27), -65.0, OP.add)
+    ts(col("pf", 29), col("sm", 121), col("pf", 28), OP.mult, 176.0, OP.add)
+    ts(M(LK, 16), z(16), col("pf", 29), OP.add)
+    ts(M(LSTI, 16), io(16), col("pf", 20), OP.mult, col("pf", 21), OP.add)
+    cp(L(LS, LOWN + 7 - LS), M(LS, LOWN + 7 - LS))
     iota(V("la", 48, 64), [[16, 16]], 0, 0)
     ts(col("pf", 6), pq, 16.0, OP.mult)
     ts(L(LA, 16), V("la", 48, 64), col("pf", 6), OP.max, ph, OP.add)
@@ -293,28 +325,36 @@ def program(CYC, SLOW, PICK):
     level(V("ib", 240, 256), 15)
     select(V("ez"), V("ez"), [[1, 520]], OP.is_equal, 0.0, -3, -4)
     iota(V("scv"), [[1, 16], [16, 16]], int(LIFT), 0)
-    for name, c in (("own", 16), ("pay", 33), ("fl", 32), ("cu", 40), ("ef", 255), ("eb", 384), ("rq", 128)) + ((("s1", 271),) if DIRECT else ()):
+    for name, c in (("own", 16), ("pay", 33), ("pay", 50), ("fl", 32), ("cu", 40), ("ef", 255), ("eb", 384), ("rq", 176)) + ((("s1", 271),) if DIRECT else ()):
         level(col(name, c), 0)
-    for name, n in (("ki", 128), ("ini", 256)):
+    for name, n in (("ki", 176), ("ini", 256)):
         level(V(name, 0, n), 0)
-    level(col("ki", 64), 99)
     level(V("eb", 128, 144), 0)
     for r in range(ROUNDS):
-        iota(V("ct%d" % r, 136, 144), [[-1, 8]], 0, 0)
-        level(V("ct%d" % r, 64, 80), 0)
+        iota(V("ct%d" % r, 184, 192), [[-1, 8]], 0, 0)
+        level(V("ct%d" % r, 112, 128), 0)
     for b in range(4):
         quant(V("qe", 128 * b, 128 * b + 128), V("se", 128 * b, 128 * b + 128), V("ez", 3 - b, 515 - b))
 
-    cp(V("nf"), G(V("ni"), L(LD, 4)))
-    tp(V("nt"), V("nf"))
-    cp(V("t3", 0, 48), G(V("nt"), L(LT3, 3)))
+    if TWICE:
+        for at in (32, 0):
+            tp(V("nt", at, at + 32), V("nf", at, at + 32))
+    else:
+        cp(V("nf"), G(V("ni"), L(LD, 4)))
+        tp(V("nt"), V("nf"))
+    if TWICE:
+        cp(V("t3", 32, 48), G(V("nt", 32, 64), L(LT3, 1)))
+        cp(V("t3", 0, 32), G(V("nt", 0, 32), L(LT3, 2)))
+    else:
+        cp(V("t3", 0, 48), G(V("nt"), L(LT3, 3)))
     par0, colv = V("t3", 32, 48), V("t3", 0, 16)
     en, pk = V("own", 0, 16), V("own", 17, 33)
     cp(V("lg1"), V("t3", 16, 32))
     cp(V("lcol"), colv)
-    ts(V("sm", 0, 16), colv, COL, OP.mult)
-    tt(V("pe", 16, 32), V("sm", 0, 16), io(16), OP.add)
-    act(pk, V("pe", 16, 32))
+    ts(pk if COLS else V("sm", 0, 16), colv, COL, OP.mult)
+    tt(V("pe", 16, 32), pk if COLS else V("sm", 0, 16), io(16), OP.add)
+    if not COLS:
+        act(pk, V("pe", 16, 32))
     tt(V("pe", 0, 15), V("pe", 16, 31), V("pe", 17, 32), OP.subtract)
     act(col("pe", 15), col("pe", 31), AF.Identity, 1.0, 256 * TAKE)
     act(V("dnb"), G(V("pe", 0, 16), L(LO, 7)))
@@ -338,8 +378,8 @@ def program(CYC, SLOW, PICK):
             tt(V("cu", 24, 40), cur, V("pp", 16, 32), OP.subtract)
             act(last16("aa"), cur, AF.Identity, 1.0, col("pf", 16))
 
-    def ancestors(unit, parts, plain):
-        for k in range(4):
+    def ancestors(unit, parts, plain, done=0):
+        for k in range(done, 4):
             for lo, hi in parts:
                 rows = lambda name: V(name, 16 * lo, 16 * hi)
                 src = G(V("cu", 48, 65) if plain else V("cu", 24, 41), V("p1", lo, hi)) if k else G(V("cu", 0, 17), V("p0", lo, hi))
@@ -354,33 +394,53 @@ def program(CYC, SLOW, PICK):
         for j in range(4):
             ts(V("bits", 64 * j, 64 * j + 64), V("w4"), 4 * j + 3 * WIDE, OP.logical_shift_right, 1, OP.bitwise_and)
 
-    cp(V("p0"), G(V("nt"), L(LT3 + 2, 1)))
+    cp(V("p0"), G(V("nt", 32, 64), L(LT3, 1)))
     ONE, TWO = ((0, 16),), ((0, 8), (8, 16))
     for lo, hi in (TWO if ASPLIT & 1 else ONE):
         (act if lo == 0 else vact)(V("dstb", 16 * lo, 16 * hi), G(par0, V("p0", lo, hi)), AF.Identity, 1.0, 33.0)
     scan(V("sp"), V("dstb"), V("a2"), OP.max, OP.add)
-    tt(V("sm", 16, 32), par0, V("pp", 0, 16), OP.add)
-    act(V("sm", 32, 48), V("sm", 16, 32), AF.Copy, 1 / 16)
     tt(V("ba", 48, 64), par0, io(16), OP.is_lt)
     tt(V("sm", 80, 96), V("ba", 48, 64), io(16, 1), OP.mult)
     tt(V("sm", 48, 64), last16("sp"), V("sm", 80, 96), OP.is_equal)
-    tt(V("cu", 0, 16), V("sm", 32, 48), V("sm", 48, 64), OP.max)
     act(V("w"), par0, AF.Exp, LN2)
-    act(V("hh"), io(16, 32), AF.Copy, PTR)
-    tt(V("ba", 0, 16), V("hh"), V("pw2"), OP.subtract)
-    tt(V("ba", 16, 32), V("ba", 0, 16), V("w"), OP.subtract)
-    tt(V("ba", 32, 48), V("sm", 48, 64), V("ba", 16, 32), OP.mult)
-    tt(last16("aa"), V("pwd"), V("ba", 32, 48), OP.add)
     for j in range(4 * WIDE):
         level(V("eight", 16 * j, 16 * j + 16), 8 >> j)
     if PLAIN:
         level(col("cu", 64), int(16 * PTR))
         act(col("pf", 17), col("un", 15), AF.Identity, LIFT, 1.5 * 2.0 ** 23 * PTR)
-    ancestors(16 * PTR, TWO if ASPLIT & 1 else ONE, PLAIN & 1)
+    if SHORT:
+        level(V("ba", 0, 15), -1)
+        level(col("ba", 15), 15)
+        tt(V("sm", 16, 32), last16("sp"), V("sm", 80, 96), OP.not_equal)
+        scan(V("sm", 32, 48), V("sm", 16, 32), V("ba", 0, 16))
+        ts(V("sm", 64, 80), par0, col("sm", 47), OP.is_equal, 16 * PTR, OP.mult)
+        act(V("ba", 16, 32), last16("sp"), AF.Identity, PTR, -PTR)
+        tt(V("ba", 32, 48), V("ba", 16, 32), V("w"), OP.add)
+        act(V("ex", 0, 16), V("pw2"), AF.Identity, -1.0, 16 * PTR)
+        tt(V("ex", 16, 32), V("sm", 48, 64), V("ex", 0, 16), OP.mult)
+        tt(V("ex", 32, 48), V("ba", 32, 48), V("ex", 16, 32), OP.max)
+        tt(V("ex", 48, 64), V("ex", 32, 48), V("sm", 64, 80), OP.max)
+        ts(V("p1"), V("ex", 48, 64), 1 / PTR, OP.mult)
+        tt(V("cu", 48, 64), V("ex", 48, 64), V("pw2"), OP.add)
+        ts(V("hh"), V("ex", 48, 64), 1.5 * 2.0 ** 23 * PTR, OP.add, col("pf", 17), OP.subtract)
+        tt(last16("aa"), V("cu", 48, 64), V("hh"), OP.subtract)
+    else:
+        tt(V("sm", 16, 32), par0, V("pp", 0, 16), OP.add)
+        act(V("sm", 32, 48), V("sm", 16, 32), AF.Copy, 1 / 16)
+        tt(V("cu", 0, 16), V("sm", 32, 48), V("sm", 48, 64), OP.max)
+        act(V("hh"), io(16, 32), AF.Copy, PTR)
+        tt(V("ba", 0, 16), V("hh"), V("pw2"), OP.subtract)
+        tt(V("ba", 16, 32), V("ba", 0, 16), V("w"), OP.subtract)
+        tt(V("ba", 32, 48), V("sm", 48, 64), V("ba", 16, 32), OP.mult)
+        tt(last16("aa"), V("pwd"), V("ba", 32, 48), OP.add)
+    ancestors(16 * PTR, TWO if ASPLIT & 1 else ONE, PLAIN & 1, SHORT)
     act(V("dpb"), G(V("pe", 16, 32), V("p0")), AF.Identity, 1.0, LIFT)
     act(last16("aa"), z(16), AF.Identity, 1.0, col("pf", 16))
     scan(V("ep"), V("dpb"), V("aa"), OP.max, OP.add)
-    tt(V("df", 0, 16), pk, last16("ep"), OP.subtract)
+    tt(V("df", 0, 16), V("pe", 16, 32), last16("ep"), OP.subtract)
+    if COLS:
+        tt(V("df", 32, 48), io(16), par0, OP.subtract)
+        tt(V("df", 0, 16), V("df", 0, 16), V("df", 32, 48), OP.subtract)
 
     def beside(link):
         ts(V("p16"), link, 16.0, OP.mult, 15.0, OP.add)
@@ -390,13 +450,14 @@ def program(CYC, SLOW, PICK):
         ts(col("pf", 19), col("un", 15), 32.0, OP.mult, -16.0, OP.add)
         beside(par0)
 
-    cp(V("lnod"), V("ni", 0, 16))
+    cp(V("lnod"), V("nf" if TWICE else "ni", 0, 16))
     for lo, hi in TWO:
         cp(G(V("rr"), V("lnod", lo, hi)), V("scv", 16 * lo, 16 * hi))
     scan(V("sr"), V("rr"), V("aa"), OP.max, OP.add)
     cp(V("inv"), last16("sr"))
 
     bank = lambda b, n: V("pa", 512 * b, 512 * b + n)
+    side = lambda b, n: V("pb" if b < 2 else "ps", 512 * (b % 2), 512 * (b % 2) + n)
     eq = lambda b: (V("qe", 128 * b, 128 * b + 128), V("se", 128 * b, 128 * b + 128))
 
     def state_product(lq, ls):
@@ -408,26 +469,28 @@ def program(CYC, SLOW, PICK):
     for r in range(ROUNDS):
         ct, last = "ct%d" % r, r == ROUNDS - 1
         state_product(V("qu"), V("su"))
-        home = r in HOME_MADE
-
         pieces = ((0, 128), (128, 256)) if r in PIECES else ((0, 256),)
+        home = [r in HOME_MADE for k in range(len(pieces))]
+        begins, bulk = len(ops), []
 
-        def cross(q, s):
-            for k, (lo, hi) in enumerate(pieces):
-                late = (FAR if last else NEAR) * (0.6 if hi < 256 else 1.0) - 600.0 * k
-                send(r, "av%d" % k, V("pq%d" % r, lo, hi), V(q, lo, hi), late)
-                ops[-1]["cost"] += 0.0 if r or k else 1500.0
-                if k:
-                    ops[-1]["behind"] = len(ops) - 2
-                send(r, "av%d" % k, V("pp%d" % r, lo, hi), V(s, lo, hi), late)
-                ops[-1]["behind"] = len(ops) - 2
+        def cross(k, q, s):
+            lo, hi = pieces[k]
+            late = LANDS[r] * (0.6 if len(pieces) > 1 else 1.0)
+            send(r, "av%d" % k, V("pq%d" % r, lo, hi), V(q, lo, hi), late)
+            ops[-1]["cost"] += 0.0 if r or k else 1200.0 * SLOW ** 2
+            if k:
+                ops[-1]["behind"] = bulk[0]
+            send(r, "av%d" % k, V("pp%d" % r, lo, hi), V(s, lo, hi), late)
+            ops[-1]["behind"] = len(ops) - 2
+            bulk.append(len(ops) - 1)
 
-        def again():
-            for h in range(2):
-                quant(V("qf", 128 * h, 128 * h + 128), V("sf", 128 * h, 128 * h + 128), V("ft", 512 * h, 512 * h + 512))
+        def again(tile, q, s, lo, hi):
+            for at in range(lo, hi, 128):
+                quant(V(q, at, at + 128), V(s, at, at + 128), V(tile, 4 * at, 4 * at + 512))
 
-        if not home:
-            cross("qx", "sx")
+        for k in range(len(pieces)):
+            if not home[k]:
+                cross(k, "qx", "sx")
         for b in range(4):
             mx(bank(b, 256), eq(b)[0], eq(b)[1], V("qx"), V("sx"))
         for h in range(2):
@@ -447,22 +510,23 @@ def program(CYC, SLOW, PICK):
             act(V("fw", 512 * b, 512 * b + 256), bank(b, 256))
         for b in BYNODE:
             act(V("fn", 256 * b, 256 * b + 256), G(V("fw", 512 * b, 512 * b + 256), V("lcol")))
-        made = "pq%d" % r, "pp%d" % r
-        if home:
-            for b in range(4):
-                vact(V("ft", b, 1024, 4), V("fw", 512 * b, 512 * b + 256), AF.Copy, 2.0)
-            again()
-            cross("qf", "sf")
-        else:
-            for lo, hi in pieces:
+        for k, (lo, hi) in enumerate(pieces):
+            made = "pq%d" % r, "pp%d" % r
+            if home[k]:
                 for b in range(4):
-                    mx(bank(b, hi - lo), eq(b)[0], eq(b)[1], V(made[0], lo, hi), V(made[1], lo, hi))
-                    act(V("ft", 4 * lo + b, 4 * hi, 4), bank(b, hi - lo), AF.Copy, 2.0)
-            again()
-            made = "qf", "sf"
-        for lo, hi in pieces:
+                    vact(V("fh", 4 * lo + b, 4 * hi, 4), V("fw", 512 * b + lo, 512 * b + hi), AF.Copy, 2.0)
+                again("fh", "qh", "sh", lo, hi)
+                cross(k, "qh", "sh")
+            else:
+                for b in range(4):
+                    out = side(b, hi - lo) if BANKS & 1 << k else bank(b, hi - lo)
+                    mx(out, eq(b)[0], eq(b)[1], V(made[0], lo, hi), V(made[1], lo, hi))
+                    ops[-1]["also"] = [(bulk[0] - 1, LANDS[r])] * k
+                    act(V("ft", 4 * lo + b, 4 * hi, 4), out, AF.Copy, 2.0)
+                again("ft", "qf", "sf", lo, hi)
+                made = "qf", "sf"
             for b in range(4):
-                out = V("pb", 512 * (b % 2), 512 * (b % 2) + hi - lo) if lo == 0 and hi < 256 else bank(b, hi - lo)
+                out = side(b, hi - lo) if BANKS & 4 << k else bank(b, hi - lo)
                 mx(out, eq(b)[0], eq(b)[1], V(made[0], lo, hi), V(made[1], lo, hi))
                 act(V("fw", 512 * b + 256 + lo, 512 * b + 256 + hi), out)
         act(V("w"), last16("s1"), AF.Exp, LN2)
@@ -486,52 +550,59 @@ def program(CYC, SLOW, PICK):
         tt(V("pay", 0, 33), V("own", 0, 33), V("fl", 16, 49), OP.subtract)
         tt(V("d3", 0, 33), V("pay", 0, 33), V("pay", 1, 34), OP.subtract)
         act(V("dbe"), G(V("d3", 0, 16), L(LO, 8)))
-        whole(V("wd", 0, 16), V("d3", 17, 33), COL)
-        act(V("dbc"), G(V("wd", 0, 16), L(LO, 7)), AF.Copy, 1 / COL)
-        act(V("wd", 16, 32), V("wd", 0, 16), AF.Copy, TAKE / COL)
-        tt(V("wd", 32, 48), V("wd", 16, 32), V("d3", 17, 33), OP.add)
+        if COLS:
+            act(V("dbc"), G(V("d3", 0, 40), L(LO17, 7)), AF.Copy, 1 / COL)
+            tt(V("fl", 50, 66), V("df", 32, 48), V("fl", 0, 16), OP.mult)
+            tt(V("pay", 34, 50), io(16), V("fl", 50, 66), OP.subtract)
+            tt(V("wd", 0, 16), V("pay", 34, 50), V("pay", 35, 51), OP.subtract)
+            act(V("wd", 16, 32), V("d3", 17, 33), AF.Copy, TAKE / COL + 1)
+            tt(V("wd", 32, 48), V("wd", 16, 32), V("wd", 0, 16), OP.add)
+        else:
+            whole(V("wd", 0, 16), V("d3", 17, 33), COL)
+            act(V("dbc"), G(V("wd", 0, 16), L(LO, 7)), AF.Copy, 1 / COL)
+            act(V("wd", 16, 32), V("wd", 0, 16), AF.Copy, TAKE / COL)
+            tt(V("wd", 32, 48), V("wd", 16, 32), V("d3", 17, 33), OP.add)
         act(V("dbp"), G(V("wd", 32, 48), L(LO, 7)))
         tt(V("mk", 16, 128), G(V("posm"), L(LE, 7)), V("ib", 16, 128), OP.not_equal)
         scan(V("eb", 16, 128), V("mk", 16, 128), V("dbe", 0, 112))
         scan(V("eb", 144, 256), V("mk", 16, 128), V("dbc"))
         cp(V("ws%d" % r), G(V("eb", 0, 256), L(LS, 4)))
-        send(r, "aw", V(ct, 80, 136), V("ws%d" % r, 0, 56), 1900.0 if last else 1600.0)
+        send(r, "aw", V(ct, 128, 184), V("ws%d" % r, 0, 56), WAY * WORD[r])
+        ops[-1]["also"] = [(bulk[-1], 0.0), (bulk[0] - 1, LANDS[r] / 2)] if r in APART else [(bulk[-1], ops[bulk[-1]]["late"]), (bulk[0] - 1, LANDS[r])]
         act(V("sto", 0, 112), G(en, L(LO, 7)))
         act(V("sti"), G(V("own", 0, 17), L(LSTI, 16)))
         act(V("ini", 0, 256, 16), en, AF.Exp, 2 * LN2, -LN2)
         tt(V("mk", 128, 256), G(V("posm"), L(LE, 8)), V("ib", 128, 256), OP.not_equal)
         scan(V("eb", 256, 384), V("mk", 128, 256), V("dbe"))
-        act(V(ct, 0, 64), G(V("eb", 256, 385), L(LOWN, 4)))
-        act(V("ki", 0, 64, 8), last16("eb", 256, 128))
-        tt(V("oq"), G(V("ki", 0, 65), L(LTO, 4)), V(ct, 0, 64), OP.not_equal)
-        scan(V("ro"), V("oq"), V("ki", 0, 64))
-        act(V("ki", 0, 64, 8), V("ro", 7, 64, 8))
+        act(V(ct, 0, 112), G(V("eb", 256, 385), L(LOWN, 7)))
+        act(V("ki", 0, 112, 16), last16("eb", 256, 112))
+        act(V(ct, 192, 199), last16("eb", 256, 112))
         scan(V("ef", 128, 240), V("mk", 128, 240), V("dbp"))
         scan(V("ef", 0, 16), V("mk", 240, 256), V("wd", 32, 48))
         dca = V("dca", 16 * last, 16 * last + 16)
         act(col("dca", 16 * last + 15), col("ef", 15), AF.Identity, -1.0, col("pf", 9 + last))
         if not last:
             act(last16("aa"), V("pwd"))
-        act(V("ki", 72, 128, 8), V(ct, 128, 135))
-        tt(V("qq"), G(V(ct, 128, 144), L(LTR, 8)), V(ct, 0, 128), OP.not_equal)
+        act(V("ki", 120, 176, 8), V(ct, 176, 183))
+        tt(V("qq"), G(V(ct, 176, 199), L(LTR, 11)), V(ct, 0, 176), OP.not_equal)
         ops[-1]["r"] += [V("inv"), V("ef", 128, 240), V("sti"), V("sto", 0, 112)] if HINT else []
-        scan(V("rq", 0, 128), V("qq"), V("ki", 0, 128))
+        scan(V("rq", 0, 176), V("qq"), V("ki"))
         cuts = [(16 * lo, 16 * hi) for lo, hi in (TWO if CSPLIT & 4 else ONE)]
         for lo, hi in cuts:
-            tt(V("dd", lo, hi), G(V("rq", 0, 129), L(LK, (hi - lo) // 16)), V("sti", lo, hi), OP.subtract)
+            tt(V("dd", lo, hi), G(V("rq", 0, 177), L(LK, (hi - lo) // 16)), V("sti", lo, hi), OP.subtract)
             ts(V("fi", lo, hi), V("dd", lo, hi), 1.0, OP.min, -0.25, OP.max)
             scan(V("mg", lo, hi), V("fi", lo, hi), V("ini", lo, hi))
             ts(V("mm", lo, hi), V("mg", lo, hi), ROUGH, OP.add, ROUGH, OP.is_equal)
-        act(col("ma", 32), col(ct, 128), AF.Relu, 1.0, -2.0)
+        act(col("ma", 32), col(ct, 176), AF.Relu, 1.0, -2.0)
         ts(V("ma", 0, 16), en, -2.0, OP.add, col("ma", 32), OP.not_equal)
         scan(V("dsx", 1, 17), V("ma", 0, 16), dca)
-        act(last16("dnb", 0, 112), V(ct, 87, 136, 8), AF.Identity, TAKE, col("pe", 15))
-        tt(V("mo"), G(V(ct, 128, 144), L(LMO, 7)), V("sto", 0, 112), OP.not_equal)
+        act(last16("dnb", 0, 112), V(ct, 135, 184, 8), AF.Identity, TAKE, col("pe", 15))
+        tt(V("mo"), G(V(ct, 176, 192), L(LMO, 7)), V("sto", 0, 112), OP.not_equal)
         scan(V("ef", 16, 128), V("mo"), V("dnb"))
         tt(V("dsx", 17, 32), last16("ef", 0, 240), last16("ef", 16, 240), OP.subtract)
-        act(V("dsb"), G(V("dsx", 16, 32), L(LO, 8)))
-        for lo, hi in ((0, 128), (128, 256)):
-            scan(V("sr", lo, hi), V("mm", lo, hi), V("dsb"))
+        act(V("dsb", 0, ROWS * 16), G(V("dsx", 16, 32), L(LO, ROWS)))
+        for lo in range(0, 256, ROWS * 16):
+            scan(V("sr", lo, lo + ROWS * 16), V("mm", lo, lo + ROWS * 16), V("dsb", 0, ROWS * 16))
         for lo, hi in (TWO if CSPLIT & 16 else ONE):
             ts(V("sl", lo, hi), last16("sr", 16 * lo, 16 * (hi - lo)), 1 / TAKE, OP.mult)
         for b in range(4):
@@ -570,18 +641,26 @@ def program(CYC, SLOW, PICK):
             cp(V("p0"), V("lk"))
             tt(V("cu", 0, 16), V("lk"), V("pp", 0, 16), OP.add)
             whole(V("ex", 16, 32), last16("sr"), TAKE)
-            tt(V("ex", 32, 48), last16("sr"), V("ex", 16, 32), OP.subtract)
+            tt(V("ex", 32, 48), V("ex", 0, 16) if COLS else last16("sr"), V("ex", 16, 32), OP.subtract)
             tt(V("df", 0, 16), pk, V("ex", 32, 48), OP.subtract)
+            if COLS:
+                tt(V("df", 32, 48), io(16), V("lk"), OP.subtract)
             if DIRECT:
                 beside(V("lk"))
+            at = len(ops)
             ancestors(PTR, TWO if ASPLIT & 2 else ONE, PLAIN & 2)
+            ops[at]["also"] = [(n, 0.0) for n in range(begins, at) if ops[n]["w"] and ops[n]["w"][0][0] in AFTER]
     state_product(V("qv"), V("sv"))
     for h in range(2):
         store("s", "oc", V("qx", 128 * h, 128 * h + 128))
-        act(V("ysb", 128 * h, 128 * h + 128), V("ps", 512 * h, 512 * h + 128))
+        vact(V("ysb", 128 * h, 128 * h + 128), V("ps", 512 * h, 512 * h + 128))
         store("a", "y", V("ysb", 128 * h, 128 * h + 128))
     for k in range(4):
         store("sa"[k % 2], "osc", V("sx"), k)
+    writes = lambda name, upto: [n for n in range(upto) if ops[n]["w"] and ops[n]["w"][0][0] == name]
+    for then, names in SOON:
+        n = writes(then, len(ops))[0]
+        ops[n]["also"] = ops[n].get("also", []) + [(d, 0.0) for name in names for d in writes(name, n)]
     return ops
 
 
@@ -670,9 +749,9 @@ def order(ops):
             far |= above[d]
         o["near"] = sorted(d for d in o["deps"] if not far >> d & 1)
         above.append(far | sum(1 << d for d in o["deps"] - {o.get("behind")}))
-    timed = [program(pace[0], pace[3], pace[4]) for pace in PACES]
-    flat = [[(QUEUES.index(o["q"]), t["cost"] + ISSUE, o["late"], [(d, 0.0 if d == o.get("behind") else ops[d]["late"] + lag) for d in o["near"]], wake) for o, t in zip(ops, same)]
-            for same, (cycle, lag, wake, slow, pick) in zip(timed, PACES)]
+    timed = [program(pace[0], pace[3], pace[4], pace[5]) for pace in PACES]
+    flat = [[(QUEUES.index(o["q"]), t["cost"] + ISSUE, t["late"], [(d, 0.0 if d == o.get("behind") else same[d]["late"] + lag) for d in o["near"]] + t.get("also", []), wake) for o, t in zip(ops, same)]
+            for same, (cycle, lag, wake, slow, pick, way) in zip(timed, PACES)]
     spare = [{n: (QUEUES.index(t["other"][0]), t["other"][3] + ISSUE) + table[n][2:] for n, t in enumerate(same) if "other" in t} for same, table in zip(timed, flat)]
 
     def swap(n):
@@ -791,8 +870,8 @@ def order(ops):
                 swap(n)
         return seq
 
-    def rebuild(seq, seed, rounds):
-        stale = True
+    def rebuild(seq, seed, rounds, span):
+        stale, taken = True, 0
         for turn, (a, b, c, e, f) in enumerate(np.random.default_rng(seed).random((rounds, 5)).tolist()):
             if stale:
                 runs = [replay(t, seq) for t in flat]
@@ -811,7 +890,7 @@ def order(ops):
             pace = turn % len(flat)
             table, end, rest = flat[pace], runs[pace][1][:], rests[pace]
             size = 12 + int(b * SPAN)
-            lo = int(a * (len(seq) - size))
+            lo = int((span[0] + a * span[1]) * (len(seq) - size))
             part = seq[lo:lo + size]
             inside = set(part)
             free, after = [0.0] * len(QUEUES), [None] * len(QUEUES)
@@ -861,18 +940,77 @@ def order(ops):
                 continue
             for n in turned:
                 swap(n)
-            if sum(shift(t, new, run, lo, lo + size)[0] for t, run in zip(flat, runs)) <= LOOSE * (1.0 - turn / rounds) ** 2 * noise[0]:
-                seq, stale = new, True
+            moved = [shift(t, new, run, lo, lo + size) for t, run in zip(flat, runs)]
+            if sum(m[0] for m in moved) <= (LOOSE if span[1] == 1.0 else LOOSER) * (1.0 - turn / rounds) ** 2 * noise[0]:
+                for by, end, at in moved:
+                    if by:
+                        for m in new[at:]:
+                            end[m] += by
+                seq, runs, taken = new, [(run[0] + m[0], m[1]) for run, m in zip(runs, moved)], taken + 1
+                stale = taken % FRESH == 0
             else:
                 for n in turned:
                     swap(n)
         return seq
 
+    def pull(seq, seed, rounds):
+        total, zero = score(seq), [0.0] * len(ops)
+        for turn, (a, b, c) in enumerate(np.random.default_rng(seed).random((rounds, 3)).tolist()):
+            table = flat[turn % len(flat)]
+            end = replay(table, seq)[1]
+            key = [end[n] - table[n][1] for n in range(len(ops))]
+            first = seq[int(a * a * len(seq))]
+            limit, todo = key[first] - 300.0 - 6000.0 * b * b, [first]
+            while todo:
+                n = todo.pop()
+                if key[n] > limit:
+                    key[n] = limit - 1e-3 * (len(ops) - n)
+                    todo += [d for d, lag in table[n][3]]
+            ahead = [table[n][3] for n in range(len(ops))]
+            for n in range(len(ops)):
+                for d, lag in ahead[n]:
+                    if key[d] >= key[n]:
+                        key[n] = key[d] + 1e-6
+            start = lay(sorted(range(len(ops)), key=lambda n: key[n]), [[table[n][:2] + (0.0,)] for n in range(len(ops))], ahead, zero)[0]
+            new = sorted(range(len(ops)), key=lambda n: (start[n], n))
+            mark = score(new)
+            if mark <= total + EASE * c:
+                seq, total = new, mark
+        return seq
+
     links = [{(d, n): lag for n in range(len(ops)) for d, lag in table[n][3]} for table in flat]
-    begin = best
-    for seed in range(1, 1 + STARTS):
+    def join(a, b, cut):
+        keys = []
+        for run in (a, b):
+            queues(run[2])
+            end = replay(flat[0], run[1])[1]
+            keys.append([end[n] - flat[0][n][1] - end[cut] + flat[0][cut][1] for n in range(len(ops))])
+        early = [k < 0 for k in keys[0]]
+        key = [keys[0][n] if early[n] else max(keys[1][n], 0.0) for n in range(len(ops))]
+        queues([a[2][n] if early[n] else b[2][n] for n in range(len(ops))])
+        for n in range(len(ops)):
+            for d, lag in flat[0][n][3]:
+                if key[d] >= key[n]:
+                    key[n] = key[d] + 1e-6
+        seq = sorted(range(len(ops)), key=lambda n: key[n])
+        at = seq.index(cut) / len(seq)
+        seq = rebuild(seq, cut, MEND, (max(at - 0.04, 0.0), 0.06))
+        return score(seq), seq, [o["q"] for o in ops]
+
+    begin, runs = best, []
+    for seed in range(RUNS):
         queues(begin[2])
-        seq = rebuild(list(begin[1]), seed, REBUILDS)
+        seq = rebuild(list(begin[1]), 100 + seed, REBUILDS, (0.0, 1.0))
+        runs.append((score(seq), seq, [o["q"] for o in ops]))
+    best = min(runs + [best])
+    for cut in [n for n, o in enumerate(ops) if o["w"] and o["w"][0][:2] in CUTS]:
+        for run in runs:
+            best = min(best, join(best, run, cut), join(run, best, cut))
+    for seed in range(1, STARTS):
+        queues(best[2])
+        at = (seed - 1) * 0.382 % 1.0 * (1.0 - PART)
+        seq = pull(list(best[1]), seed, PULLS) if seed % 4 == 1 else list(best[1])
+        seq = rebuild(seq, seed + 1, REBUILDS // (6 if seed else 1), (0.0, 0.999) if seed % 4 == 1 else (at, PART) if seed else (0.0, 1.0))
         if score(seq) < best[0]:
             best = (score(seq), seq, [o["q"] for o in ops])
     for seed in range(TRIES):
@@ -920,7 +1058,7 @@ def order(ops):
     return seq
 
 
-OPS = program(PACES[0][0], PACES[0][3], PACES[0][4])
+OPS = program(PACES[0][0], PACES[0][3], PACES[0][4], PACES[0][5])
 SEQ = order(OPS)
 
 
@@ -955,8 +1093,11 @@ def rank_program(g, core, T, topo):
             r, sem, out, src = a
             rid, pid, sengine = topo.addr(partner[r])
             local = "sent" if sem == "aw" else "left%s%d" % (sem, r)
-            lanes = len(topo.engines(core, partner[r]))
-            g.remote_dma(raw(out), raw(src), T.sem["%s%d" % (sem, r)], T.sem[local], pid, rid, topo.mask(core, partner[r]))
+            use = topo.engines(core, partner[r])
+            if r in APART and sem != "av0":
+                use = use[len(use) // 2:] if sem == "aw" else use[:len(use) // 2]
+            lanes = len(use)
+            g.remote_dma(raw(out), raw(src), T.sem["%s%d" % (sem, r)], T.sem[local], pid, rid, sum(1 << k for k in use))
             sent[local] = sent.get(local, 0) + lanes
             mark[n] = ("%s%d" % (sem, r), lanes * (1 if sem == "aw" else 2))
             continue
@@ -997,7 +1138,7 @@ def rank_program(g, core, T, topo):
             if a[4] is None:
                 ins = e.activation(ap(a[0]), ap(a[1]), a[2], scale=a[3])
             else:
-                ins = e.activation(ap(a[0]), ap(a[1]), a[2], bias=ap(a[4]), scale=a[3])
+                ins = e.activation(ap(a[0]), ap(a[1]), a[2], bias=ap(a[4]), scale=ap(a[3]))
         elif kind == "mx":
             ins = e.matmul_mx(ap(a[0]), ap(a[1]), ap(a[2]), ap(a[3]), ap(a[4]), True, True)
         elif kind == "iota":

import math
import numpy as np
from concourse.mybir import dt, AluOpType as OP, ActivationFunctionType as AF

ROUNDS = 3
F, B, I, U, Q4, S1 = "float32", "bfloat16", "int32", "uint16", "float8_e4m3fn_x4", "uint8"
SIZE = {F: 4, B: 2, I: 4, U: 2, Q4: 4, S1: 1}
BUF = {
    "xt": (B, 1024), "qx": (Q4, 256), "sx": (S1, 256), "ut": (B, 512), "qu0": (Q4, 128), "su0": (S1, 128), "qu": (Q4, 128), "su": (S1, 128),
    "vt": (B, 512), "qv": (Q4, 128), "sv": (S1, 128), "qw": (Q4, 512), "sw": (S1, 512), "ez": (B, 520), "qe": (Q4, 512), "se": (S1, 512),
    "fw": (B, 2048), "ft": (B, 1024), "fn": (B, 1024), "lcol": (U, 16), "hn": (B, 1024), "zt": (B, 1024), "z32": (B, 1024), "x32": (B, 1024), "qz": (Q4, 256), "sz": (S1, 256),
    "ysb": (F, 256), "qf": (Q4, 256), "sf": (S1, 256), "fh": (B, 1024), "qh": (Q4, 256), "sh": (S1, 256),
    "pi": (I, 8), "pf": (F, 32), "iof": (F, 48), "lc": (U, 200), "lf": (F, 200), "la": (I, 96), "lb": (I, 96), "rm": (B, 256), "rh": (B, 256), "ms": (B, 256), "ib": (B, 256),
    "scv": (F, 256), "z16": (F, 16), "pw2": (B, 16), "un": (F, 48), "a2": (B, 256), "aa": (F, 256),
    "ni": (I, 32), "nf": (F, 64), "nt": (F, 64), "t3": (F, 48), "lg1": (U, 16), "lnod": (U, 16), "rr": (F, 256),
    "inv": (U, 16), "pe": (F, 48), "dnb": (F, 112), "dca": (F, 32), "sm": (F, 128), "wd": (F, 48), "dsx": (F, 32), "ex": (F, 64), "pp": (F, 32), "p16": (U, 16),
    "ssb": (F, 256), "g1": (F, 256), "tr": (F, 256), "gb": (F, 256), "c1": (B, 256), "s1": (B, 272), "own": (F, 48), "w": (B, 16),
    "dstb": (B, 256), "sti": (B, 256), "sto": (B, 128), "pr": (B, 256), "bm": (F, 256), "gg": (F, 16),
    "ai": (F, 256), "c2": (B, 256), "posm": (B, 256), "sp": (B, 256), "df": (F, 48), "fl": (F, 72), "pay": (F, 56), "d3": (F, 48),
    "dbp": (F, 112), "dbe": (B, 128), "mk": (B, 256), "eb": (B, 400), "dbc": (B, 112), "ef": (F, 256), "dsb": (F, 128),
    "ki": (B, 176), "qq": (B, 176), "rq": (B, 192), "dd": (B, 256), "fi": (B, 256), "ini": (B, 256),
    "mg": (B, 256), "ma": (F, 64), "mm": (B, 256), "sr": (F, 256), "sl": (U, 16), "mo": (B, 112), "dpb": (F, 256),
    "ep": (F, 256), "p0": (U, 16), "p1": (U, 16), "cu": (F, 72), "eight": (B, 64), "hh": (F, 16), "ba": (F, 64), "pwd": (F, 16), "ddb": (F, 256), "hop": (F, 256),
    "w4": (I, 64), "bits": (I, 256), "lk": (F, 16),
}
TWICE = 1
if TWICE:
    BUF["nf"] = BUF["nt"] = (I, 64)
for _r in range(ROUNDS):
    BUF["ws%d" % _r] = (B, 64)
    BUF["ct%d" % _r] = (B, 208)
    BUF["pq%d" % _r] = (Q4, 256)
    BUF["pp%d" % _r] = (S1, 256)
PS = {"pa": 2048, "ps": 1024, "pb": 1024}
HALVES, GSPLIT = 1, 1
BYNODE, FIRST, ZSPLIT, ZLAST = (2, 3), (0, 2), (0, 1, 2, 3), (0, 1, 2, 3)
HOME_MADE = ()
BANKS, ROWS, SHORT = 1, 4, 1
LISTS = ()
APART = (2,)
AFTER = ()
COLS = 0
DIRECT, DSPLIT = 1, 1
MASKS, PLAIN, WIDE = 0, 1, 1
PIECES = (2,)
LANDS = (4500.0, 3000.0, 6200.0)
LOAD, WORD = 1250.0, (750.0, 750.0, 1150.0)
ASPLIT, CSPLIT, MERGE, HINT = 1, 31, 0, 0
HOME, _fill = {}, {"shortf": 0, "shortb": 0}
for _k in ("pf", "sm", "gg", "df", "fl", "pay", "pw2", "pe", "dca", "w", "d3", "ma", "un", "cu", "hh", "ba", "pwd", "wd", "dsx", "ex", "pp"):
    _h = "shortf" if BUF[_k][0] == F else "shortb"
    HOME[_k] = (_h, _fill[_h])
    _fill[_h] += BUF[_k][1]
SCRATCH = {k: ("sbuf", [128, n], d) for k, (d, n) in BUF.items() if k not in HOME}
SCRATCH["shortf"] = ("sbuf", [128, _fill["shortf"]], F)
SCRATCH["shortb"] = ("sbuf", [128, _fill["shortb"]], B)
for _k, _n in PS.items():
    SCRATCH[_k] = ("psum", [128, _n], F)
QUEUES = ["v", "a", "p", "g", "s"]
NDMA = 20
SEMAPHORES = ["q" + q for q in QUEUES] + ["d%d" % i for i in range(NDMA)] + ["sent"] + ["%s%d" % (s, r) for s in ("aw", "av0", "av1", "leftav0", "leftav1") for r in range(ROUNDS)]

ISSUE, START = 0.0, 220.0
PACES = ((0.85, 225.0, 0.0, 1.3, 1.55, 1.15), (1.03, 250.0, 0.0, 1.7, 1.3, 0.85), (1.2, 225.0, 0.0, 1.7, 1.9, 1.3))
PLANS, SWEEPS, TOLL, GRAIN = 30, 4, 2.0, 400.0
STARTS, REBUILDS, SPAN, LOOSE, STAY = 18, 48000, 25, 900.0, 500.0
PART, FRESH, LOOSER = 0.15, 6, 300.0
PULLS, EASE = 100, 100.0
RUNS, MEND, CUTS = 1, 250, ()
SOON = (("dstb", ("ez",)),)
TRIES, STRETCHES = 9, 8
MOVES, SLACK = 24000, 150.0
LN2 = math.log(2.0)
HALF = 32767.5 / 32768
PTR, LIFT = 2.0 ** 17, 2.0 ** 22
COL, TAKE = 64.0, 2.0 ** 15
ROUGH = 1.5 * 2.0 ** 24
LD, LO, LO17, LA, LB, LU, LT3, LE, LO16, LS, LTR, LMO, LK, LSTI, LOWN = 0, 32, 48, 64, 80, 96, 104, 112, 120, 136, 140, 152, 160, 176, 192


def V(name, lo=0, hi=None, step=1):
    if hi is None:
        hi = (BUF[name][1] if name in BUF else PS[name])
    return (name, lo, hi, step)


def col(name, c):
    return (name, c, c + 1, 1)


def L(at, n):
    return V("lc", at, at + n)


def G(win, off):
    return ("@", win, off)


def count(v):
    if v[0] == "@":
        return 16 * count(v[2])
    return len(range(v[1], v[2], v[3]))


def cells(v):
    if v[0] == "@":
        return cells(v[1]) | cells(v[2])
    if v[0] in PS:
        return {(v[0], c // 512) for c in range(v[1], v[2], v[3])}
    return {(v[0], c) for c in range(v[1], v[2], v[3])}


def narrow(*vs):
    return all(v[0] in BUF and SIZE[BUF[v[0]][0]] == 2 for v in vs)


def real(*vs):
    names = [v[1][0] if v[0] == "@" else v[0] for v in vs]
    return all(n in PS or BUF[n][0] in (F, B) or n in LISTS for n in names)


def program(CYC, SLOW, PICK, WAY):
    ops = []

    def add(q, kind, args, reads, writes, cost, late=0.0):
        ops.append({"q": q, "kind": kind, "args": args, "r": [x for x in reads if isinstance(x, tuple)], "w": writes, "cost": cost, "late": late})

    def vcost(n, src, per):
        if src[0] == "@":
            return 50 + PICK * n * CYC
        return max(64, n * per) * CYC

    def acost(n, src):
        return 65 + PICK * n * CYC if src[0] == "@" else max(64, n) * CYC

    def either(first, out, src, scale=1.0, bias=None):
        n = count(out)
        if scale == 0.0:
            form = ("fill", (out, bias))
        elif bias is None:
            form = ("copy", (out, src)) if scale == 1.0 else ("ts", (out, src, scale, None, OP.mult, None))
        else:
            form = ("ts", (out, src, scale, bias, OP.mult, OP.add))
        forms = [("v",) + form + (vcost(n, src, 0.5 if narrow(out, src) else 1),),
                 ("a", "act", (out, src, AF.Copy if bias is None else AF.Identity, scale, bias), acost(n, src))]
        q, kind, args, cost = forms[first == "a"]
        add(q, kind, args, [src, bias, scale], [out], cost)
        ops[-1]["other"] = forms[first == "v"]

    def cp(out, src):
        if out[0] == "@":
            add("v", "copy", (out, src), [src, out[2]], [out[1]], 50 + 3.0 * count(src) * CYC)
        elif real(out, src):
            either("v", out, src)
        else:
            add("v", "copy", (out, src), [src], [out], vcost(count(out), src, 0.5 if narrow(out, src) else 1))

    def tt(out, a, b, op):
        add("v", "tt", (out, a, b, op), [a, b], [out], vcost(count(out), a, 1 if a[0] in PS else 2))

    def ts(out, a, s1, op0, s2=None, op1=None):
        if real(out, a) and op0 == OP.mult and (op1 == OP.add or op1 is None and not isinstance(s1, tuple)):
            return either("v", out, a, s1, s2)
        if real(out, a) and op0 == OP.add and op1 is None:
            return either("v", out, a, 1.0, s1)
        add("v", "ts", (out, a, s1, s2, op0, op1), [a, s1, s2], [out], vcost(count(out), a, 0.5 if narrow(out, a) else 1))

    def scan(out, d0, d1, op0=OP.mult, op1=OP.add, init=0.0):
        add("v", "scan", (out, d0, d1, init, op0, op1), [d0, d1], [out], vcost(count(out), d0, 0.5 if narrow(out, d0, d1) else 1))

    def tp(out, src):
        add("v", "tp", (out, src), [src], [out], vcost(count(out), src, 0.5 if narrow(out, src) else 1))

    def fill(out, c):
        add("v", "fill", (out, c), [], [out], vcost(count(out), out, 0.5 if narrow(out) else 1))

    def quant(q, s, src):
        add("v", "quant", (q, s, src), [src], [q, s], (12 + 0.22 * count(src)) * CYC / 0.8)

    def act(out, src, func=AF.Copy, scale=1.0, bias=None):
        if func in (AF.Copy, AF.Identity):
            return either("a", out, src, scale, bias)
        add("a", "act", (out, src, func, scale, bias), [src, bias], [out], acost(count(out), src))

    def vact(out, src, func=AF.Copy, scale=1.0, bias=None):
        either("v", out, src, scale, bias)

    def mx(out, lq, ls, rq, rs):
        add("p", "mx", (out, lq, ls, rq, rs), [lq, ls, rq, rs], [out], (count(out) + 16) * CYC * SLOW)

    def iota(out, pattern, base, chan):
        add("g", "iota", (out, pattern, base, chan), [], [out], 130 + 2 * count(out) * CYC)

    def load(q, out, name, after=()):
        add(q, "load", (out, name), [name] + list(after), [out], START, WAY * (LOAD if count(out) <= 16 else 1600.0))

    def store(q, name, src, part=None):
        add(q, "store", (name, src, part), [src], [], START, 1800.0 if part is not None else 2000.0)
        ops[-1]["other"] = ("s" if q == "a" else "a", "store", (name, src, part), START)

    def send(r, sem, out, src, late):
        add("g", "send", (r, sem, out, src), [src], [out], 300, late)

    def whole(out, src, unit):
        ts(out, src, 1.5 * 2.0 ** 23 * unit, OP.add, 1.5 * 2.0 ** 23 * unit, OP.subtract)

    def level(out, c):
        iota(out, [[0, count(out)]], c, 0)
        ops[-1]["other"] = ("v", "fill", (out, float(c)), vcost(count(out), out, 0.5 if narrow(out) else 1))

    def select(out, src, pattern, op, other, base, chan):
        add("g", "select", (out, src, pattern, op, other, base, chan), [src], [out], 170 + 2 * count(out) * CYC)

    last16 = lambda name, lo=0, n=256: V(name, lo + 15, lo + n, 16)
    z = lambda n: V("z16", 0, n)
    io = lambda n, lo=0: V("iof", lo, lo + n)

    if TWICE:
        load("s", V("nf", 32, 48), "par")
        load("a", V("nf", 48, 64), "par")
        load("s", V("nf", 0, 16), "nod")
        ops[-1]["behind"] = 0
        load("s", V("nf", 16, 32), "nod")
        ops[-1]["behind"] = len(ops) - 2
    else:
        load("s", V("ni", 16, 32), "par")
        load("a", V("ni", 0, 16), "nod")
    load("s", V("ut"), "u")
    ops[-1]["behind"] = len(ops) - 2
    load("s", V("xt"), "x")
    ops[-1]["behind"] = len(ops) - 2
    for out, name in (("qw", "wc"), ("sw", "ws"), ("vt", "v")):
        load("s", V(out), name, (col("xt", 0), col("ut", 0)))

    iota(V("pi", 0, 1), [[0, 1]], 0, 1)
    iota(V("iof", 0, 32), [[1, 32]], 0, 0)
    iota(V("iof", 32, 48), [[-1, 16]], 16, 0)
    p0 = col("pi", 0)
    for i, (shift, mask) in enumerate(((0, 15), (4, 1), (0, 7), (0, 1), (0, 31), (3, 1))):
        ts(col("pi", 1 + i), p0, shift, OP.logical_shift_right, mask, OP.bitwise_and)
    cp(V("pf", 0, 1), V("pi", 1, 2))
    cp(V("pf", 1, 6), V("pi", 2, 7))
    pq, ph, p8, p2, p32, pe = [col("pf", i) for i in range(6)]
    fill(V("z16"), 0.0)
    iota(V("lb", 0, 64), [[16, 4], [0, 16]], 0, 0)
    if not TWICE:
        ts(V("lc", LD, LD + 4), V("lb", 0, 32, 8), pq, OP.add)
    ts(L(LO, 16), z(16), pq, OP.add)
    if COLS:
        ts(L(LO17, 7), z(7), pq, OP.add, 17.0, OP.add)
    ts(col("pf", 7), p2, 15.0, OP.mult, pq, OP.add)
    ts(V("lc", LT3, LT3 + 3, 2), V("lb", 0, 33, 32), p32, OP.add)
    ts(L(LT3 + 1, 1), col("pf", 7), ph, OP.add)
    ts(col("pf", 8), pq, 16.0, OP.mult, 15.0, OP.add)
    M = lambda at, n: V("lf", at, at + n)
    ts(M(LE, 8), z(8), col("pf", 8), OP.add)
    ts(M(LO16, 16), io(16), 16.0, OP.mult, 15.0, OP.add)
    cp(L(LE, LS - LE), M(LE, LS - LE))
    ts(col("pf", 11), p2, 16.0, OP.mult)
    iota(V("la", 32, 40), [[32, 4], [0, 2]], 0, 0)
    ts(L(LU, 8), V("la", 32, 40), col("pf", 11), OP.add)
    ts(V("un", 16, 32), io(16), pq, OP.is_equal)
    ts(V("un", 32, 48), io(16, 1), pq, OP.is_equal, -2.0, OP.mult)
    tt(V("un", 0, 15), V("un", 16, 31), V("un", 32, 47), OP.add)
    ts(col("un", 15), pq, 15.0, OP.is_equal, -2.0, OP.add)
    ts(V("a2"), G(V("un", 0, 16), L(LO, 16)), 32.0, OP.mult)
    act(V("aa"), V("a2"), AF.Copy, LIFT / 32)
    act(col("pf", 16), col("un", 15), AF.Copy, LIFT)
    ts(V("sm", 96, 100), io(4), 2.0, OP.mult, pe, OP.add)
    later, head, end = col("pf", 13), col("pf", 12), col("pf", 14)
    ts(later, p8, 0.0, OP.is_gt)
    ts(head, p8, 0.0, OP.is_equal, 128.0, OP.mult)
    ts(end, p8, 7.0, OP.is_equal, 112.0, OP.mult)
    ts(V("sm", 100, 103), V("sm", 96, 99), 16.0, OP.mult, 47.0, OP.add)
    ts(col("sm", 104), head, end, OP.add)
    ts(M(LS, 3), V("sm", 100, 103), later, OP.mult, col("sm", 104), OP.add)
    ts(col("pf", 15), p8, 16.0, OP.mult, 31.0, OP.add)
    ts(M(LS + 3, 1), col("pf", 15), end, OP.add)
    ts(col("pf", 20), pq, 0.0, OP.is_gt)
    ts(col("pf", 21), pq, 0.0, OP.is_equal, 16.0, OP.mult)
    ts(col("pf", 22), col("pf", 21), 8.0, OP.mult)
    ts(M(LOWN, 7), M(LO16, 7), col("pf", 20), OP.mult, col("pf", 22), OP.add)
    ts(col("pf", 23), pe, 9.0, OP.mult, pq, OP.add)
    ts(col("pf", 24), col("pf", 21), 9 / 16, OP.mult, -10.0, OP.add)
    ts(col("pf", 30), col("pf", 23), col("pf", 24), OP.add)
    ts(col("pf", 31), pq, -8.0, OP.add)
    ts(V("sm", 108, 115), io(7), col("pf", 31), OP.is_gt, col("pf", 30), OP.mult)
    ts(M(LTR, 7), V("sm", 108, 115), 9.0, OP.add)
    ts(col("pf", 25), head, 9 / 128, OP.mult, p8, OP.add)
    ts(col("pf", 26), col("pf", 25), -10.0, OP.add)
    ts(V("sm", 116, 120), V("sm", 96, 100), p8, OP.is_gt, col("pf", 26), OP.mult)
    ts(M(LTR + 7, 4), V("sm", 116, 120), 9.0, OP.add)
    iota(M(LMO - 1, 9), [[1, 9]], -1, 0)
    ts(col("sm", 120), pq, 8.0, OP.mult, -240.0, OP.add)
    ts(col("pf", 18), pq, 9.0, OP.is_ge, col("sm", 120), OP.mult)
    ts(col("pf", 27), pq, 8.0, OP.mult, col("pf", 18), OP.add)
    ts(col("pf", 28), pq, 2.0, OP.is_ge)
    ts(col("sm", 121), col("pf", 27), -65.0, OP.add)
    ts(col("pf", 29), col("sm", 121), col("pf", 28), OP.mult, 176.0, OP.add)
    ts(M(LK, 16), z(16), col("pf", 29), OP.add)
    ts(M(LSTI, 16), io(16), col("pf", 20), OP.mult, col("pf", 21), OP.add)
    cp(L(LS, LOWN + 7 - LS), M(LS, LOWN + 7 - LS))
    iota(V("la", 48, 64), [[16, 16]], 0, 0)
    ts(col("pf", 6), pq, 16.0, OP.mult)
    ts(L(LA, 16), V("la", 48, 64), col("pf", 6), OP.max, ph, OP.add)
    ts(L(LB, 16), V("la", 48, 64), col("pf", 6), OP.min, ph, OP.add)
    if MASKS:
        iota(V("ms"), [[0, 16], [1, 16]], 0, 0)
        select(V("rh"), V("ms"), [[0, 16], [1, 16]], OP.is_equal, 0.5, 0, 0)
        select(V("rm"), V("ms"), [[0, 16], [1, 16]], OP.is_equal, 1.0, 0, 0)
        select(V("ms"), V("ms"), [[0, 16], [1, 16]], OP.is_equal, 1.0, 0, 0)
    else:
        for name, c in (("rh", 0.5), ("rm", 1.0), ("ms", 1.0)):
            fill(V(name), c)
            level(V(name, 0, 256, 16), 0)
    level(V("ms", 17, 256, 17), -1)
    act(V("pw2"), io(16), AF.Exp, LN2)
    ops[-1]["cost"] += 1500.0
    ts(V("pwd"), V("pw2"), col("pf", 16), OP.add)
    act(V("pp", 0, 16), V("pw2"), AF.Copy, 1 / PTR)
    act(V("pp", 16, 32), io(16), AF.Copy, PTR)
    level(col("cu", 16), 16)
    fill(V("ez"), 0.5)
    iota(V("ib", 16, 240), [[-1, 14], [0, 16]], 14, 0)
    level(V("ib", 240, 256), 15)
    select(V("ez"), V("ez"), [[1, 520]], OP.is_equal, 0.0, -3, -4)
    iota(V("scv"), [[1, 16], [16, 16]], int(LIFT), 0)
    for name, c in (("own", 16), ("pay", 33), ("pay", 50), ("fl", 32), ("cu", 40), ("ef", 255), ("eb", 384), ("rq", 176)) + ((("s1", 271),) if DIRECT else ()):
        level(col(name, c), 0)
    for name, n in (("ki", 176), ("ini", 256)):
        level(V(name, 0, n), 0)
    level(V("eb", 128, 144), 0)
    for r in range(ROUNDS):
        iota(V("ct%d" % r, 184, 192), [[-1, 8]], 0, 0)
        level(V("ct%d" % r, 112, 128), 0)
    for b in range(4):
        quant(V("qe", 128 * b, 128 * b + 128), V("se", 128 * b, 128 * b + 128), V("ez", 3 - b, 515 - b))

    if TWICE:
        for at in (32, 0):
            tp(V("nt", at, at + 32), V("nf", at, at + 32))
    else:
        cp(V("nf"), G(V("ni"), L(LD, 4)))
        tp(V("nt"), V("nf"))
    if TWICE:
        cp(V("t3", 32, 48), G(V("nt", 32, 64), L(LT3, 1)))
        cp(V("t3", 0, 32), G(V("nt", 0, 32), L(LT3, 2)))
    else:
        cp(V("t3", 0, 48), G(V("nt"), L(LT3, 3)))
    par0, colv = V("t3", 32, 48), V("t3", 0, 16)
    en, pk = V("own", 0, 16), V("own", 17, 33)
    cp(V("lg1"), V("t3", 16, 32))
    cp(V("lcol"), colv)
    ts(pk if COLS else V("sm", 0, 16), colv, COL, OP.mult)
    tt(V("pe", 16, 32), pk if COLS else V("sm", 0, 16), io(16), OP.add)
    if not COLS:
        act(pk, V("pe", 16, 32))
    tt(V("pe", 0, 15), V("pe", 16, 31), V("pe", 17, 32), OP.subtract)
    act(col("pe", 15), col("pe", 31), AF.Identity, 1.0, 256 * TAKE)
    act(V("dnb"), G(V("pe", 0, 16), L(LO, 7)))
    act(V("pe", 32, 48), colv, AF.Copy, TAKE + COL)
    tt(V("dca", 0, 15), V("pe", 32, 47), V("pe", 33, 48), OP.subtract)
    act(V("dca", 16, 31), V("dca", 0, 15), AF.Identity, 1.0, -1.0)
    act(col("pf", 9), col("pe", 47), AF.Identity, 1.0, 16.0)
    act(col("pf", 10), col("pe", 47), AF.Identity, 1.0, 15.0)
    quant(V("qu0"), V("su0"), V("ut"))
    add("v", "pickq", (V("qu"), V("qu0"), L(LU, 8)), [V("qu0"), L(LU, 8)], [V("qu")], 50 + 1.5 * 128 * CYC)
    add("a", "picks", (V("su"), V("su0"), L(LU, 8)), [V("su0"), L(LU, 8)], [V("su")], 65 + 1.5 * 128 * CYC)
    quant(V("qv"), V("sv"), V("vt"))

    def aim(cur, plain):
        ts(V("p1"), cur, 1 / PTR, OP.mult)
        if plain:
            act(V("cu", 48, 64), cur)
            ts(V("hh"), cur, 1.5 * 2.0 ** 23 * PTR, OP.add, col("pf", 17), OP.subtract)
            tt(last16("aa"), cur, V("hh"), OP.subtract)
        else:
            tt(V("cu", 24, 40), cur, V("pp", 16, 32), OP.subtract)
            act(last16("aa"), cur, AF.Identity, 1.0, col("pf", 16))

    def ancestors(unit, parts, plain, done=0):
        for k in range(done, 4):
            for lo, hi in parts:
                rows = lambda name: V(name, 16 * lo, 16 * hi)
                src = G(V("cu", 48, 65) if plain else V("cu", 24, 41), V("p1", lo, hi)) if k else G(V("cu", 0, 17), V("p0", lo, hi))
                (act if lo == 0 else vact)(rows("ddb"), src, AF.Identity, 1.0 if k else unit, LIFT)
                scan(rows("hop"), rows("ddb"), rows("aa"), OP.max, OP.add)
            if k < 3:
                aim(last16("hop"), plain)
        if WIDE:
            tt(V("w4"), G(V("hop"), L(LE, 4)), V("eight"), OP.mult)
        for j in range(0 if WIDE else 4):
            ts(V("w4", 16 * j, 16 * j + 16), last16("hop"), 0.5 ** j, OP.mult, 0.5 ** (j + 1) - 0.5, OP.add)
        for j in range(4):
            ts(V("bits", 64 * j, 64 * j + 64), V("w4"), 4 * j + 3 * WIDE, OP.logical_shift_right, 1, OP.bitwise_and)

    cp(V("p0"), G(V("nt", 32, 64), L(LT3, 1)))
    ONE, TWO = ((0, 16),), ((0, 8), (8, 16))
    for lo, hi in (TWO if ASPLIT & 1 else ONE):
        (act if lo == 0 else vact)(V("dstb", 16 * lo, 16 * hi), G(par0, V("p0", lo, hi)), AF.Identity, 1.0, 33.0)
    scan(V("sp"), V("dstb"), V("a2"), OP.max, OP.add)
    tt(V("ba", 48, 64), par0, io(16), OP.is_lt)
    tt(V("sm", 80, 96), V("ba", 48, 64), io(16, 1), OP.mult)
    tt(V("sm", 48, 64), last16("sp"), V("sm", 80, 96), OP.is_equal)
    act(V("w"), par0, AF.Exp, LN2)
    for j in range(4 * WIDE):
        level(V("eight", 16 * j, 16 * j + 16), 8 >> j)
    if PLAIN:
        level(col("cu", 64), int(16 * PTR))
        act(col("pf", 17), col("un", 15), AF.Identity, LIFT, 1.5 * 2.0 ** 23 * PTR)
    if SHORT:
        level(V("ba", 0, 15), -1)
        level(col("ba", 15), 15)
        tt(V("sm", 16, 32), last16("sp"), V("sm", 80, 96), OP.not_equal)
        scan(V("sm", 32, 48), V("sm", 16, 32), V("ba", 0, 16))
        ts(V("sm", 64, 80), par0, col("sm", 47), OP.is_equal, 16 * PTR, OP.mult)
        act(V("ba", 16, 32), last16("sp"), AF.Identity, PTR, -PTR)
        tt(V("ba", 32, 48), V("ba", 16, 32), V("w"), OP.add)
        act(V("ex", 0, 16), V("pw2"), AF.Identity, -1.0, 16 * PTR)
        tt(V("ex", 16, 32), V("sm", 48, 64), V("ex", 0, 16), OP.mult)
        tt(V("ex", 32, 48), V("ba", 32, 48), V("ex", 16, 32), OP.max)
        tt(V("ex", 48, 64), V("ex", 32, 48), V("sm", 64, 80), OP.max)
        ts(V("p1"), V("ex", 48, 64), 1 / PTR, OP.mult)
        tt(V("cu", 48, 64), V("ex", 48, 64), V("pw2"), OP.add)
        ts(V("hh"), V("ex", 48, 64), 1.5 * 2.0 ** 23 * PTR, OP.add, col("pf", 17), OP.subtract)
        tt(last16("aa"), V("cu", 48, 64), V("hh"), OP.subtract)
    else:
        tt(V("sm", 16, 32), par0, V("pp", 0, 16), OP.add)
        act(V("sm", 32, 48), V("sm", 16, 32), AF.Copy, 1 / 16)
        tt(V("cu", 0, 16), V("sm", 32, 48), V("sm", 48, 64), OP.max)
        act(V("hh"), io(16, 32), AF.Copy, PTR)
        tt(V("ba", 0, 16), V("hh"), V("pw2"), OP.subtract)
        tt(V("ba", 16, 32), V("ba", 0, 16), V("w"), OP.subtract)
        tt(V("ba", 32, 48), V("sm", 48, 64), V("ba", 16, 32), OP.mult)
        tt(last16("aa"), V("pwd"), V("ba", 32, 48), OP.add)
    ancestors(16 * PTR, TWO if ASPLIT & 1 else ONE, PLAIN & 1, SHORT)
    act(V("dpb"), G(V("pe", 16, 32), V("p0")), AF.Identity, 1.0, LIFT)
    act(last16("aa"), z(16), AF.Identity, 1.0, col("pf", 16))
    scan(V("ep"), V("dpb"), V("aa"), OP.max, OP.add)
    tt(V("df", 0, 16), V("pe", 16, 32), last16("ep"), OP.subtract)
    if COLS:
        tt(V("df", 32, 48), io(16), par0, OP.subtract)
        tt(V("df", 0, 16), V("df", 0, 16), V("df", 32, 48), OP.subtract)

    def beside(link):
        ts(V("p16"), link, 16.0, OP.mult, 15.0, OP.add)
        act(last16("a2"), link, AF.Identity, 1.0, col("pf", 19))

    if DIRECT:
        ts(col("pf", 19), col("un", 15), 32.0, OP.mult, -16.0, OP.add)
        beside(par0)

    cp(V("lnod"), V("nf" if TWICE else "ni", 0, 16))
    for lo, hi in TWO:
        cp(G(V("rr"), V("lnod", lo, hi)), V("scv", 16 * lo, 16 * hi))
    scan(V("sr"), V("rr"), V("aa"), OP.max, OP.add)
    cp(V("inv"), last16("sr"))

    bank = lambda b, n: V("pa", 512 * b, 512 * b + n)
    side = lambda b, n: V("pb" if b < 2 else "ps", 512 * (b % 2), 512 * (b % 2) + n)
    eq = lambda b: (V("qe", 128 * b, 128 * b + 128), V("se", 128 * b, 128 * b + 128))

    def state_product(lq, ls):
        for h in range(2):
            q, s = V("qx", 128 * h, 128 * h + 128), V("sx", 128 * h, 128 * h + 128)
            quant(q, s, V("xt", 512 * h, 512 * h + 512))
            mx(V("ps", 512 * h, 512 * h + 128), lq, ls, q, s)

    for r in range(ROUNDS):
        ct, last = "ct%d" % r, r == ROUNDS - 1
        state_product(V("qu"), V("su"))
        pieces = ((0, 128), (128, 256)) if r in PIECES else ((0, 256),)
        home = [r in HOME_MADE for k in range(len(pieces))]
        begins, bulk = len(ops), []

        def cross(k, q, s):
            lo, hi = pieces[k]
            late = LANDS[r] * (0.6 if len(pieces) > 1 else 1.0)
            send(r, "av%d" % k, V("pq%d" % r, lo, hi), V(q, lo, hi), late)
            ops[-1]["cost"] += 0.0 if r or k else 1200.0 * SLOW ** 2
            if k:
                ops[-1]["behind"] = bulk[0]
            send(r, "av%d" % k, V("pp%d" % r, lo, hi), V(s, lo, hi), late)
            ops[-1]["behind"] = len(ops) - 2
            bulk.append(len(ops) - 1)

        def again(tile, q, s, lo, hi):
            for at in range(lo, hi, 128):
                quant(V(q, at, at + 128), V(s, at, at + 128), V(tile, 4 * at, 4 * at + 512))

        for k in range(len(pieces)):
            if not home[k]:
                cross(k, "qx", "sx")
        for b in range(4):
            mx(bank(b, 256), eq(b)[0], eq(b)[1], V("qx"), V("sx"))
        for h in range(2):
            act(V("ssb", 128 * h, 128 * h + 128), V("ps", 512 * h, 512 * h + 128))
        for lo, hi in (TWO if CSPLIT & 8 else ONE):
            act(V("g1", 16 * lo, 16 * hi), G(V("ssb"), V("lg1", lo, hi)))
            tp(V("tr", 16 * lo, 16 * hi), V("g1", 16 * lo, 16 * hi))
        parts = ((0, 8), (8, 16)) if GSPLIT else ((0, 16),)
        for lo, hi in parts:
            act(V("gb", 16 * lo, 16 * hi), G(V("tr"), L(LB + lo, hi - lo)))
            tt(V("c1", 16 * lo, 16 * hi), G(V("tr"), L(LA + lo, hi - lo)), V("gb", 16 * lo, 16 * hi), OP.is_gt)
        cuts = [(16 * lo, 16 * hi) for lo, hi in (TWO if CSPLIT & 1 else ONE)]
        for lo, hi in cuts:
            scan(V("s1", lo, hi), V("ms", lo, hi), V("c1", lo, hi))
        tt(en, io(16, 32), last16("s1"), OP.subtract)
        for b in range(4):
            act(V("fw", 512 * b, 512 * b + 256), bank(b, 256))
        for b in BYNODE:
            act(V("fn", 256 * b, 256 * b + 256), G(V("fw", 512 * b, 512 * b + 256), V("lcol")))
        for k, (lo, hi) in enumerate(pieces):
            made = "pq%d" % r, "pp%d" % r
            if home[k]:
                for b in range(4):
                    vact(V("fh", 4 * lo + b, 4 * hi, 4), V("fw", 512 * b + lo, 512 * b + hi), AF.Copy, 2.0)
                again("fh", "qh", "sh", lo, hi)
                cross(k, "qh", "sh")
            else:
                for b in range(4):
                    out = side(b, hi - lo) if BANKS & 1 << k else bank(b, hi - lo)
                    mx(out, eq(b)[0], eq(b)[1], V(made[0], lo, hi), V(made[1], lo, hi))
                    ops[-1]["also"] = [(bulk[0] - 1, LANDS[r])] * k
                    act(V("ft", 4 * lo + b, 4 * hi, 4), out, AF.Copy, 2.0)
                again("ft", "qf", "sf", lo, hi)
                made = "qf", "sf"
            for b in range(4):
                out = side(b, hi - lo) if BANKS & 4 << k else bank(b, hi - lo)
                mx(out, eq(b)[0], eq(b)[1], V(made[0], lo, hi), V(made[1], lo, hi))
                act(V("fw", 512 * b + 256 + lo, 512 * b + 256 + hi), out)
        act(V("w"), last16("s1"), AF.Exp, LN2)
        for lo, hi in (TWO if DSPLIT else ONE):
            src = G(V("s1"), V("p16", lo, hi)) if DIRECT else G(V("own", 0, 17), V("p0", lo, hi))
            act(V("dstb", 16 * lo, 16 * hi), src, AF.Identity, 1.0, 32.0)
        for lo, hi in [(16 * lo, 16 * hi) for lo, hi in (TWO if CSPLIT & 2 else ONE)]:
            tt(V("pr", lo, hi), G(V("w"), L(LO, (hi - lo) // 16)), V("bits", lo, hi), OP.mult)
            scan(V("bm", lo, hi), V("rh", lo, hi), V("pr", lo, hi))
        act(V("gg"), last16("bm"), AF.Abs, 1.0, -HALF)
        for lo, hi in parts:
            act(V("ai", 16 * lo, 16 * hi), G(V("bm", 16 * lo, 16 * hi), L(LO16, hi - lo)), AF.Abs, 1.0, -HALF)
            tt(V("c2", 16 * lo, 16 * hi), G(V("gg"), L(LO, hi - lo)), V("ai", 16 * lo, 16 * hi), OP.is_gt)
        for lo, hi in cuts:
            scan(V("posm", lo, hi), V("rm", lo, hi), V("c2", lo, hi))
        scan(V("sp"), V("dstb"), V("a2"), OP.max, OP.add)
        tt(V("df", 16, 32), en, last16("sp"), OP.add if DIRECT else OP.subtract)
        ts(V("fl", 0, 16), last16("bm"), HALF, OP.is_lt)
        tt(V("fl", 16, 32), V("df", 16, 32), V("fl", 0, 16), OP.mult)
        tt(V("fl", 33, 49), V("df", 0, 16), V("fl", 0, 16), OP.mult)
        tt(V("pay", 0, 33), V("own", 0, 33), V("fl", 16, 49), OP.subtract)
        tt(V("d3", 0, 33), V("pay", 0, 33), V("pay", 1, 34), OP.subtract)
        act(V("dbe"), G(V("d3", 0, 16), L(LO, 8)))
        if COLS:
            act(V("dbc"), G(V("d3", 0, 40), L(LO17, 7)), AF.Copy, 1 / COL)
            tt(V("fl", 50, 66), V("df", 32, 48), V("fl", 0, 16), OP.mult)
            tt(V("pay", 34, 50), io(16), V("fl", 50, 66), OP.subtract)
            tt(V("wd", 0, 16), V("pay", 34, 50), V("pay", 35, 51), OP.subtract)
            act(V("wd", 16, 32), V("d3", 17, 33), AF.Copy, TAKE / COL + 1)
            tt(V("wd", 32, 48), V("wd", 16, 32), V("wd", 0, 16), OP.add)
        else:
            whole(V("wd", 0, 16), V("d3", 17, 33), COL)
            act(V("dbc"), G(V("wd", 0, 16), L(LO, 7)), AF.Copy, 1 / COL)
            act(V("wd", 16, 32), V("wd", 0, 16), AF.Copy, TAKE / COL)
            tt(V("wd", 32, 48), V("wd", 16, 32), V("d3", 17, 33), OP.add)
        act(V("dbp"), G(V("wd", 32, 48), L(LO, 7)))
        tt(V("mk", 16, 128), G(V("posm"), L(LE, 7)), V("ib", 16, 128), OP.not_equal)
        scan(V("eb", 16, 128), V("mk", 16, 128), V("dbe", 0, 112))
        scan(V("eb", 144, 256), V("mk", 16, 128), V("dbc"))
        cp(V("ws%d" % r), G(V("eb", 0, 256), L(LS, 4)))
        send(r, "aw", V(ct, 128, 184), V("ws%d" % r, 0, 56), WAY * WORD[r])
        ops[-1]["also"] = [(bulk[-1], 0.0), (bulk[0] - 1, LANDS[r] / 2)] if r in APART else [(bulk[-1], ops[bulk[-1]]["late"]), (bulk[0] - 1, LANDS[r])]
        act(V("sto", 0, 112), G(en, L(LO, 7)))
        act(V("sti"), G(V("own", 0, 17), L(LSTI, 16)))
        act(V("ini", 0, 256, 16), en, AF.Exp, 2 * LN2, -LN2)
        tt(V("mk", 128, 256), G(V("posm"), L(LE, 8)), V("ib", 128, 256), OP.not_equal)
        scan(V("eb", 256, 384), V("mk", 128, 256), V("dbe"))
        act(V(ct, 0, 112), G(V("eb", 256, 385), L(LOWN, 7)))
        act(V("ki", 0, 112, 16), last16("eb", 256, 112))
        act(V(ct, 192, 199), last16("eb", 256, 112))
        scan(V("ef", 128, 240), V("mk", 128, 240), V("dbp"))
        scan(V("ef", 0, 16), V("mk", 240, 256), V("wd", 32, 48))
        dca = V("dca", 16 * last, 16 * last + 16)
        act(col("dca", 16 * last + 15), col("ef", 15), AF.Identity, -1.0, col("pf", 9 + last))
        if not last:
            act(last16("aa"), V("pwd"))
        act(V("ki", 120, 176, 8), V(ct, 176, 183))
        tt(V("qq"), G(V(ct, 176, 199), L(LTR, 11)), V(ct, 0, 176), OP.not_equal)
        ops[-1]["r"] += [V("inv"), V("ef", 128, 240), V("sti"), V("sto", 0, 112)] if HINT else []
        scan(V("rq", 0, 176), V("qq"), V("ki"))
        cuts = [(16 * lo, 16 * hi) for lo, hi in (TWO if CSPLIT & 4 else ONE)]
        for lo, hi in cuts:
            tt(V("dd", lo, hi), G(V("rq", 0, 177), L(LK, (hi - lo) // 16)), V("sti", lo, hi), OP.subtract)
            ts(V("fi", lo, hi), V("dd", lo, hi), 1.0, OP.min, -0.25, OP.max)
            scan(V("mg", lo, hi), V("fi", lo, hi), V("ini", lo, hi))
            ts(V("mm", lo, hi), V("mg", lo, hi), ROUGH, OP.add, ROUGH, OP.is_equal)
        act(col("ma", 32), col(ct, 176), AF.Relu, 1.0, -2.0)
        ts(V("ma", 0, 16), en, -2.0, OP.add, col("ma", 32), OP.not_equal)
        scan(V("dsx", 1, 17), V("ma", 0, 16), dca)
        act(last16("dnb", 0, 112), V(ct, 135, 184, 8), AF.Identity, TAKE, col("pe", 15))
        tt(V("mo"), G(V(ct, 176, 192), L(LMO, 7)), V("sto", 0, 112), OP.not_equal)
        scan(V("ef", 16, 128), V("mo"), V("dnb"))
        tt(V("dsx", 17, 32), last16("ef", 0, 240), last16("ef", 16, 240), OP.subtract)
        act(V("dsb", 0, ROWS * 16), G(V("dsx", 16, 32), L(LO, ROWS)))
        for lo in range(0, 256, ROWS * 16):
            scan(V("sr", lo, lo + ROWS * 16), V("mm", lo, lo + ROWS * 16), V("dsb", 0, ROWS * 16))
        for lo, hi in (TWO if CSPLIT & 16 else ONE):
            ts(V("sl", lo, hi), last16("sr", 16 * lo, 16 * (hi - lo)), 1 / TAKE, OP.mult)
        for b in range(4):
            for lo, hi in (TWO if b in FIRST else ONE):
                out, src = V("hn", 256 * b + 16 * lo, 256 * b + 16 * hi), G(V("fw", 512 * b, 512 * b + 512), V("sl", lo, hi))
                if b in BYNODE:
                    tt(out, src, V("fn", 256 * b + 16 * lo, 256 * b + 16 * hi), OP.add)
                else:
                    act(out, src)
            for lo, hi in (((0, 128), (128, 256)) if b in (ZLAST if last else ZSPLIT) else ((0, 256),)):
                out, src = V("zt", 4 * lo + b, 4 * hi, 4), G(V("hn", 256 * b, 256 * b + 256), V("inv", lo // 16, hi // 16))
                if b in BYNODE:
                    act(out, src)
                else:
                    tt(out, src, V("fw", 512 * b + lo, 512 * b + hi), OP.add)
                if not MERGE & 1:
                    act(V("z32", 4 * lo + b, 4 * hi, 4), V("zt", 4 * lo + b, 4 * hi, 4), AF.Copy, 32.0)
        for h, (lo, hi) in enumerate(((0, 128), (128, 256)) if HALVES else ((0, 256),)):
            quant(V("qz", lo, hi), V("sz", lo, hi), V("zt", 4 * lo, 4 * hi))
            if MERGE & 1:
                act(V("z32", 4 * lo, 4 * hi), V("zt", 4 * lo, 4 * hi), AF.Copy, 32.0)
            for b in range(4):
                out = (bank(b, hi - lo) if h == 0 else V("pb" if b < 2 else "ps", 512 * (b % 2), 512 * (b % 2) + 128))
                mx(out, V("qw", 128 * b, 128 * b + 128), V("sw", 128 * b, 128 * b + 128), V("qz", lo, hi), V("sz", lo, hi))
                x32 = V("x32", 4 * lo + b, 4 * hi, 4)
                tt(x32, out, V("z32", 4 * lo + b, 4 * hi, 4), OP.add)
                if not MERGE & (2 << h):
                    (act if b < 3 or h == 0 else vact)(V("xt", 4 * lo + b, 4 * hi, 4), x32, AF.Copy, 0.03125)
            if MERGE & (2 << h):
                (vact if h else act)(V("xt", 4 * lo, 4 * hi), V("x32", 4 * lo, 4 * hi), AF.Copy, 0.03125)
        whole(V("ex", 0, 16), last16("sr"), COL)
        tt(V("lk"), last16("sr"), V("ex", 0, 16), OP.subtract)
        if last:
            store("s", "op", V("lk"))
        else:
            cp(V("p0"), V("lk"))
            tt(V("cu", 0, 16), V("lk"), V("pp", 0, 16), OP.add)
            whole(V("ex", 16, 32), last16("sr"), TAKE)
            tt(V("ex", 32, 48), V("ex", 0, 16) if COLS else last16("sr"), V("ex", 16, 32), OP.subtract)
            tt(V("df", 0, 16), pk, V("ex", 32, 48), OP.subtract)
            if COLS:
                tt(V("df", 32, 48), io(16), V("lk"), OP.subtract)
            if DIRECT:
                beside(V("lk"))
            at = len(ops)
            ancestors(PTR, TWO if ASPLIT & 2 else ONE, PLAIN & 2)
            ops[at]["also"] = [(n, 0.0) for n in range(begins, at) if ops[n]["w"] and ops[n]["w"][0][0] in AFTER]
    state_product(V("qv"), V("sv"))
    for h in range(2):
        store("s", "oc", V("qx", 128 * h, 128 * h + 128))
        vact(V("ysb", 128 * h, 128 * h + 128), V("ps", 512 * h, 512 * h + 128))
        store("a", "y", V("ysb", 128 * h, 128 * h + 128))
    for k in range(4):
        store("sa"[k % 2], "osc", V("sx"), k)
    writes = lambda name, upto: [n for n in range(upto) if ops[n]["w"] and ops[n]["w"][0][0] == name]
    for then, names in SOON:
        n = writes(then, len(ops))[0]
        ops[n]["also"] = ops[n].get("also", []) + [(d, 0.0) for name in names for d in writes(name, n)]
    return ops


def replay(table, seq):
    free, end, top = [0.0] * len(QUEUES), [0.0] * len(seq), 0.0
    for n in seq:
        q, cost, late, deps, wake = table[n]
        t = t0 = free[q]
        for d, lag in deps:
            if end[d] + lag > t:
                t = end[d] + lag
        t += cost + wake if t > t0 else cost
        end[n] = free[q] = t
        if late and t + late > top:
            top = t + late
    return top, end


def shift(table, seq, run, lo, hi):
    top, old = run
    end, free, same, last = old[:], [0.0] * len(QUEUES), 0, None
    for n in seq[max(lo - 60, 0):lo]:
        free[table[n][0]] = old[n]
    for i in range(lo, len(seq)):
        n = seq[i]
        q, cost, late, deps, wake = table[n]
        t = t0 = free[q]
        for d, lag in deps:
            if end[d] + lag > t:
                t = end[d] + lag
        t += cost + wake if t > t0 else cost
        end[n] = free[q] = t
        if i > hi:
            t -= old[n]
            if last is not None and -1e-6 < t - last < 1e-6:
                same += 1
                if same == 30:
                    return t, end, i + 1
            else:
                same, last = 0, t
    return max(end[n] + table[n][2] for n in seq[-40:]) - top, end, len(seq)


def blocked(table, seq, end):
    before, last = {}, {}
    for n in seq:
        before[n] = last.get(table[n][0])
        last[table[n][0]] = n
    n = max(seq, key=lambda m: end[m] + table[m][2])
    pairs = []
    while n is not None:
        start, m = end[n] - table[n][1], before[n]
        if m is not None and abs(end[m] - start) < 1e-6:
            pairs.append((m, n))
            n = m
        else:
            n = next((d for d, lag in table[n][3] if abs(end[d] + lag + table[n][4] - start) < 1e-6), None)
    return pairs


def order(ops):
    writer, readers = {}, {}
    for n, o in enumerate(ops):
        deps, rd, wr = set(), set(), set()
        for v in o["r"]:
            rd |= cells(v)
        for v in o["w"]:
            wr |= cells(v)
        wr |= {c for c in rd if c[0] in PS}
        for c in rd | wr:
            if c in writer:
                deps.add(writer[c])
        for c in wr:
            deps |= readers.get(c, set())
        for c in wr:
            writer[c] = n
            readers[c] = set()
        for c in rd:
            readers.setdefault(c, set()).add(n)
        deps.discard(n)
        o["deps"] = deps | ({o["behind"]} if "behind" in o else set())
    above = []
    for n, o in enumerate(ops):
        far = 0
        for d in o["deps"]:
            far |= above[d]
        o["near"] = sorted(d for d in o["deps"] if not far >> d & 1)
        above.append(far | sum(1 << d for d in o["deps"] - {o.get("behind")}))
    timed = [program(pace[0], pace[3], pace[4], pace[5]) for pace in PACES]
    flat = [[(QUEUES.index(o["q"]), t["cost"] + ISSUE, t["late"], [(d, 0.0 if d == o.get("behind") else same[d]["late"] + lag) for d in o["near"]] + t.get("also", []), wake) for o, t in zip(ops, same)]
            for same, (cycle, lag, wake, slow, pick, way) in zip(timed, PACES)]
    spare = [{n: (QUEUES.index(t["other"][0]), t["other"][3] + ISSUE) + table[n][2:] for n, t in enumerate(same) if "other" in t} for same, table in zip(timed, flat)]

    def swap(n):
        o = ops[n]
        o["q"], o["kind"], o["args"], o["cost"], o["other"] = o["other"] + ((o["q"], o["kind"], o["args"], o["cost"]),)
        for table, rest in zip(flat, spare):
            table[n], rest[n] = rest[n], table[n]

    score = lambda s: sum(replay(t, s)[0] for t in flat)
    tail = [o["cost"] + o["late"] for o in ops]
    users = [[] for o in ops]
    for n in range(len(ops) - 1, -1, -1):
        for d, lag in flat[0][n][3]:
            tail[d] = max(tail[d], ops[d]["cost"] + lag + tail[n])
            users[d].append(n)
    def queues(want):
        for n, q in enumerate(want):
            if ops[n]["q"] != q:
                swap(n)

    def lay(turns, forms, before, first):
        starts, ends = [[] for q in QUEUES], [[] for q in QUEUES]
        end, start, where = [0.0] * len(ops), [0.0] * len(ops), [0] * len(ops)
        for n in turns:
            ready = first[n]
            for d, lag in before[n]:
                if end[d] + lag > ready:
                    ready = end[d] + lag
            found = None
            for q, cost, toll in forms[n]:
                s, e, t = starts[q], ends[q], ready
                i = len(e)
                while i and e[i - 1] > t:
                    i -= 1
                while i < len(s) and s[i] < t + cost - 1e-6:
                    t = max(t, e[i])
                    i += 1
                if found is None or t + cost + toll < found[0]:
                    found = (t + cost + toll, q, i, t, cost)
            key, q, i, t, cost = found
            starts[q].insert(i, t)
            ends[q].insert(i, t + cost)
            start[n], end[n], where[n] = t, t + cost, q
        return start, end, where

    def turns_by(key, before, after):
        key = list(key)
        for n in (range(len(ops)) if before is ahead else range(len(ops) - 1, -1, -1)):
            for d, lag in before[n]:
                if key[d] >= key[n]:
                    key[n] = key[d] + 1e-3
        return sorted(range(len(ops)), key=lambda n: key[n])

    best, rng = None, np.random.default_rng(0)
    both = [[(table[n][:2],) + ((rest[n][:2],) if n in rest else ()) for n in range(len(ops))] for table, rest in zip(flat, spare)]
    late, zero = [o["late"] for o in ops], [0.0] * len(ops)
    for plan in range(PLANS):
        pace = plan % len(flat)
        ahead = [flat[pace][n][3] for n in range(len(ops))]
        behind = [[] for o in ops]
        for n in range(len(ops)):
            for d, lag in ahead[n]:
                behind[d].append((n, lag))
        toll, grain = rng.random(2).tolist()
        forms = [[(q, c, TOLL * toll * c * e if q == 0 else 0.0) for q, c in f] for f, e in zip(both[pace], (0.5 + rng.random(len(ops))).tolist())]
        if best is None or plan % 4 == 0:
            key = [-t for t in tail]
        else:
            key = best[3]
        key = [k + GRAIN * grain * e for k, e in zip(key, rng.random(len(ops)).tolist())]
        for sweep in range(SWEEPS):
            start, end, where = lay(turns_by(key, ahead, behind), forms, ahead, zero)
            queues([QUEUES[q] for q in where])
            seq = sorted(range(len(ops)), key=lambda n: (start[n], n))
            total = score(seq)
            if best is None or total < best[0]:
                best = (total, seq, [QUEUES[q] for q in where], start)
            start, end, where = lay(turns_by([-e for e in end], behind, ahead), forms, behind, late)
            key = [-e for e in end]
    best = best[:3]
    def improve(seq, seed, moves, span):
        taken, pool = 0, seq[max(span[0], 0):span[1]]
        free = set(pool)
        for turn, (a, b, c, e) in enumerate(np.random.default_rng(seed).random((moves, 4)).tolist()):
            if taken % 16 == 0:
                runs = [replay(t, seq) for t in flat]
                end = runs[0][1]
                seq.sort(key=lambda m: end[m] - ops[m]["cost"])
                held = [p for p in blocked(flat[turn % len(flat)], seq, runs[turn % len(flat)][1]) if p[1] in free]
                taken += 1
            step = 1 if b < 0.5 else -1
            n = held[int(a * len(held))][step < 0] if e < 0.8 and held else pool[int(a * len(pool))]
            i = seq.index(n)
            turned = "other" in ops[n] and turn % 3 == 0
            if turned:
                swap(n)
            hops, j, to = int(c ** 3 * 30) + (0 if turned else 1), i, i
            stop = set(users[n]) if step > 0 else ops[n]["deps"]
            while hops and 0 <= j + step < len(seq) and seq[j + step] not in stop:
                j += step
                if ops[seq[j]]["q"] == ops[n]["q"]:
                    hops -= 1
                    to = j
            if to == i and not turned:
                continue
            new = seq[:i] + seq[i + 1:]
            new.insert(to, n)
            moved = [shift(t, new, run, min(i, to), max(i, to)) for t, run in zip(flat, runs)]
            if sum(m[0] for m in moved) <= SLACK * (1.0 - turn / moves) ** 2 * c:
                for by, end, rest in moved:
                    if by:
                        for m in new[rest:]:
                            end[m] += by
                seq, runs, taken = new, [(run[0] + m[0], m[1]) for run, m in zip(runs, moved)], taken + 1
            elif turned:
                swap(n)
        return seq

    def rebuild(seq, seed, rounds, span):
        stale, taken = True, 0
        for turn, (a, b, c, e, f) in enumerate(np.random.default_rng(seed).random((rounds, 5)).tolist()):
            if stale:
                runs = [replay(t, seq) for t in flat]
                seq.sort(key=lambda m: runs[0][1][m] - flat[0][m][1])
                rests = []
                for table in flat:
                    rest, nxt = [0.0] * len(ops), [0.0] * len(QUEUES)
                    for n in reversed(seq):
                        q, cost, late, deps, wake = table[n]
                        t = rest[n] = nxt[q] = max(rest[n], nxt[q], late) + cost
                        for d, lag in deps:
                            if rest[d] < t + lag:
                                rest[d] = t + lag
                    rests.append(rest)
                stale = False
            pace = turn % len(flat)
            table, end, rest = flat[pace], runs[pace][1][:], rests[pace]
            size = 12 + int(b * SPAN)
            lo = int((span[0] + a * span[1]) * (len(seq) - size))
            part = seq[lo:lo + size]
            inside = set(part)
            free, after = [0.0] * len(QUEUES), [None] * len(QUEUES)
            for n in seq[max(lo - 60, 0):lo]:
                free[table[n][0]] = end[n]
            for n in seq[lo + size:lo + size + 80]:
                if after[table[n][0]] is None:
                    after[table[n][0]] = rest[n]
            noise = np.random.default_rng(seed * rounds + turn).random(2 * size).tolist()
            chain = {}
            for i, n in enumerate(sorted(part, reverse=True)):
                t = max(table[n][2], after[table[n][0]] or 0.0)
                for m in users[n]:
                    lag = links[pace][n, m]
                    t = max(t, (chain[m] if m in inside else rest[m]) + lag)
                chain[n] = t + table[n][1]
            key = {n: GRAIN * c * r - chain[n] for n, r in zip(part, noise)}
            for n in sorted(part):
                for d, lag in table[n][3]:
                    if d in inside and key[d] >= key[n]:
                        key[n] = key[d] + 1e-3
            starts, ends, start, turned = [[] for q in QUEUES], [[] for q in QUEUES], {}, []
            for n, r in zip(sorted(part, key=key.get), noise[size:]):
                ready, found = 0.0, None
                for d, lag in table[n][3]:
                    if end[d] + lag > ready:
                        ready = end[d] + lag
                for q, cost in both[pace][n]:
                    s, u, t = starts[q], ends[q], max(ready, free[q])
                    i = len(u)
                    while i and u[i - 1] > t:
                        i -= 1
                    while i < len(s) and s[i] < t + cost - 1e-6:
                        t = max(t, u[i])
                        i += 1
                    mark = t + cost + (TOLL * e * cost * r if q == 0 else 0.0) + (STAY * f if q != table[n][0] else 0.0)
                    if found is None or mark < found[0]:
                        found = (mark, q, i, t, cost)
                mark, q, i, t, cost = found
                starts[q].insert(i, t)
                ends[q].insert(i, t + cost)
                start[n], end[n] = t, t + cost
                if q != table[n][0]:
                    turned.append(n)
            new = seq[:lo] + sorted(part, key=lambda n: (start[n], n)) + seq[lo + size:]
            if new == seq and not turned:
                continue
            for n in turned:
                swap(n)
            moved = [shift(t, new, run, lo, lo + size) for t, run in zip(flat, runs)]
            if sum(m[0] for m in moved) <= (LOOSE if span[1] == 1.0 else LOOSER) * (1.0 - turn / rounds) ** 2 * noise[0]:
                for by, end, at in moved:
                    if by:
                        for m in new[at:]:
                            end[m] += by
                seq, runs, taken = new, [(run[0] + m[0], m[1]) for run, m in zip(runs, moved)], taken + 1
                stale = taken % FRESH == 0
            else:
                for n in turned:
                    swap(n)
        return seq

    def pull(seq, seed, rounds):
        total, zero = score(seq), [0.0] * len(ops)
        for turn, (a, b, c) in enumerate(np.random.default_rng(seed).random((rounds, 3)).tolist()):
            table = flat[turn % len(flat)]
            end = replay(table, seq)[1]
            key = [end[n] - table[n][1] for n in range(len(ops))]
            first = seq[int(a * a * len(seq))]
            limit, todo = key[first] - 300.0 - 6000.0 * b * b, [first]
            while todo:
                n = todo.pop()
                if key[n] > limit:
                    key[n] = limit - 1e-3 * (len(ops) - n)
                    todo += [d for d, lag in table[n][3]]
            ahead = [table[n][3] for n in range(len(ops))]
            for n in range(len(ops)):
                for d, lag in ahead[n]:
                    if key[d] >= key[n]:
                        key[n] = key[d] + 1e-6
            start = lay(sorted(range(len(ops)), key=lambda n: key[n]), [[table[n][:2] + (0.0,)] for n in range(len(ops))], ahead, zero)[0]
            new = sorted(range(len(ops)), key=lambda n: (start[n], n))
            mark = score(new)
            if mark <= total + EASE * c:
                seq, total = new, mark
        return seq

    links = [{(d, n): lag for n in range(len(ops)) for d, lag in table[n][3]} for table in flat]
    def join(a, b, cut):
        keys = []
        for run in (a, b):
            queues(run[2])
            end = replay(flat[0], run[1])[1]
            keys.append([end[n] - flat[0][n][1] - end[cut] + flat[0][cut][1] for n in range(len(ops))])
        early = [k < 0 for k in keys[0]]
        key = [keys[0][n] if early[n] else max(keys[1][n], 0.0) for n in range(len(ops))]
        queues([a[2][n] if early[n] else b[2][n] for n in range(len(ops))])
        for n in range(len(ops)):
            for d, lag in flat[0][n][3]:
                if key[d] >= key[n]:
                    key[n] = key[d] + 1e-6
        seq = sorted(range(len(ops)), key=lambda n: key[n])
        at = seq.index(cut) / len(seq)
        seq = rebuild(seq, cut, MEND, (max(at - 0.04, 0.0), 0.06))
        return score(seq), seq, [o["q"] for o in ops]

    begin, runs = best, []
    for seed in range(RUNS):
        queues(begin[2])
        seq = rebuild(list(begin[1]), 100 + seed, REBUILDS, (0.0, 1.0))
        runs.append((score(seq), seq, [o["q"] for o in ops]))
    best = min(runs + [best])
    for cut in [n for n, o in enumerate(ops) if o["w"] and o["w"][0][:2] in CUTS]:
        for run in runs:
            best = min(best, join(best, run, cut), join(run, best, cut))
    for seed in range(1, STARTS):
        queues(best[2])
        at = (seed - 1) * 0.382 % 1.0 * (1.0 - PART)
        seq = pull(list(best[1]), seed, PULLS) if seed % 4 == 1 else list(best[1])
        seq = rebuild(seq, seed + 1, REBUILDS // (6 if seed else 1), (0.0, 0.999) if seed % 4 == 1 else (at, PART) if seed else (0.0, 1.0))
        if score(seq) < best[0]:
            best = (score(seq), seq, [o["q"] for o in ops])
    for seed in range(TRIES):
        queues(best[2])
        part = (seed - 1) % STRETCHES * len(ops) // STRETCHES
        span = (part - 30, part + len(ops) // STRETCHES + 30) if seed else (0, len(ops))
        seq = improve(list(best[1]), seed, MOVES // (8 if seed else 1), span)
        if score(seq) < best[0]:
            best = (score(seq), seq, [o["q"] for o in ops])
    queues(best[2])
    seq = best[1]
    end = replay(flat[0], seq)[1]
    for n, o in enumerate(ops):
        o["at"] = end[n] - o["cost"]
    place = {n: i for i, n in enumerate(seq)}
    known = {q: {} for q in QUEUES}
    for n in seq:
        o = ops[n]
        k = known[o["q"]]
        need = {}
        for d in o["deps"] - {o.get("behind")}:
            kind = ops[d]["kind"]
            if kind == "send":
                side = "out" if any(cells(ops[d]["r"][0]) & cells(v) for v in o["w"]) else "in"
                key = (side,) + ops[d]["args"][:2]
            else:
                key = ("dma", d) if kind in ("load", "store") else ops[d]["q"]
            if k.get(key, -1) < place[d] and place[d] > place.get(need.get(key, -1), -1):
                need[key] = d
        waits = []
        for key, d in sorted(need.items(), key=lambda e: -place[e[1]]):
            if k.get(key, -1) >= place[d]:
                continue
            waits.append((d, key[0] == "out"))
            ops[d]["inc"] = True
            if key[0] in ("in", "out"):
                k[key] = len(seq)
                continue
            k[key] = place[d]
            for kk, vv in ops[d]["seen"].items():
                if k.get(kk, -1) < vv:
                    k[kk] = vv
        o["waits"] = waits
        o["seen"] = dict(k)
    return seq


OPS = program(PACES[0][0], PACES[0][3], PACES[0][4], PACES[0][5])
SEQ = order(OPS)


def rank_program(g, core, T, topo):
    rank = T.rank_of(core)
    if rank is None:
        return
    eng = {"v": g.vector, "a": g.scalar, "p": g.tensor, "g": g, "s": g.sync}

    def ap(v):
        if not isinstance(v, tuple):
            return v
        if v[0] == "@":
            return ap(v[1]).indirect(ap(v[2]))
        name, at = HOME.get(v[0], (v[0], 0))
        if v[3] == 1:
            return T[name][:, at + v[1]:at + v[2]]
        return T[name][:, at + v[1]:at + v[2]:v[3]]

    def raw(v):
        return ap(v).bitcast(dt.uint8) if BUF[v[0]][0] == Q4 else ap(v)

    partner = [T.cores[rank ^ (1 << r)] for r in range(ROUNDS)]
    done = {q: 0 for q in QUEUES}
    mark, ndma, sent, stores = {}, [0], {}, []
    for n in SEQ:
        o = OPS[n]
        e, kind, a = eng[o["q"]], o["kind"], o["args"]
        for d, left in o["waits"]:
            e.wait_ge(T.sem[("left" if left else "") + mark[d][0]], mark[d][1])
        if kind == "send":
            r, sem, out, src = a
            rid, pid, sengine = topo.addr(partner[r])
            local = "sent" if sem == "aw" else "left%s%d" % (sem, r)
            use = topo.engines(core, partner[r])
            if r in APART and sem != "av0":
                use = use[len(use) // 2:] if sem == "aw" else use[:len(use) // 2]
            lanes = len(use)
            g.remote_dma(raw(out), raw(src), T.sem["%s%d" % (sem, r)], T.sem[local], pid, rid, sum(1 << k for k in use))
            sent[local] = sent.get(local, 0) + lanes
            mark[n] = ("%s%d" % (sem, r), lanes * (1 if sem == "aw" else 2))
            continue
        if kind in ("load", "store"):
            if kind == "load":
                ins = e.dma_start(raw(a[0]), raw(a[1]) if isinstance(a[1], tuple) else T[a[1]][:])
            elif a[0] == "op":
                ins = e.dma_start(T[a[0]][:], raw(a[1]))
            elif a[2] is None:
                wide = 4 if a[0] == "oc" else 1
                ins = e.dma_start(T[a[0]][:, wide * a[1][1]:wide * a[1][2]], raw(a[1]))
            else:
                ins = e.dma_start(T[a[0]][4 * a[2]:4 * a[2] + 4, :], T[a[1][0]][32 * a[2]:32 * a[2] + 4, :])
            mark[n] = ("d%d" % ndma[0], 16)
            ndma[0] += 1
            ins.then_inc(T.sem[mark[n][0]], 16)
            if kind == "store":
                stores.append((e, mark[n]))
            continue
        if kind == "copy":
            ins = e.tensor_copy(ap(a[0]), ap(a[1]))
        elif kind == "tt":
            ins = e.tensor_tensor(ap(a[0]), ap(a[1]), ap(a[2]), a[3])
        elif kind == "ts":
            if a[5] is None:
                ins = e.tensor_scalar(ap(a[0]), ap(a[1]), ap(a[2]), None, a[4])
            else:
                ins = e.tensor_scalar(ap(a[0]), ap(a[1]), ap(a[2]), ap(a[3]), a[4], a[5])
        elif kind == "scan":
            ins = e.tensor_tensor_scan(ap(a[0]), ap(a[1]), ap(a[2]), a[3], a[4], a[5])
        elif kind == "tp":
            ins = e.transpose(ap(a[0]), ap(a[1]))
        elif kind == "fill":
            ins = e.memset(ap(a[0]), a[1])
        elif kind == "quant":
            ins = e.quantize_mx(ap(a[0]), ap(a[1]), ap(a[2]))
        elif kind == "act":
            if a[4] is None:
                ins = e.activation(ap(a[0]), ap(a[1]), a[2], scale=a[3])
            else:
                ins = e.activation(ap(a[0]), ap(a[1]), a[2], bias=ap(a[4]), scale=ap(a[3]))
        elif kind == "mx":
            ins = e.matmul_mx(ap(a[0]), ap(a[1]), ap(a[2]), ap(a[3]), ap(a[4]), True, True)
        elif kind == "iota":
            if BUF[a[0][0]][0] == I:
                ins = e.iota(ap(a[0]), a[1], a[2], a[3])
            else:
                ins = e.iota(ap(a[0]), a[1], a[2], a[3], allow_small_or_imprecise_dtypes=True)
        elif kind == "select":
            ins = e.affine_select(ap(a[0]), ap(a[1]), a[2], a[3], a[4], a[5], a[6])
        elif kind == "pickq":
            ins = e.tensor_copy(ap(a[0]).bitcast(dt.uint32), ap(a[1]).bitcast(dt.uint32).indirect(ap(a[2])))
        else:
            ins = e.activation(ap(a[0]), ap(a[1]).indirect(ap(a[2])), AF.Copy)
        if o.get("inc"):
            done[o["q"]] += 1
            mark[n] = ("q" + o["q"], done[o["q"]])
            ins.then_inc(T.sem[mark[n][0]], 1)
    for local, total in sent.items():
        g.wait_ge(T.sem[local], total)
    for e, m in stores:
        e.wait_ge(T.sem[m[0]], m[1])
